import numpy as np, ml_dtypes
CORES = [40,41,42,43,44,45,46,47]
N = 8
import mx_ref
BF = ml_dtypes.bfloat16
def gcols(t, e):
    v = np.concatenate([t.reshape(8, 16, -1, 4), np.zeros((8, 16, 1, 4), BF)], axis=2)
    return np.ascontiguousarray(np.stack([v[g][:, e[g]] for g in range(8)])).reshape(128, -1)
def tile(rs):
    return np.stack(rs, axis=2).reshape(128, -1).astype(BF)
def pick(q, e):
    c = np.concatenate([q[0].reshape(128, -1, 4), np.zeros((128, 1, 4), np.uint8)], axis=1); s = np.concatenate([q[1], np.ones((16, 1), np.uint8)], axis=1)
    return (np.ascontiguousarray(c[:, e].reshape(128, -1)), np.ascontiguousarray(s[:, e]))
def join(*qs):
    return (np.concatenate([q[0] for q in qs], axis=1), np.concatenate([q[1] for q in qs], axis=1))
def put(q, e, v):
    c, s = q[0].reshape(128, -1, 4).copy(), q[1].copy(); c[:, e] = v[0].reshape(128, -1, 4); s[:, e] = v[1]
    return (c.reshape(128, -1), s)
def pk(c, s):
    return (np.ascontiguousarray(c), mx_ref.live(s))
def emit(q):
    return q[0], q[1]
def packed(v, rng):
    q = [mx_ref.quantize(np.ascontiguousarray(v[r])) for r in range(N)]
    return np.stack([a for a, b in q]), np.stack([mx_ref.plane(b, rng) for a, b in q])
def values_of_codes():
    e, c = np.zeros((128, 128, 4), np.float32), np.zeros((128, 2, 4), np.uint8)
    e[np.arange(128), np.arange(128), 0] = 1
    c[:127, :, 0] = np.arange(256).reshape(2, 128).T[:127]
    return mx_ref.matmul(mx_ref.quantize(e.reshape(128, 512).astype(BF)), (c.reshape(128, 8), np.full((16, 2), 127, np.uint8))).T.reshape(-1).astype(np.float64)
CODE_VALUE, SCALE_VALUE = values_of_codes(), 2.0 ** (np.arange(256) - 127.0)
def decode(q):
    return (CODE_VALUE[q[0]].reshape(16, 8, -1, 4) * SCALE_VALUE[q[1]][:, None, :, None] + 0.0).reshape(128, -1).astype(np.float32)
def f(rng, *shape):
    return mx_ref.flush((rng.standard_normal(shape, dtype=np.float32) * np.exp2(rng.integers(-2, 3, shape[:-1] + (1,)))).astype(BF))
def wide(rng, *shape, cols=0):
    v = rng.standard_normal(shape, dtype=np.float32) * np.exp2(rng.integers(-12, 13, shape)).astype(np.float32)
    if cols: v *= np.repeat(np.exp2(rng.integers(-cols, cols + 1, shape[:-2] + (1, shape[-1] // 4))) * (rng.random(shape[:-2] + (1, shape[-1] // 4)) > 0.0625), 4, axis=-1).astype(np.float32)
    return mx_ref.flush(v.astype(BF))
C, K, R = 384, 96, 3
STEP = [1, 2, 3]
def order(p):
    return np.argsort(-(p[::16] + np.float32(0.0)), axis=1, kind="stable")
def big(v):
    v = v.astype(np.float32)
    v[np.abs(v) < np.float32(2.0 ** -16)] = 0
    return v.astype(BF)
def numbers_of(rng):
    return {"x": big(f(rng, N, 128, 4 * C)), "u": np.array(f(rng, N, 128, 512)), "v": np.array(f(rng, N, 128, 512))}
def layers(rng, still=0):
    w = big(f(rng, N, 128, 2048)).reshape(N, 8, 16, 4, 8, 16, 4)
    w[:, :, :still] = 0
    w[:, :, :, :, :, :still] = 0
    return w
def weights(rng, w):
    c, p = packed(np.ascontiguousarray(w).reshape(N, 128, 2048), rng)
    return {"wc": c, "ws": p}
def signs(rng):
    return np.stack([rng.permutation(8) % 2 * 2.0 - 1.0 for r in range(N)])
def setup_inputs(rng):
    return {**numbers_of(rng), **weights(rng, layers(rng))}
def setup_inputs_ties(rng):
    d = numbers_of(rng)
    e = rng.permutation(N)
    x = d["x"].reshape(N, 8, 16, C, 4)
    for r in range(N):
        k = np.zeros(C, int) if r == e[0] else rng.permutation(C) % 3
        a = x[r][:, :8, :3].copy()
        a[:, :, 2] = 0
        x[r][:, :8] = a[:, :, k]
    x[e[1]] = 0
    u = d["u"].reshape(N, 8, 16, 8, 16, 4)
    k = u.copy()
    u[:, :, :, :, :4] = 0
    for g in range(8): u[:, g, :8, g, :4] = k[:, g, :8, g, :4]
    return {"x": x.reshape(N, 128, 4 * C), "u": u.reshape(N, 128, 512), "v": d["v"], **weights(rng, layers(rng, 8))}
def setup_inputs_near(rng):
    d = numbers_of(rng)
    x = np.zeros((N, 8, 16, C, 4), np.float32)
    d["u"].reshape(N, 128, 8, 16, 4)[:, :, :, :4] = 0
    u = d["u"].reshape(N, 128, 128, 4)
    o, c = rng.permutation(N) % 4, signs(rng)
    upper = np.arange(C) // (C // 2)
    for r in range(N):
        i = (np.arange(C) + rng.integers(0, C, (8, 1))) % C
        if o[r] == 3: i = i % (C // 2) * 2 + upper
        s = (i + 1) // 2
        size = 1.0 if o[r] < 2 else 2.0 ** -4
        z = ((s[:, :, None] >> np.arange(8)) & 1) * np.exp2(np.arange(8) - 23.0) * size
        if o[r] < 2: x[r, :, 0, :, 0] = c[r][:, None]
        if o[r] == 1:
            for g in rng.permutation(8)[:4]: x[r, g, 0, rng.integers(C), 0] *= np.float32(2.0 ** 30)
        if o[r] == 3: x[r, :, 0, :, 0] = (8 + upper) * 2.0 ** -30
        a = rng.integers(-1, 2, (8, 3, C))
        if o[r] < 2: x[r, :, 1:4, :, 0] = a
        else:
            x[r, :, 1:4, :, 0] = (5 * a * a + a) * 2.0 ** -31
            x[r, :, 1:4, :, 1] = (a - 5 * a * a) * 2.0 ** -31
        x[r, :, 8] = z[:, :, :4]
        x[r, :, 9] = z[:, :, 4:]
        x[r, :, 10:] = rng.integers(4, 8, (8, 6, C, 4)) * 2.0 ** -20 * size
        k = 1.0 if o[r] == 0 else 2.0 ** -30
        for h in range(0, 128, 16):
            for n in range(4): u[r, h + n, h + n, :2] = k
            u[r, h + 8:h + 10, h] = k
    w = np.abs(layers(rng, 10).astype(np.float32)) * np.float32(2.0 ** -6)
    return {"x": x.reshape(N, 128, 4 * C).astype(BF), "u": u.reshape(N, 128, 512), "v": d["v"], **weights(rng, w.astype(BF))}
def setup_inputs_huge(rng):
    d = numbers_of(rng)
    c = np.stack([rng.permutation(C) % 2 * 2.0 - 1.0 for r in range(N)])
    c[rng.permutation(N) < N // 2] = -1
    x = 2.0 ** 30 * (0.75 + 0.13 * rng.random((N, 128, C, 4))) * c[:, None, :, None]
    s = np.stack([signs(rng) for i in range(4)], axis=2)
    a = 2.0 ** 30 * (1 - 0.25 * rng.random((N, 128, 8, 4, 4))) * s[:, None, :, :, None]
    d["u"].reshape(N, 128, 8, 16, 4)[:, :, :, :4] = a.astype(np.float32).astype(BF)
    w = np.zeros((N, 128, 4, 128, 4), np.float32)
    i = np.arange(128)
    for b in range(4): w[:, i, b, i, b] = -1
    return {"x": x.astype(np.float32).reshape(N, 128, 4 * C).astype(BF), "u": d["u"], "v": d["v"], **weights(rng, w.astype(BF))}
def setup_inputs_votes(rng):
    d = numbers_of(rng)
    x = d["x"].reshape(N, 8, 16, C, 4)
    x[:, :, :8] = 0
    kinds = rng.permutation(8)
    for g in range(8):
        e0, a0 = rng.permutation(C)[:K], rng.integers(0, 8, C)
        s0, q = int(rng.integers(C - K + 1)), int(rng.integers(1, C // 16))
        for r in range(N):
            e, a = rng.permutation(C)[:K], rng.integers(0, 8, C)
            if kinds[g] == 0: a[:] = r
            if kinds[g] == 1:
                e = (np.arange(K) + rng.integers(C)) % C
                a[:] = 7
            if kinds[g] == 2:
                e = rng.permutation(C // 2)[:K // 2]
                e, a = np.concatenate([e, e + C // 2]), np.tile(a[:C // 2], 2)
            if kinds[g] == 3:
                s = 16 * int(rng.integers(C // 16)) + int(rng.integers(2))
                e, a = (e0 + s) % C, np.roll(a0, s)
            if kinds[g] == 4: e = np.arange(K)
            if kinds[g] == 5: e = np.arange(C - K, C)
            if kinds[g] == 6:
                e = (s0 - 16 * q * (1 - r % 2) + np.arange(K)) % C
                if r % 2 == 0: e[1] = (s0 - 16 * q + K + 16) % C
                a[:] = 7
            p = -1.0 * rng.integers(0, 2, C)
            p[e] = 1 + 0.125 * rng.integers(0, 8, K)
            x[r, g, 0, :, 0] = p.astype(BF)
            for i in range(3): x[r, g, 1 + i, :, 0] = np.where((a >> i) & 1 == 1, 1.0, -1.0 * rng.integers(0, 2, C)).astype(BF)
    d["u"].reshape(N, 128, 8, 16, 4)[:, :, :, :4] = 0
    u = d["u"].reshape(N, 128, 128, 4)
    for h in range(0, 128, 16):
        for n in range(4): u[:, h + n, h + n, 0] = 1
    return {"x": x.reshape(N, 128, 4 * C), "u": u.reshape(N, 128, 512), "v": d["v"], **weights(rng, layers(rng, 8))}
def setup_inputs_spread(rng):
    d = setup_inputs(rng)
    d["x"] = big(wide(rng, N, 128, 4 * C, cols=6))
    return d
def check_inputs(d):
    b = []
    for k in ("x", "u", "v"):
        a = np.abs(d[k].astype(np.float32))
        if not (np.isfinite(a).all() and ((a == 0) | (a >= 2.0 ** -30) & (a <= 2.0 ** 30)).all()): b.append("a value of " + k)
    none, least, most = [emit(mx_ref.quantize(np.full((128, 16), k, np.float32).astype(BF)))[1][0, 0] for k in (0.0, 2.0 ** -30, 2.0 ** 30)]
    for r in range(N):
        if ((d["wc"][r] == 0x7F) | (d["wc"][r] == 0xFF)).any(): b.append("wc: a code that is no number")
        s = mx_ref.live(d["ws"][r])
        if ((s != none) & ((s < least) | (s > most))).any(): b.append("ws: a scale out of range")
    return b
def reference(x, u, v, wc, ws):
    qu = [mx_ref.quantize(u[r]) for r in range(N)]
    lay = [pk(wc[r], ws[r]) for r in range(N)]
    now = [x[r] for r in range(N)]
    y, ol = np.zeros((N, 128, C), np.float32), np.zeros((N, 8, C), np.float32)
    oc, osc = np.zeros((N, 128, 4 * C), np.uint8), np.zeros((N, 16, C), np.uint8)
    for t in range(R):
        came, peak, key = [], [], []
        for r in range(N):
            p = mx_ref.matmul(qu[r], mx_ref.quantize(now[r]))
            e = np.sort(order(p)[:, :K], axis=1)
            a = np.take_along_axis((p[1::16] > 0) + 2 * (p[2::16] > 0) + 4 * (p[3::16] > 0), e, axis=1)
            peak.append(e)
            key.append(a + 8 * np.roll(a, -1, axis=1))
            came.append(decode(mx_ref.quantize(gcols(now[r], e))))
        made = []
        for r in range(N):
            o = (r + STEP[t]) % N
            at = (peak[o][:, None, :] - peak[r][:, :, None]) % C // 16
            same = key[o][:, None, :] == key[r][:, :, None]
            shift = np.array([16 * np.argmax(np.bincount(at[g][same[g]], minlength=C // 16)) for g in range(8)])
            place = (np.arange(C) + shift[:, None]) % C
            m = np.sum(peak[o][:, None, :] <= place[:, :, None], axis=2) - 1
            m = np.where(m < 0, K - 1, m)
            ol[r] = np.take_along_axis(peak[o], m, axis=1)
            own = now[r].astype(np.float32)
            z = ((own + gcols(came[o].astype(BF), m).astype(np.float32)) * np.float32(0.5)).astype(BF)
            q = mx_ref.quantize(z)
            made.append(tile([mx_ref.matmul(pick(lay[r], np.arange(128 * b, 128 * b + 128)), q) * np.float32(0.03125) + own[:, b::4] for b in range(4)]))
        now = made
    for r in range(N):
        q = mx_ref.quantize(now[r])
        y[r] = mx_ref.matmul(mx_ref.quantize(v[r]), q)
        oc[r], osc[r] = emit(q)
    return {"y": y, "ol": ol, "oc": oc, "osc": osc}

@@ -1,0 +1,477 @@
+from concourse.mybir import dt, AluOpType, AxisListType, ActivationFunctionType
+
+A = AluOpType
+F = ActivationFunctionType
+C, K, R, N = 384, 96, 3, 8
+HC = C // 2
+STEP = [1, 2, 3]
+BIG = 2.0 ** 90
+MAGIC = 1.5 * 2.0 ** 29
+CODE = "float8_e4m3fn_x4"
+
+SCRATCH = {}
+for _d, _l in (
+        ("bfloat16", dict(xin=4 * C, uin=512, vin=512, X=4 * C, Z=4 * C, Y=4 * C, Xh=3 * C, IB=2 * C, alt=2 * C, Dsb=4 * C, Dc=512,
+                          eone=528, ebf=528, c16=C, mask=C, keep=C, mbig=C, horn=72, sg=72, aH=80, AX=C, Arow=C, FL=8 * C, SC=8 * 192,
+                          JS=16 * C, gt=400, sgn=C, ge=C, cap=C, cnt=C, CH=C, g8=112, hrow=K, hm=K, hw=K, Hpos=R * C, Hm=C, T2=2 * C,
+                          EX=192, TX=192, hr4=C, E=24 * K, JE=24 * K, PX=192, TP=192, PR=112)),
+        ("float32", dict(cf=80, lc=16, lb=8, rstA=16, kpB=16, rstC=16, kpV=32, PV=16, W3=56, cS=16, pen=32, LH=32, Rr=48, EXT=96, TT=96,
+                         tv=8, cP=4, vt=32, vT=32, vs=32, vx=32, vy=32, mv=4, OL=C, ysb=C)),
+        ("uint16", dict(cu=96, po=8, off4=24, rot=2, moff=32)),
+        ("int32", dict(li=4)),
+        (CODE, dict(qu=128, qu2=C, qv=128, qw=512, qe=512, qz=C, qx0=C, qx1=C, qx2=C, qx3=C, lq0=C, lq1=C, lq2=C)),
+        ("uint8", dict(su=128, su2=C, sv=128, sw=512, se=512, sz=C, sx0=C, sx1=C, sx2=C, sx3=C, ls0=C, ls1=C, ls2=C))):
+    for _n in _l:
+        SCRATCH[_n] = ("sbuf", [128, _l[_n]], _d)
+SCRATCH["St"] = ("sbuf", [128, 24, 16], "float32")
+for _t in range(R):
+    for _n, _w in (("sa", 16), ("la", 16), ("sb", 24), ("lb", 64)):
+        SCRATCH["%s%d" % (_n, _t)] = ("sbuf", [128, _w], "bfloat16")
+for _b in range(8):
+    SCRATCH["p%d" % _b] = ("psum", [128, 512], "float32")
+
+SEMAPHORES = ["cV", "cS", "cT", "cG", "sent"] + ["d%d" % i for i in range(16)] + [a + str(t) for a in ("aq", "aa", "ab") for t in range(R)]
+
+O_A, O_T, O_H, O_P, O_V, O_U, O_G, O_L = 0, 24, 30, 42, 54, 56, 80, 86
+
+
+def rank_program(g, core, T, topo):
+    rank = T.rank_of(core)
+    if rank is None:
+        return
+    eng = {"V": g.vector, "S": g.scalar, "T": g.tensor, "G": g, "Y": g.sync}
+    csem = {"V": "cV", "S": "cS", "T": "cT", "G": "cG"}
+    count = {}
+    waited = {q: {} for q in eng}
+    lastw, readers = {}, {}
+    ndma = [0]
+
+    def need(q, toks):
+        best = {}
+        for (s, v) in toks:
+            if v > best.get(s, 0):
+                best[s] = v
+        for s in best:
+            if waited[q].get(s, 0) < best[s]:
+                eng[q].wait_ge(T.sem[s], best[s])
+                waited[q][s] = best[s]
+
+    def deps(q, Rd, W):
+        toks = []
+        for k in Rd.split():
+            toks += lastw.get(k, [])
+            if k[0] == "p" and k[1:].isdigit():
+                toks += [x for x in readers.get(k, []) if x[0] != csem.get(q)]
+        for k in W.split():
+            toks += lastw.get(k, []) + readers.get(k, [])
+        need(q, toks)
+
+    def done(tok, Rd, W):
+        for k in Rd.split():
+            readers.setdefault(k, []).append(tok)
+        for k in W.split():
+            lastw[k] = [tok]
+            readers[k] = []
+
+    def op(q, fn, Rd, W):
+        deps(q, Rd, W)
+        s = csem[q]
+        count[s] = count.get(s, 0) + 1
+        fn().then_inc(T.sem[s], 1)
+        done((s, count[s]), Rd, W)
+
+    def dma(q, out, in_, Rd, W):
+        deps(q, Rd, W)
+        sem = "d%d" % ndma[0]
+        ndma[0] += 1
+        count[sem] = 16
+        eng[q].dma_start(out, in_).then_inc(T.sem[sem], 16)
+        done((sem, 16), Rd, W)
+
+    V, S, PE = g.vector, g.scalar, g.tensor
+
+    def ks(p, *r):
+        return " ".join(p + str(i) for i in range(*r)) + " "
+
+    def ts(out, in0, s1, s2, o0, o1, Rd, W):
+        if o1 is None:
+            op("V", lambda: V.tensor_scalar(out, in0, s1, None, o0), Rd, W)
+        else:
+            op("V", lambda: V.tensor_scalar(out, in0, s1, s2, o0, o1), Rd, W)
+
+    def tt(out, a, b, o, Rd, W):
+        op("V", lambda: V.tensor_tensor(out, a, b, o), Rd, W)
+
+    def cp(out, a, Rd, W):
+        op("V", lambda: V.tensor_copy(out, a), Rd, W)
+
+    def scan(out, d0, d1, init, o0, o1, Rd, W):
+        op("V", lambda: V.tensor_tensor_scan(out, d0, d1, init, o0, o1), Rd, W)
+
+    def tr(out, a, Rd, W):
+        op("V", lambda: V.transpose(out, a), Rd, W)
+
+    def red(out, a, o, Rd, W):
+        op("V", lambda: V.tensor_reduce(out, a, AxisListType.X, o), Rd, W)
+
+    def ms(ap, c, W):
+        op("V", lambda: V.memset(ap, c), "", W)
+
+    def act(out, a, f, Rd, W, **kw):
+        op("S", lambda: S.activation(out, a, f, **kw), Rd, W)
+
+    def qmx(qn, sn, lo, hi, a, Rd, W):
+        op("V", lambda: V.quantize_mx(T[qn][:, lo:hi], T[sn][:, lo:hi], a), Rd, W)
+
+    def mm(bank, wq, wsn, wlo, mq, msn, Rd, lo=0, hi=C):
+        op("T", lambda: PE.matmul_mx(T["p%d" % bank][:, 0:hi - lo], T[wq][:, wlo:wlo + 128], T[wsn][:, wlo:wlo + 128],
+                                     T[mq][:, lo:hi], T[msn][:, lo:hi], True, True), Rd, "p%d" % bank)
+
+    def iota(out, pat, base, W):
+        op("G", lambda: g.iota(out, pat, base, 0, allow_small_or_imprecise_dtypes=True), "", W)
+
+    def send(t, out, in_, rsem, Rd):
+        dst = T.cores[(rank - STEP[t]) % N]
+        rid, pid, _ = topo.addr(dst)
+        deps("G", Rd, "")
+        g.remote_dma(out, in_, T.sem[rsem], T.sem.sent, pid, rid, topo.mask(core, dst))
+        count["sent"] = count.get("sent", 0) + len(topo.engines(core, dst))
+
+    for t in range(R):
+        n = len(topo.engines(T.cores[(rank + STEP[t]) % N], core))
+        for key, sem, m in (("lq", "aq", 2 * n), ("la", "aa", n), ("lb", "ab", n)):
+            lastw[key + str(t)] = [(sem + str(t), m)]
+            count[sem + str(t)] = m
+
+    dma("S", T.uin[:], T.u[:], "", "uin")
+    dma("Y", T.xin[:, 0:768], T.x[:, 0:768], "", "xa")
+    dma("S", T.xin[:, 768:1536], T.x[:, 768:1536], "", "xb")
+
+    cf, cu, lc, lb = T.cf, T.cu, T.lc, T.lb
+    St, PV, FL, SC, JS = T.St, T.PV, T.FL, T.SC, T.JS
+    iota(cf[:, O_U:O_U + 16], [[16, 2], [32, 4], [0, 2]], 0, "cf0")
+    iota(cf[:, O_U + 16:O_U + 24], [[16, 8]], 0, "cf1")
+    op("G", lambda: g.iota(T.li[:, 0:1], [[0, 1]], 0, 1), "", "li0")
+    iota(T.c16[:], [[0, 24], [1, 16]], 0, "c16")
+    iota(cf[:, O_A:O_A + 24], [[3, 24]], 2, "cf2")
+    iota(cf[:, O_T:O_T + 6], [[8, 6]], 7, "cf3")
+    iota(cf[:, O_H:O_H + 24], [[-6, 2], [1, 6], [0, 2]], 6, "cf4")
+    iota(cf[:, O_V:O_V + 2], [[16, 2]], 15, "cf5")
+    ms(T.eone[:], 1.0, "eone")
+    op("G", lambda: g.affine_select(T.ebf[:], T.eone[:], [[-1, 528]], A.is_equal, 0.0, 3, 4), "eone", "ebf")
+
+    ms(T.rstA[:], 4 * BIG, "rstA")
+    ms(T.kpB[:], 1.0, "kpB")
+    ms(T.kpV[:], 1.0, "kpV")
+    ms(T.horn[:], 2.0, "horn")
+    ms(T.gt[:, C:400], 0.0, "gtx")
+    ms(T.aH[:, 72:80], 0.0, "aHx")
+    ms(T.cS[:], 0.0, ks("cS", 16))
+    ms(T.rstA[:, 0::8], -4 * BIG, "rstA")
+    ms(T.kpB[:, 0::8], 0.0, "kpB")
+    ms(T.kpV[:, 0::16], 0.0, "kpV")
+    ms(T.horn[:, 0::3], 0.0, "horn")
+    ms(T.kpB[:, 4::8], 2.0, "kpB")
+    act(T.rstC[:], T.rstA[:], F.Copy, "rstA", "rstC", scale=-1.0)
+    act(T.sa0[:, 8:16], T.eone[:, 0:8], F.Copy, "eone", "sad0", scale=0.0)
+    act(T.Hpos[:, 0:C], T.eone[:, 0:C], F.Copy, "eone", "Hpos0", scale=0.0)
+    cp(cu[:, O_U:O_U + 24], cf[:, O_U:O_U + 24], "cf0 cf1", "cuU")
+    ts(T.li[:, 1:2], T.li[:, 0:1], 15, None, A.bitwise_and, None, "li0", "li1")
+    ts(T.li[:, 2:3], T.li[:, 0:1], 31, None, A.bitwise_and, None, "li0", "li2")
+    cp(lb[:, 0:2], T.li[:, 1:3], "li1 li2", "lane")
+    ts(lc[:, 0:6], cf[:, O_U + 16:O_U + 22], lb[:, 0:1], 0.5, A.add, A.add, "cf1 lane", "lc0")
+    ts(lc[:, 6:8], cf[:, O_U + 16:O_U + 18], lb[:, 0:1], 31.0, A.add, A.add, "cf1 lane", "lc1")
+    ts(lc[:, 8:9], lb[:, 1:2], -1.0, 31.0, A.mult, A.add, "lane", "lc2")
+    ts(cu[:, O_G:O_G + 6], cf[:, O_U + 16:O_U + 22], 2.0, lb[:, 1:2], A.mult, A.add, "cf1 lane", "cuG")
+    ts(lb[:, 2:4], T.kpV[:, 1:3], lb[:, 0:1], 7.5, A.mult, A.is_gt, "kpV lane", "laneq")
+    ts(lb[:, 4:5], lb[:, 0:1], 2.0, None, A.mult, None, "lane", "laner")
+    ts(T.mask[:], T.c16[:], lb[:, 0:1], None, A.is_equal, None, "c16 lane", "mask")
+    ts(cu[:, O_L:O_L + 2], lb[:, 2:4], -15.0, lb[:, 4:5], A.mult, A.add, "laneq laner", "cuL")
+    cp(cu[:, 0:O_U], cf[:, 0:O_U], "cf2 cf3 cf4 cf5", "cu")
+    act(T.keep[:], T.mask[:], F.Identity, "mask", "keep", scale=-1.0, bias=1.0)
+    act(T.mbig[:], T.mask[:], F.Copy, "mask", "mbig", scale=256.0)
+    qmx("qu", "su", 0, 128, T.uin[:], "uin", "qu")
+    uoff = cu[:, O_U:O_U + 24]
+    cp(T.qu2[:].bitcast(dt.uint32), T.qu[:].bitcast(dt.uint32).indirect(uoff), "qu cuU", "qu2")
+    act(T.su2[:], T.su[:].indirect(uoff), F.Copy, "qu cuU", "su2")
+
+    def first_half(t, src, Rd):
+        qx, sx = "qx%d" % t, "sx%d" % t
+        qmx(qx, sx, 0, HC, src[:, 0:4 * HC], Rd, qx + "a")
+        if t < R:
+            mm(3, "qu", "su", 0, qx, sx, "qu %sa" % qx, 0, HC)
+        else:
+            mm(3, "qv", "sv", 0, qx, sx, "qv %sa" % qx, 0, HC)
+            dma("Y", T.oc[:, 0:4 * HC], T[qx][:, 0:HC].bitcast(dt.uint8), qx + "a", "")
+
+    def w3(i, h):
+        return T.W3[:, 8 * i + 4 * h:8 * i + 4 * h + 4]
+
+    def sort3(h):
+        a, b, c = (St[:, 12 * h + 4 * i:12 * h + 4 * i + 4, 0] for i in range(3))
+        k, s = "S" + "ab"[h], str(h)
+        tt(w3(0, h), a, b, A.max, k, "mx" + s)
+        tt(w3(1, h), a, b, A.min, k, "mn" + s)
+        tt(w3(2, h), w3(0, h), c, A.min, k + " mx" + s, "tq" + s)
+        tt(w3(3, h), w3(0, h), c, A.max, k + " mx" + s, "hi" + s)
+        tt(PV[:, 4 * h:4 * h + 4], w3(1, h), w3(2, h), A.max, "mn%s tq%s" % (s, s), "PV" + s)
+
+    def spass(c):
+        bank = "p4" if c % 2 else "p0"
+        act(JS[:, C * c:C * c + C], T[bank][:, 0:C], F.Sign, bank + " PV%d" % (c // 4), "JS%d cS%d" % (c, c),
+            bias=PV[:, c:c + 1], scale=-1.0, accum_out=T.cS[:, c:c + 1])
+
+    def vpass(c):
+        m = c // 2
+        ts(FL[:, C * m:C * m + C], T.p1[:, 0:C], PV[:, c:c + 1], None, A.is_gt, None, "p1 PV%d" % (c // 4), "FL%d" % m)
+
+    def vsum(c):
+        m = c // 2
+        scan(SC[:, 192 * m:192 * m + 192], FL[:, C * m:C * m + 192], FL[:, C * m + 192:C * m + C], 0.0, A.add, A.add, "FL%d" % m, "SC%d" % m)
+
+    def second(h):
+        tt(w3(6, h), w3(3, h), w3(5, h), A.add, "hi%d q%da q%db" % (h, h, h), "tm%d" % h)
+        tt(PV[:, 8 + 4 * h:12 + 4 * h], w3(6, h), w3(4, h), A.max, "tm%d lo" % h, "PV%d" % (2 + h))
+
+    def halves(t, bs):
+        for b in bs:
+            out = T.Xh[:, C * b:C * b + C] if b < 3 else T.IB[:, 1::2]
+            if t == 0:
+                act(out, T.xin[:, b::4], F.Copy, "xa xb", "Xh%d" % b, scale=0.5)
+            else:
+                act(out, T.Y[:, C * b:C * b + C], F.Copy, "Y%d Y%d" % (b, b + 4), "Xh%d" % b, scale=2.0 ** -6)
+
+    def unpack(t, bs):
+        for b in bs:
+            mm(4 + b, "qe", "se", 128 * b, "lq%d" % t, "ls%d" % t, "qe%d lq%d" % (b, t))
+
+    def halve_d(bs):
+        for b in bs:
+            act(T.Dsb[:, C * b:C * b + C], T["p%d" % (4 + b)][:, 0:C], F.Copy, "p%d" % (4 + b), "Dsb%d" % b, scale=0.5)
+
+    first_half(0, T.xin, "xa")
+    tr(St[:, 0:12, :], T.p3[:, 0:HC], "p3", "Sa")
+    qmx("qx0", "sx0", HC, C, T.xin[:, 4 * HC:4 * C], "xb", "qx0b")
+    dma("Y", T.qw[:].bitcast(dt.uint8), T.wc[:], "xa xb", "qw")
+    dma("Y", T.sw[:], T.ws[:], "", "sw")
+    dma("Y", T.vin[:], T.v[:], "", "vin")
+
+    for t in range(R):
+        qx, sx, lq, ls, sa, la, sb, lbn = ("%s%d" % (s, t) for s in ("qx", "sx", "lq", "ls", "sa", "la", "sb", "lb"))
+        SA, LA, SB, LB = T[sa], T[la], T[sb], T[lbn]
+        qk = "%sa %sb" % (qx, qx)
+        u2 = "qu2 su2 " + qk
+        mm(7, "qu", "su", 0, qx, sx, "qu " + qk, HC, C)
+        mm(0, "qu2", "su2", 0, qx, sx, u2)
+        mm(1, "qu2", "su2", 128, qx, sx, u2)
+        mm(4, "qu2", "su2", 128, qx, sx, u2)
+        mm(2, "qu2", "su2", 256, qx, sx, u2)
+        mm(3, "qu2", "su2", 256, qx, sx, u2)
+        send(t, T[lq][:].bitcast(dt.uint8), T[qx][:].bitcast(dt.uint8), "aq%d" % t, qk)
+        send(t, T[ls][:], T[sx][:], "aq%d" % t, qk)
+        sort3(0)
+        for c in (0, 2, 1, 3):
+            spass(c)
+        tr(St[:, 12:24, :], T.p7[:, 0:HC], "p7", "Sb")
+        sort3(1)
+        spass(4)
+        spass(6)
+        vpass(5)
+        tt(T.W3[:, 32:40], T.W3[:, 8:16], T.W3[:, 16:24], A.min, "mn0 mn1 tq0 tq1", "lo")
+        vpass(7)
+        vsum(5)
+        ts(T.sg[:], St[:, :, 1:4], 0.0, None, A.is_gt, None, "Sa Sb", "sg")
+        vsum(7)
+        ts(w3(5, 0), T.cS[:, 0:4], 192.5, -BIG, A.is_gt, A.mult, ks("cS", 4), "q0a q0b")
+        ts(T.W3[:, 45:48:2], SC[:, 575:768:192], 95.5, -BIG, A.is_lt, A.mult, "SC2 SC3", "q1b")
+        second(0)
+        spass(8)
+        spass(10)
+        vpass(9)
+        ts(T.W3[:, 44:48:2], T.cS[:, 4:8:2], 192.5, -BIG, A.is_gt, A.mult, "cS4 cS6", "q1a")
+        vsum(9)
+        second(1)
+        spass(15)
+        spass(12)
+        spass(14)
+        vpass(11)
+        scan(T.aH[:, 0:72], T.horn[:], T.sg[:], 0.0, A.mult, A.add, "horn sg", "aH")
+        vpass(13)
+        vsum(11)
+        vsum(13)
+        act(T.AX[:], T.aH[:].indirect(cu[:, O_A:O_A + 24]), F.Copy, "aH aHx cu", "AX")
+        halves(t, (0, 1))
+        ts(T.pen[:, 8:16], T.cS[:, 1::2], 192.5, -BIG, A.is_gt, A.mult, "cS1 cS3 cS15", "penb")
+        ts(T.pen[:, 10:15], SC[:, 575:1344:192], 95.5, -BIG, A.is_lt, A.mult, ks("SC", 2, 7), "penb")
+        ts(T.pen[:, 24:32], T.pen[:, 8:16], BIG, None, A.add, None, "penb", "pend")
+        ts(T.pen[:, 0:8], T.cS[:, 0::2], 192.5, -BIG, A.is_gt, A.mult, ks("cS", 0, 16, 2), "pena")
+        ts(T.pen[:, 16:24], T.cS[:, 0::2], 192.5, BIG, A.is_lt, A.mult, ks("cS", 0, 16, 2), "penc")
+        scan(T.Rr[:, 32:48], T.kpB[:], T.pen[:, 0:16], 0.0, A.mult, A.add, "kpB pena penb", "Rc")
+        tt(T.LH[:], PV[:].indirect(cu[:, O_L:O_L + 2]), T.pen[:], A.add, ks("PV", 4) + "cuL pena penb penc pend", "LH")
+        scan(T.Rr[:, 0:16], T.rstA[:], T.LH[:, 0:16], 0.0, A.min, A.max, "rstA LH", "Ra")
+        scan(T.Rr[:, 16:32], T.rstC[:], T.LH[:, 16:32], 0.0, A.max, A.min, "rstC LH", "Rb")
+        cp(T.EXT[:], T.Rr[:].indirect(cu[:, O_T:O_T + 6]), "Ra Rb Rc cu", "EXT")
+        tr(T.TT[:], T.EXT[:], "EXT", "TT")
+        if t > 0:
+            unpack(t, (1, 2, 3, 0))
+        red(T.tv[:, 0:1], T.TT[:, 64:96], A.add, "TT", "tv0")
+        red(T.tv[:, 3:4], T.TT[:, 0:32], A.max, "TT", "tv3")
+        ts(T.tv[:, 1:2], T.tv[:, 0:1], -95.5 * BIG, -4 * BIG, A.is_gt, A.mult, "tv0", "tv1")
+        red(T.tv[:, 4:5], T.TT[:, 32:64], A.min, "TT", "tv4")
+        ts(T.tv[:, 2:3], T.tv[:, 1:2], T.tv[:, 4:5], T.tv[:, 3:4], A.add, A.max, "tv1 tv3 tv4", "tv2")
+        act(T.sgn[:], T.p3[:, 0:C], F.Sign, "p3 tv2", "sgn", bias=T.tv[:, 2:3], scale=-1.0)
+        ts(T.gt[:, 0:C], T.p2[:, 0:C], T.tv[:, 2:3], None, A.is_gt, None, "p2 tv2", "gt")
+        if t == 0:
+            ms(T.po[:], 0, "poa pob poc")
+        scan(T.cap[:, ::-1], T.eone[:, 0:C], T.gt[:, C:0:-1], 96.0, A.mult, A.subtract, "eone gt gtx", "cap")
+        ts(T.ge[:], T.sgn[:], 0.5, None, A.is_lt, None, "sgn", "ge")
+        scan(T.cnt[:], T.ge[:], T.cap[:], 0.0, A.add, A.min, "ge cap", "cnt")
+        if t > 0:
+            halve_d((1,))
+        else:
+            halves(t, (2,))
+        for s in range(3):
+            act(JS[:, C * s:C * s + 336], T.cnt[:, 0:336], F.Sign, "cnt lc0", "JS%d cP%d" % (s, s),
+                bias=lc[:, s:s + 1], scale=-1.0, accum_out=T.cP[:, s:s + 1])
+        for s in range(3):
+            ts(FL[:, C * s:C * s + 336], T.cnt[:, 48:C], lc[:, 3 + s:4 + s], None, A.is_le, None, "cnt lc0", "FL%d" % s)
+        for s in range(3):
+            o = C * s
+            scan(SC[:, 192 * s:192 * s + 168], FL[:, o:o + 168], FL[:, o + 168:o + 336], -168.0, A.add, A.add, "FL%d" % s, "SC%d" % s)
+        tr(T.Arow[:], T.AX[:], "AX", "Arow")
+        ts(T.po[:, 3:6], SC[:, 167:576:192], 216.0, None, A.add, None, ks("SC", 3), "pob")
+        ts(T.po[:, 6:7], T.cP[:, 0:1], 0.5, 168.0, A.mult, A.add, "cP0", "poc")
+        ts(T.po[:, 0:3], T.cP[:, 0:3], 0.5, 168.0, A.mult, A.add, ks("cP", 3), "poa")
+        if t > 0:
+            halve_d((2, 3, 0))
+            halves(t, (2, 3))
+        else:
+            halves(t, (3,))
+            act(T.Y[:, 0:3 * C], T.Xh[:], F.Copy, ks("Xh", 3), ks("Y", 3) + ks("Y", 4, 7), scale=64.0)
+        ts(T.g8[:], T.Arow[:].indirect(T.po[:, 0:7]), 8.0, 1.0, A.mult, A.add, "Arow poa pob poc", "g8")
+        tt(T.hrow[:], T.Arow[:].indirect(T.po[:, 0:6]), T.g8[:, 1:97], A.add, "Arow g8 poa pob", "hrow")
+        ts(SA[:, 0:6], T.po[:, 0:6], -192.0, None, A.add, None, "poa pob", "saa%d" % t)
+        scan(T.hm[:], T.hrow[:], T.mask[:, 0:K], 0.0, A.max, A.mult, "hrow mask", "hm")
+        scan(T.hw[:], T.keep[:, 0:K], T.hm[:], 0.0, A.mult, A.add, "hm keep", "hw")
+        cp(SA[:, 6:12], T.hw[:, 15::16], "hw", "sad%d" % t)
+        send(t, LA[:], SA[:], "aa%d" % t, "saa%d sad%d" % (t, t))
+        if t == 0:
+            for b in range(4):
+                qmx("qe", "se", 128 * b, 128 * b + 128, T.ebf[:, 3 - b:515 - b], "ebf", "qe%d" % b)
+            unpack(t, range(4))
+            halve_d(range(4))
+        H = T.Hpos[:, C * t:C * t + C]
+        cp(H.indirect(T.po[:, 0:6]), T.hrow[:], "hrow poa pob", "Hpos%d" % t)
+        scan(T.CH[:], T.mbig[:], T.cnt[:], 0.0, A.add, A.min, "mbig cnt", "CH")
+        scan(T.Hm[:], H, T.mask[:], 0.0, A.max, A.mult, "Hpos%d mask" % t, "Hm")
+        cp(SB[:], T.CH[:, 15::16], "CH", sb)
+        send(t, LB[:, 0:24], SB[:], "ab%d" % t, sb)
+        scan(T.T2[:, 0:C], T.keep[:], T.Hm[:], 0.0, A.mult, A.add, "Hm keep", "T2a")
+        ms(LB[:, 24:64], 0.0, "lbx%d" % t)
+        scan(T.T2[:, C:2 * C], T.keep[:], T.Hm[:], T.T2[:, C - 1:C], A.mult, A.add, "Hm keep T2a", "T2b")
+        if t == 0:
+            ms(T.vt[:, 24:32], 0.0, "vtx")
+        if t == R - 1:
+            qmx("qv", "sv", 0, 128, T.vin[:], "vin", "qv")
+            ms(T.PR[:, 0:16], 0.0, "PRx")
+        else:
+            ms(T["sa%d" % (t + 1)][:, 8:16], 0.0, "sad%d" % (t + 1))
+        if t == 1:
+            ms(T.Hpos[:, 2 * C:3 * C], 0.0, "Hpos2")
+        cp(T.EX[:], LA[:].indirect(cu[:, O_H:O_H + 12]), la + " cu", "EX")
+        for j in (3, 2, 1, 0):
+            ts(T.off4[:, 6 * j:6 * j + 6], LA[:, 0:6], float(240 - 16 * j), None, A.add, None, la, "off%d" % j)
+            if j == 3:
+                tr(T.TX[:], T.EX[:], "EX", "TX")
+            if j == 2:
+                cp(T.hr4[:, 0:K], T.TX[:].indirect(cu[:, O_G:O_G + 6]), "TX cuG", "hra")
+        if t > 0:
+            act(T.hr4[:, K:2 * K], T.hr4[:, 0:K], F.Copy, "hra", "hrb")
+        else:
+            cp(T.hr4[:, K:2 * K], T.hr4[:, 0:K], "hra", "hrb")
+        cp(T.hr4[:, 2 * K:3 * K], T.hr4[:, 0:K], "hra", "hrc")
+        cp(T.hr4[:, 3 * K:4 * K], T.hr4[:, 0:K], "hra", "hrd")
+
+        def compact():
+            for b in range(4):
+                act(T.Dc[:, 128 * b + 16:128 * b + 112], T.Dsb[:, C * b:C * b + C].indirect(T.off4[:, 18:24]), F.Copy,
+                    "Dsb%d off3" % b, "Dc%d" % b)
+            act(T.Dc[:, 15::128], T.Dc[:, 111::128], F.Copy, ks("Dc", 4), "Dcx")
+
+        if t > 0:
+            compact()
+        else:
+            act(T.Dc[:], T.eone[:, 0:512], F.Copy, "eone", ks("Dc", 4) + "Dcx", scale=0.0)
+        act(LB[:, 24:48], LB[:, 0:24], F.Copy, lbn, "lbx%d" % t)
+        for i in range(6):
+            tt(T.E[:, C * i:C * i + C], T.T2[:, 336 - 64 * i:2 * C].indirect(T.off4[:]), T.hr4[:], A.is_equal,
+               "T2a T2b hra hrb hrc hrd " + ks("off", 4), "E%d" % i)
+            for bn in range(4 * i, 4 * i + 4):
+                if bn < 22:
+                    act(T.JE[:, K * bn:K * bn + K], T.E[:, K * bn:K * bn + K], F.Identity, "E%d" % i, "JE%d vt%d" % (bn, bn),
+                        accum_out=T.vt[:, bn:bn + 1])
+                else:
+                    red(T.vt[:, bn:bn + 1], T.E[:, K * bn:K * bn + K], A.add, "E5", "vt%d" % bn)
+        if t == 0:
+            compact()
+        if t == R - 1:
+            act(T.PX[:], LA[:].indirect(cu[:, O_P:O_P + 12]), F.Copy, la + " cu", "PX")
+        tr(T.vT[:], T.vt[:], ks("vt", 24) + "vtx", "vT")
+        scan(T.vs[:], T.kpV[:], T.vT[:], 0.0, A.mult, A.add, "kpV vT", "vs")
+        ts(T.vx[:], T.vs[:].indirect(cu[:, O_V:O_V + 2]), 64.0, lc[:, 8:9], A.mult, A.add, "vs cu lc2", "vx")
+        if t == 0:
+            ms(T.alt[:], 1.0, "alt")
+        tr(T.vy[:], T.vx[:], "vx", "vy")
+        if t == R - 1:
+            tr(T.TP[:], T.PX[:], "PX", "TP")
+            act(T.PR[:, 16:112], T.TP[:].indirect(cu[:, O_G:O_G + 6]), F.Copy, "TP cuG", "PR")
+            act(T.PR[:, 15:16], T.PR[:, 111:112], F.Copy, "PR", "PRx")
+        red(T.mv[:, 0:1], T.vy[:], A.max, "vy", "mv0")
+        if t == 0:
+            ms(T.alt[:, 0::2], 0.0, "alt")
+        ts(T.mv[:, 1:2], T.mv[:, 0:1], MAGIC, MAGIC, A.add, A.subtract, "mv0", "mv1")
+        ts(T.rot[:], lc[:, 6:8], T.mv[:, 0:1], T.mv[:, 1:2], A.subtract, A.add, "lc1 mv0 mv1", "rot")
+        ts(T.moff[:], LB[:].indirect(T.rot[:]), 15.0, None, A.add, None, lbn + " rot lbx%d" % t, "moff")
+        mo = T.moff[:, 0:24]
+        act(T.IB[:, 0::2], T.Dc[:, 384:496].indirect(mo), F.Copy, "Dc3 Dcx moff", "IB")
+        for b in (0, 3, 1, 2):
+            if b == 3:
+                scan(T.Z[:, 1::2], T.alt[:], T.IB[:], 0.0, A.mult, A.add, "alt IB Xh3", "Z1 Z3")
+            else:
+                tt(T.Z[:, b::4], T.Dc[:, 128 * b:128 * b + 112].indirect(mo), T.Xh[:, C * b:C * b + C], A.add,
+                   "Dc%d Xh%d Dcx moff" % (b, b), "Z%d" % b)
+        if t == 0:
+            act(T.Y[:, 3 * C:4 * C], T.xin[:, 3::4], F.Copy, "xa xb", "Y3 Y7", scale=32.0)
+            act(T.Hpos[:, C:2 * C], T.eone[:, 0:C], F.Copy, "eone", "Hpos1", scale=0.0)
+        if t == R - 1:
+            act(T.OL[:], T.PR[:].indirect(mo), F.Identity, "PR PRx moff", "OL", bias=192.0)
+            dma("S", T.ol[:], T.OL[0::16, :], "OL", "")
+        for h in range(2):
+            qmx("qz", "sz", HC * h, HC * h + HC, T.Z[:, 4 * HC * h:4 * HC * (h + 1)], ks("Z", 4), "qz%d" % h)
+            for b in range(4):
+                mm(4 * h + b, "qw", "sw", 128 * b, "qz", "sz", "qw sw qz%d" % h, HC * h, HC * h + HC)
+        for i in range(8):
+            h, b = i // 4, i % 4
+            Yb = T.Y[:, C * b + HC * h:C * b + HC * h + HC]
+            Xb = T.X[:, 4 * HC * h + b:4 * HC * (h + 1):4]
+            tt(Yb, T["p%d" % i][:, 0:HC], Yb, A.add, "p%d Y%d" % (i, i), "Y%d" % i)
+            if i < 7:
+                act(Xb, Yb, F.Copy, "Y%d" % i, "X%d" % i, scale=2.0 ** -5)
+            if i == 5:
+                first_half(t + 1, T.X, ks("X", 4))
+        if t < R - 1:
+            tr(St[:, 0:12, :], T.p3[:, 0:HC], "p3", "Sa")
+        else:
+            act(T.ysb[:, 0:HC], T.p3[:, 0:HC], F.Copy, "p3", "ya")
+            dma("S", T.y[:, 0:HC], T.ysb[:, 0:HC], "ya", "")
+        ts(Xb, Yb, 2.0 ** -5, None, A.mult, None, "Y7", "X7")
+        qmx("qx%d" % (t + 1), "sx%d" % (t + 1), HC, C, T.X[:, 4 * HC:4 * C], ks("X", 4, 8), "qx%db" % (t + 1))
+
+    qx, sx = "qx%d" % R, "sx%d" % R
+    mm(0, "qv", "sv", 0, qx, sx, "qv %sb" % qx, HC, C)
+    dma("Y", T.oc[:, 4 * HC:4 * C], T[qx][:, HC:C].bitcast(dt.uint8), qx + "b", "")
+    for k in range(4):
+        dma("S", T.osc[4 * k:4 * k + 4, :], T[sx][32 * k:32 * k + 4, :], "%sa %sb" % (qx, qx), "")
+    cp(T.ysb[:, HC:C], T.p0[:, 0:HC], "p0", "yb")
+    dma("Y", T.y[:, HC:C], T.ysb[:, HC:C], "yb", "")
+    need("G", [(s, count[s]) for s in count])

@@ -5,34 +5,37 @@ F = ActivationFunctionType
 C, K, R, N = 384, 96, 3, 8
 HC = C // 2
 STEP = [1, 2, 3]
-BIG = 2.0 ** 90
-MAGIC = 1.5 * 2.0 ** 29
+H = 2.0 ** 88
+B = 2.0 ** 97
+PAD = 48
+WIN = 304
 CODE = "float8_e4m3fn_x4"
 
 SCRATCH = {}
 for _d, _l in (
-        ("bfloat16", dict(xin=4 * C, uin=512, vin=512, X=4 * C, Z=4 * C, Y=4 * C, Xh=3 * C, IB=2 * C, alt=2 * C, Dsb=4 * C, Dc=512,
-                          eone=528, ebf=528, c16=C, mask=C, keep=C, mbig=C, horn=72, sg=72, aH=80, AX=C, Arow=C, FL=8 * C, SC=8 * 192,
-                          JS=16 * C, gt=400, sgn=C, ge=C, cap=C, cnt=C, CH=C, g8=112, hrow=K, hm=K, hw=K, Hpos=R * C, Hm=C, T2=2 * C,
-                          EX=192, TX=192, hr4=C, E=24 * K, JE=24 * K, PX=192, TP=192, PR=112)),
-        ("float32", dict(cf=80, lc=16, lb=8, rstA=16, kpB=16, rstC=16, kpV=32, PV=16, W3=56, cS=16, pen=32, LH=32, Rr=48, EXT=96, TT=96,
-                         tv=8, cP=4, vt=32, vT=32, vs=32, vx=32, vy=32, mv=4, OL=C, ysb=C)),
-        ("uint16", dict(cu=96, po=8, off4=24, rot=2, moff=32)),
+        ("bfloat16", dict(xin=4 * C, uin=512, vin=512, X=4 * C, Z=4 * C, Y=4 * C, Xh=2 * C, IB2=2 * C, IB3=2 * C, alt=C, Dsb=4 * C, Dc=512,
+                          eone=528, ebf=528, c16=400, mask=400, keep=400, mbig=C, m8=K, kp16=K, horn=72, sg=72, aH=72, AX=C, Arow=PAD + C,
+                          FL=6 * C, ZB=16 * HC, JS=16 * C, gt=400, sgn=C, ge=C, cap=C, cnt=C, CH=C, SC=2 * WIN, G=K, G8=112, S1=K, S2=K,
+                          hrow=K, Hpos=R * (PAD + C), Hm=400, T2=784, hr4=C, E=24 * K, JE=24 * K, htab=80)),
+        ("float32", dict(cf=64, lc=16, lb=8, D0=16, D1=16, E0=16, E1=16, MM=32, cS=16, LL=48, LU=48, LN=48, kpN=24, kpF=48, TT=112, tz=2, TS=32,
+                         cP=2, vt=32, vy=64, mv=2, OL=C, ysb=C, ptab=C, PR=112)),
+        ("uint16", dict(cu=48, rot=2, moff=32)),
         ("int32", dict(li=4)),
-        (CODE, dict(qu=128, qu2=C, qv=128, qw=512, qe=512, qz=C, qx0=C, qx1=C, qx2=C, qx3=C, lq0=C, lq1=C, lq2=C)),
-        ("uint8", dict(su=128, su2=C, sv=128, sw=512, se=512, sz=C, sx0=C, sx1=C, sx2=C, sx3=C, ls0=C, ls1=C, ls2=C))):
+        (CODE, dict(qu=128, qu2=256, qu3=128, qv=128, qw=512, qe=512, qz=C, qx0=C, qx1=C, qx2=C, qx3=C, lq0=C, lq1=C, lq2=C)),
+        ("uint8", dict(su=128, su2=256, su3=128, sv=128, sw=512, se=512, sz=C, sx0=C, sx1=C, sx2=C, sx3=C, ls0=C, ls1=C, ls2=C))):
     for _n in _l:
         SCRATCH[_n] = ("sbuf", [128, _l[_n]], _d)
 SCRATCH["St"] = ("sbuf", [128, 24, 16], "float32")
+SCRATCH["RR"] = ("sbuf", [128, 6, 24], "float32")
+for _n in ("vT", "vS"):
+    SCRATCH[_n] = ("sbuf", [128, 2, 48], "float32")
 for _t in range(R):
-    for _n, _w in (("sa", 16), ("la", 16), ("sb", 24), ("lb", 64)):
-        SCRATCH["%s%d" % (_n, _t)] = ("sbuf", [128, _w], "bfloat16")
+    for _n, _w, _d in (("sa", 18, "uint16"), ("la", 36, "uint16"), ("sb", 24, "bfloat16"), ("lb", 48, "bfloat16")):
+        SCRATCH["%s%d" % (_n, _t)] = ("sbuf", [128, _w], _d)
 for _b in range(8):
     SCRATCH["p%d" % _b] = ("psum", [128, 512], "float32")
 
 SEMAPHORES = ["cV", "cS", "cT", "cG", "sent"] + ["d%d" % i for i in range(16)] + [a + str(t) for a in ("aq", "aa", "ab") for t in range(R)]
-
-O_A, O_T, O_H, O_P, O_V, O_U, O_G, O_L = 0, 24, 30, 42, 54, 56, 80, 86
 
 
 def rank_program(g, core, T, topo):
@@ -120,6 +123,9 @@ def rank_program(g, core, T, topo):
     def act(out, a, f, Rd, W, **kw):
         op("S", lambda: S.activation(out, a, f, **kw), Rd, W)
 
+    def const(out, n, c, W):
+        act(out, T.eone[:, 0:n], F.Copy, "eone", W, scale=float(c))
+
     def qmx(qn, sn, lo, hi, a, Rd, W):
         op("V", lambda: V.quantize_mx(T[qn][:, lo:hi], T[sn][:, lo:hi], a), Rd, W)
 
@@ -148,326 +154,368 @@ def rank_program(g, core, T, topo):
     dma("S", T.xin[:, 768:1536], T.x[:, 768:1536], "", "xb")
 
     cf, cu, lc, lb = T.cf, T.cu, T.lc, T.lb
-    St, PV, FL, SC, JS = T.St, T.PV, T.FL, T.SC, T.JS
-    iota(cf[:, O_U:O_U + 16], [[16, 2], [32, 4], [0, 2]], 0, "cf0")
-    iota(cf[:, O_U + 16:O_U + 24], [[16, 8]], 0, "cf1")
+    St, MM, FL, JS, cS = T.St, T.MM, T.FL, T.JS, T.cS
+    ZW = lambda a, b, s=1: T.ZB[:, 16 * (HC - 1) + a:16 * (HC - 1) + b:s]
+    iota(cf[:, 0:16], [[16, 2], [32, 4], [0, 2]], 0, "cf0")
+    iota(cf[:, 16:24], [[16, 8]], 0, "cf1")
     op("G", lambda: g.iota(T.li[:, 0:1], [[0, 1]], 0, 1), "", "li0")
-    iota(T.c16[:], [[0, 24], [1, 16]], 0, "c16")
-    iota(cf[:, O_A:O_A + 24], [[3, 24]], 2, "cf2")
-    iota(cf[:, O_T:O_T + 6], [[8, 6]], 7, "cf3")
-    iota(cf[:, O_H:O_H + 24], [[-6, 2], [1, 6], [0, 2]], 6, "cf4")
-    iota(cf[:, O_V:O_V + 2], [[16, 2]], 15, "cf5")
     ms(T.eone[:], 1.0, "eone")
     op("G", lambda: g.affine_select(T.ebf[:], T.eone[:], [[-1, 528]], A.is_equal, 0.0, 3, 4), "eone", "ebf")
+    iota(cf[:, 24:48], [[3, 24]], 2, "cf2")
+    iota(T.c16[:], [[0, 25], [1, 16]], 0, "c16")
+    iota(T.htab[:], [[1, 80]], 0, "htab")
 
-    ms(T.rstA[:], 4 * BIG, "rstA")
-    ms(T.kpB[:], 1.0, "kpB")
-    ms(T.kpV[:], 1.0, "kpV")
-    ms(T.horn[:], 2.0, "horn")
     ms(T.gt[:, C:400], 0.0, "gtx")
-    ms(T.aH[:, 72:80], 0.0, "aHx")
-    ms(T.cS[:], 0.0, ks("cS", 16))
-    ms(T.rstA[:, 0::8], -4 * BIG, "rstA")
-    ms(T.kpB[:, 0::8], 0.0, "kpB")
-    ms(T.kpV[:, 0::16], 0.0, "kpV")
-    ms(T.horn[:, 0::3], 0.0, "horn")
-    ms(T.kpB[:, 4::8], 2.0, "kpB")
-    act(T.rstC[:], T.rstA[:], F.Copy, "rstA", "rstC", scale=-1.0)
-    act(T.sa0[:, 8:16], T.eone[:, 0:8], F.Copy, "eone", "sad0", scale=0.0)
-    act(T.Hpos[:, 0:C], T.eone[:, 0:C], F.Copy, "eone", "Hpos0", scale=0.0)
-    cp(cu[:, O_U:O_U + 24], cf[:, O_U:O_U + 24], "cf0 cf1", "cuU")
+    ms(T.vt[:, 24:32], 0.0, "vtx")
+    ms(T.kpF[:], 1.0, "kpF")
+    ms(T.vT[:, :, 16:48], 0.0, "vTx")
+    cp(cu[:, 0:24], cf[:, 0:24], "cf0 cf1", "cuU")
     ts(T.li[:, 1:2], T.li[:, 0:1], 15, None, A.bitwise_and, None, "li0", "li1")
     ts(T.li[:, 2:3], T.li[:, 0:1], 31, None, A.bitwise_and, None, "li0", "li2")
+    ms(T.kpF[:, 16:17], 64.0, "kpF")
     cp(lb[:, 0:2], T.li[:, 1:3], "li1 li2", "lane")
-    ts(lc[:, 0:6], cf[:, O_U + 16:O_U + 22], lb[:, 0:1], 0.5, A.add, A.add, "cf1 lane", "lc0")
-    ts(lc[:, 6:8], cf[:, O_U + 16:O_U + 18], lb[:, 0:1], 31.0, A.add, A.add, "cf1 lane", "lc1")
-    ts(lc[:, 8:9], lb[:, 1:2], -1.0, 31.0, A.mult, A.add, "lane", "lc2")
-    ts(cu[:, O_G:O_G + 6], cf[:, O_U + 16:O_U + 22], 2.0, lb[:, 1:2], A.mult, A.add, "cf1 lane", "cuG")
-    ts(lb[:, 2:4], T.kpV[:, 1:3], lb[:, 0:1], 7.5, A.mult, A.is_gt, "kpV lane", "laneq")
-    ts(lb[:, 4:5], lb[:, 0:1], 2.0, None, A.mult, None, "lane", "laner")
-    ts(T.mask[:], T.c16[:], lb[:, 0:1], None, A.is_equal, None, "c16 lane", "mask")
-    ts(cu[:, O_L:O_L + 2], lb[:, 2:4], -15.0, lb[:, 4:5], A.mult, A.add, "laneq laner", "cuL")
-    cp(cu[:, 0:O_U], cf[:, 0:O_U], "cf2 cf3 cf4 cf5", "cu")
-    act(T.keep[:], T.mask[:], F.Identity, "mask", "keep", scale=-1.0, bias=1.0)
-    act(T.mbig[:], T.mask[:], F.Copy, "mask", "mbig", scale=256.0)
+    ms(T.Arow[:, 0:PAD], 0.0, "Arx")
+    ts(lc[:, 0:6], cf[:, 16:22], lb[:, 0:1], 0.5, A.add, A.add, "cf1 lane", "lc0")
+    ts(lc[:, 6:7], lb[:, 0:1], 31.0, None, A.add, None, "lane", "lc1")
+    ts(lc[:, 7:8], lb[:, 0:1], 47.0, 54.0, A.add, A.min, "lane", "lc2")
+    ts(T.vT[:, :, 32], T.eone[:, 0:2], 30.0, lb[:, 1:2], A.add, A.subtract, "eone lane", "vTx")
+    const(T.D0[:, 0::2], 8, -B, "D0x")
+    const(T.E0[:, 0::2], 8, -B, "E0x")
+    const(T.LL[:, 16:48], 32, -B, "LLx")
+    const(T.LU[:, 16:48], 32, B, "LUx")
+    const(T.LN[:, 16:48], 32, 0.0, "LNx")
+    const(T.TT[:, 96:97], 1, -95.5 * H, "TTx")
+    const(T.kpN[:, 0:4], 4, 1.0, "kpN0")
+    const(T.kpN[:, 4:5], 1, 2.0, "kpN1")
+    const(T.kpN[:, 5:24], 19, 1.0, "kpN2")
+    for i in range(3):
+        const(T.horn[:, i::3], 24, 2.0 if i else 0.0, "horn%d" % i)
     qmx("qu", "su", 0, 128, T.uin[:], "uin", "qu")
-    uoff = cu[:, O_U:O_U + 24]
-    cp(T.qu2[:].bitcast(dt.uint32), T.qu[:].bitcast(dt.uint32).indirect(uoff), "qu cuU", "qu2")
-    act(T.su2[:], T.su[:].indirect(uoff), F.Copy, "qu cuU", "su2")
-
-    def first_half(t, src, Rd):
-        qx, sx = "qx%d" % t, "sx%d" % t
-        qmx(qx, sx, 0, HC, src[:, 0:4 * HC], Rd, qx + "a")
-        if t < R:
-            mm(3, "qu", "su", 0, qx, sx, "qu %sa" % qx, 0, HC)
-        else:
-            mm(3, "qv", "sv", 0, qx, sx, "qv %sa" % qx, 0, HC)
-            dma("Y", T.oc[:, 0:4 * HC], T[qx][:, 0:HC].bitcast(dt.uint8), qx + "a", "")
-
-    def w3(i, h):
-        return T.W3[:, 8 * i + 4 * h:8 * i + 4 * h + 4]
-
-    def sort3(h):
-        a, b, c = (St[:, 12 * h + 4 * i:12 * h + 4 * i + 4, 0] for i in range(3))
-        k, s = "S" + "ab"[h], str(h)
-        tt(w3(0, h), a, b, A.max, k, "mx" + s)
-        tt(w3(1, h), a, b, A.min, k, "mn" + s)
-        tt(w3(2, h), w3(0, h), c, A.min, k + " mx" + s, "tq" + s)
-        tt(w3(3, h), w3(0, h), c, A.max, k + " mx" + s, "hi" + s)
-        tt(PV[:, 4 * h:4 * h + 4], w3(1, h), w3(2, h), A.max, "mn%s tq%s" % (s, s), "PV" + s)
-
-    def spass(c):
-        bank = "p4" if c % 2 else "p0"
-        act(JS[:, C * c:C * c + C], T[bank][:, 0:C], F.Sign, bank + " PV%d" % (c // 4), "JS%d cS%d" % (c, c),
-            bias=PV[:, c:c + 1], scale=-1.0, accum_out=T.cS[:, c:c + 1])
-
-    def vpass(c):
-        m = c // 2
-        ts(FL[:, C * m:C * m + C], T.p1[:, 0:C], PV[:, c:c + 1], None, A.is_gt, None, "p1 PV%d" % (c // 4), "FL%d" % m)
-
-    def vsum(c):
-        m = c // 2
-        scan(SC[:, 192 * m:192 * m + 192], FL[:, C * m:C * m + 192], FL[:, C * m + 192:C * m + C], 0.0, A.add, A.add, "FL%d" % m, "SC%d" % m)
-
-    def second(h):
-        tt(w3(6, h), w3(3, h), w3(5, h), A.add, "hi%d q%da q%db" % (h, h, h), "tm%d" % h)
-        tt(PV[:, 8 + 4 * h:12 + 4 * h], w3(6, h), w3(4, h), A.max, "tm%d lo" % h, "PV%d" % (2 + h))
-
-    def halves(t, bs):
-        for b in bs:
-            out = T.Xh[:, C * b:C * b + C] if b < 3 else T.IB[:, 1::2]
-            if t == 0:
-                act(out, T.xin[:, b::4], F.Copy, "xa xb", "Xh%d" % b, scale=0.5)
-            else:
-                act(out, T.Y[:, C * b:C * b + C], F.Copy, "Y%d Y%d" % (b, b + 4), "Xh%d" % b, scale=2.0 ** -6)
-
-    def unpack(t, bs):
-        for b in bs:
-            mm(4 + b, "qe", "se", 128 * b, "lq%d" % t, "ls%d" % t, "qe%d lq%d" % (b, t))
-
-    def halve_d(bs):
-        for b in bs:
-            act(T.Dsb[:, C * b:C * b + C], T["p%d" % (4 + b)][:, 0:C], F.Copy, "p%d" % (4 + b), "Dsb%d" % b, scale=0.5)
-
-    first_half(0, T.xin, "xa")
-    tr(St[:, 0:12, :], T.p3[:, 0:HC], "p3", "Sa")
-    qmx("qx0", "sx0", HC, C, T.xin[:, 4 * HC:4 * C], "xb", "qx0b")
+    for n, a, b in (("2", 0, 16), ("3", 16, 24)):
+        cp(T["qu" + n][:].bitcast(dt.uint32), T.qu[:].bitcast(dt.uint32).indirect(cu[:, a:b]), "qu cuU", "qu" + n)
+        act(T["su" + n][:], T.su[:].indirect(cu[:, a:b]), F.Copy, "qu cuU", "su" + n)
+        if n == "2":
+            qmx("qx0", "sx0", 0, HC, T.xin[:, 0:4 * HC], "xa", "qx0a")
+            mm(3, "qu", "su", 0, "qx0", "sx0", "qu qx0a", 0, HC)
+            qmx("qx0", "sx0", HC, C, T.xin[:, 4 * HC:4 * C], "xb", "qx0b")
     dma("Y", T.qw[:].bitcast(dt.uint8), T.wc[:], "xa xb", "qw")
     dma("Y", T.sw[:], T.ws[:], "", "sw")
     dma("Y", T.vin[:], T.v[:], "", "vin")
+    tr(St[:, 0:12, :], T.p3[:, 0:HC], "p3", "Sa")
+
+    def abc(h):
+        return [St[:, 12 * h + 4 * i:12 * h + 4 * i + 4, 0] for i in range(3)]
+
+    def odd(t, h):
+        return t[:, 8 * h + 1:8 * h + 8:2]
+
+    def sort_a(h):
+        a, b, c = abc(h)
+        k, s = "S" + "ab"[h], str(h)
+        tt(odd(T.D0, h), a, b, A.max, k, "mx" + s)
+        tt(odd(T.D1, h), a, b, A.min, k, "mn" + s)
+        cp(T.D1[:, 8 * h:8 * h + 8:2], c, k, "cc" + s)
+
+    def sort_b(h):
+        s = str(h)
+        scan(MM[:, 8 * h:8 * h + 8], T.D0[:, 8 * h:8 * h + 8], T.D1[:, 8 * h:8 * h + 8], 0.0, A.min, A.max,
+             "D0x mx%s mn%s cc%s" % (s, s, s), "M" + s)
+
+    def sort_c(h):
+        c = abc(h)[2]
+        k, s = "S" + "ab"[h], str(h)
+        tt(odd(T.E0, h), odd(T.D0, h), c, A.max, k + " mx" + s, "hi" + s)
+        tt(odd(T.E1, h), odd(T.D1, h), c, A.min, k + " mn" + s, "lo" + s)
+
+    def second(h):
+        s = str(h)
+        scan(MM[:, 16 + 8 * h:24 + 8 * h], T.E0[:, 8 * h:8 * h + 8], T.E1[:, 8 * h:8 * h + 8], 0.0, A.min, A.max,
+             "E0x hi%s lo%s za%s zb%s" % (s, s, s, s), "M%d" % (2 + h))
+
+    def spass(n):
+        bank = "p4" if n % 2 else "p0"
+        act(JS[:, C * n:C * n + C], T[bank][:, 0:C], F.Sign, bank + " M%d" % (n // 4), "JS%d cS%d" % (n, n),
+            bias=MM[:, 2 * n + 1:2 * n + 2], scale=-1.0, accum_out=cS[:, n:n + 1])
+
+    def vpass(n):
+        m = n // 2 - 2
+        ts(FL[:, C * m:C * m + C], T.p1[:, 0:C], MM[:, 2 * n + 1:2 * n + 2], H, A.is_gt, A.mult, "p1 M%d" % (n // 4), "FL%d" % m)
+
+    def vsum(n):
+        m = n // 2 - 2
+        scan(T.ZB[:, n::16], FL[:, C * m:C * m + HC], FL[:, C * m + HC:C * m + C], -95.5 * H, A.add, A.add, "FL%d" % m, "z%d" % n)
+
+    def zs(out, a, Rd, W):
+        ts(out, a, 192.5, -H, A.subtract, A.mult, Rd, W)
+
+    def xh(b, lo, hi):
+        return T.Xh[:, C * b + lo:C * b + hi] if b < 2 else T["IB%d" % b][:, 2 * lo + 1:2 * hi:2]
+
+    def halves(t, bs):
+        for b in bs:
+            if t == 0:
+                act(xh(b, 0, C), T.xin[:, b::4], F.Copy, "xa xb", "Xh%d" % b, scale=0.5)
+            else:
+                act(xh(b, 0, C), T.Y[:, C * b:C * b + C], F.Copy, "Y%d Y%d" % (b, b + 4), "Xh%d" % b, scale=2.0 ** -6)
+
+    sort_a(0)
+    qmx("qe", "se", 0, 128, T.ebf[:, 3:515], "ebf", "qe0")
+    sort_b(0)
+    sort_c(0)
 
     for t in range(R):
         qx, sx, lq, ls, sa, la, sb, lbn = ("%s%d" % (s, t) for s in ("qx", "sx", "lq", "ls", "sa", "la", "sb", "lb"))
         SA, LA, SB, LB = T[sa], T[la], T[sb], T[lbn]
         qk = "%sa %sb" % (qx, qx)
-        u2 = "qu2 su2 " + qk
+        mm(0, "qu2", "su2", 0, qx, sx, "qu2 su2 " + qk)
         mm(7, "qu", "su", 0, qx, sx, "qu " + qk, HC, C)
-        mm(0, "qu2", "su2", 0, qx, sx, u2)
-        mm(1, "qu2", "su2", 128, qx, sx, u2)
-        mm(4, "qu2", "su2", 128, qx, sx, u2)
-        mm(2, "qu2", "su2", 256, qx, sx, u2)
-        mm(3, "qu2", "su2", 256, qx, sx, u2)
+        mm(4, "qu2", "su2", 128, qx, sx, "qu2 su2 " + qk)
+        mm(1, "qu2", "su2", 128, qx, sx, "qu2 su2 " + qk)
+        mm(2, "qu3", "su3", 0, qx, sx, "qu3 su3 " + qk)
+        mm(3, "qu3", "su3", 0, qx, sx, "qu3 su3 " + qk)
         send(t, T[lq][:].bitcast(dt.uint8), T[qx][:].bitcast(dt.uint8), "aq%d" % t, qk)
         send(t, T[ls][:], T[sx][:], "aq%d" % t, qk)
-        sort3(0)
-        for c in (0, 2, 1, 3):
-            spass(c)
+        if t == 0:
+            iota(T.ptab[:], [[1, C]], 0, "ptab")
+        for n in (0, 2, 1, 3):
+            spass(n)
         tr(St[:, 12:24, :], T.p7[:, 0:HC], "p7", "Sb")
-        sort3(1)
+        if t == 0:
+            qmx("qe", "se", 128, 256, T.ebf[:, 2:514], "ebf", "qe1")
+        sort_a(1)
+        ts(T.sg[:], St[:, :, 1:4], 0.0, None, A.is_gt, None, "Sa Sb", "sg")
+        sort_b(1)
+        sort_c(1)
         spass(4)
         spass(6)
         vpass(5)
-        tt(T.W3[:, 32:40], T.W3[:, 8:16], T.W3[:, 16:24], A.min, "mn0 mn1 tq0 tq1", "lo")
         vpass(7)
         vsum(5)
-        ts(T.sg[:], St[:, :, 1:4], 0.0, None, A.is_gt, None, "Sa Sb", "sg")
+        zs(T.E1[:, 0:8:2], cS[:, 0:4], ks("cS", 4), "za0 zb0")
         vsum(7)
-        ts(w3(5, 0), T.cS[:, 0:4], 192.5, -BIG, A.is_gt, A.mult, ks("cS", 4), "q0a q0b")
-        ts(T.W3[:, 45:48:2], SC[:, 575:768:192], 95.5, -BIG, A.is_lt, A.mult, "SC2 SC3", "q1b")
+        zs(ZW(1, 4, 2), cS[:, 1:4:2], "cS1 cS3", "z1 z3")
         second(0)
+        scan(T.aH[:], T.horn[:], T.sg[:], 0.0, A.mult, A.add, ks("horn", 3) + "sg", "aH")
+        cp(T.E1[:, 10:16:4], ZW(5, 8, 2), "z5 z7", "zb1")
         spass(8)
         spass(10)
         vpass(9)
-        ts(T.W3[:, 44:48:2], T.cS[:, 4:8:2], 192.5, -BIG, A.is_gt, A.mult, "cS4 cS6", "q1a")
-        vsum(9)
+        zs(T.E1[:, 8:16:4], cS[:, 4:8:2], "cS4 cS6", "za1")
+        vpass(11)
         second(1)
-        spass(15)
         spass(12)
         spass(14)
-        vpass(11)
-        scan(T.aH[:, 0:72], T.horn[:], T.sg[:], 0.0, A.mult, A.add, "horn sg", "aH")
-        vpass(13)
+        vsum(9)
         vsum(11)
+        vpass(13)
+        vpass(15)
         vsum(13)
-        act(T.AX[:], T.aH[:].indirect(cu[:, O_A:O_A + 24]), F.Copy, "aH aHx cu", "AX")
+        zs(ZW(0, 16, 2), cS[:, 0::2], ks("cS", 0, 16, 2), ks("z", 0, 16, 2))
+        vsum(15)
+        if t == 0:
+            cp(cu[:, 24:48], cf[:, 24:48], "cf2", "cuA")
+        act(T.AX[:], T.aH[:].indirect(cu[:, 24:48]), F.Identity, "aH cuA", "AX", bias=1.0)
         halves(t, (0, 1))
-        ts(T.pen[:, 8:16], T.cS[:, 1::2], 192.5, -BIG, A.is_gt, A.mult, "cS1 cS3 cS15", "penb")
-        ts(T.pen[:, 10:15], SC[:, 575:1344:192], 95.5, -BIG, A.is_lt, A.mult, ks("SC", 2, 7), "penb")
-        ts(T.pen[:, 24:32], T.pen[:, 8:16], BIG, None, A.add, None, "penb", "pend")
-        ts(T.pen[:, 0:8], T.cS[:, 0::2], 192.5, -BIG, A.is_gt, A.mult, ks("cS", 0, 16, 2), "pena")
-        ts(T.pen[:, 16:24], T.cS[:, 0::2], 192.5, BIG, A.is_lt, A.mult, ks("cS", 0, 16, 2), "penc")
-        scan(T.Rr[:, 32:48], T.kpB[:], T.pen[:, 0:16], 0.0, A.mult, A.add, "kpB pena penb", "Rc")
-        tt(T.LH[:], PV[:].indirect(cu[:, O_L:O_L + 2]), T.pen[:], A.add, ks("PV", 4) + "cuL pena penb penc pend", "LH")
-        scan(T.Rr[:, 0:16], T.rstA[:], T.LH[:, 0:16], 0.0, A.min, A.max, "rstA LH", "Ra")
-        scan(T.Rr[:, 16:32], T.rstC[:], T.LH[:, 16:32], 0.0, A.max, A.min, "rstC LH", "Rb")
-        cp(T.EXT[:], T.Rr[:].indirect(cu[:, O_T:O_T + 6]), "Ra Rb Rc cu", "EXT")
-        tr(T.TT[:], T.EXT[:], "EXT", "TT")
-        if t > 0:
-            unpack(t, (1, 2, 3, 0))
-        red(T.tv[:, 0:1], T.TT[:, 64:96], A.add, "TT", "tv0")
-        red(T.tv[:, 3:4], T.TT[:, 0:32], A.max, "TT", "tv3")
-        ts(T.tv[:, 1:2], T.tv[:, 0:1], -95.5 * BIG, -4 * BIG, A.is_gt, A.mult, "tv0", "tv1")
-        red(T.tv[:, 4:5], T.TT[:, 32:64], A.min, "TT", "tv4")
-        ts(T.tv[:, 2:3], T.tv[:, 1:2], T.tv[:, 4:5], T.tv[:, 3:4], A.add, A.max, "tv1 tv3 tv4", "tv2")
-        act(T.sgn[:], T.p3[:, 0:C], F.Sign, "p3 tv2", "sgn", bias=T.tv[:, 2:3], scale=-1.0)
-        ts(T.gt[:, 0:C], T.p2[:, 0:C], T.tv[:, 2:3], None, A.is_gt, None, "p2 tv2", "gt")
+        for b in (1, 2, 3, 0) if t else ():
+            mm(4 + b, "qe", "se", 128 * b, lq, ls, "qe%d %s" % (b, lq))
+        zk = ks("z", 16)
+        tt(T.LL[:, 0:16], MM[:, 1::2], ZW(0, 16), A.min, ks("M", 4) + zk, "LL")
+        tt(T.LU[:, 0:16], MM[:, 1::2], ZW(0, 16), A.max, ks("M", 4) + zk, "LU")
+        ts(T.LN[:, 0:16], ZW(0, 16), 0.0, H, A.is_lt, A.mult, zk, "LN")
+        for e in range(2):
+            scan(T.RR[:, e, :], T.LL[:, e::2], T.LL[:, e::2], -B, A.max, A.max, "LL LLx", "RR%d" % e)
+        for e in range(2):
+            scan(T.RR[:, 2 + e, :], T.LU[:, e::2], T.LU[:, e::2], B, A.min, A.min, "LU LUx", "RR%d" % (2 + e))
+        for e in range(2):
+            scan(T.RR[:, 4 + e, :], T.kpN[:], T.LN[:, e::2], 0.0, A.mult, A.add, "LN LNx " + ks("kpN", 3), "RR%d" % (4 + e))
         if t == 0:
-            ms(T.po[:], 0, "poa pob poc")
+            qmx("qe", "se", 256, 384, T.ebf[:, 1:513], "ebf", "qe2")
+        tr(T.TT[:, 0:96], T.RR[:, :, 8:24], ks("RR", 6), "TT")
+        if t == 0:
+            qmx("qe", "se", 384, 512, T.ebf[:, 0:512], "ebf", "qe3")
+            for b in (1, 2, 3, 0):
+                mm(4 + b, "qe", "se", 128 * b, lq, ls, "qe%d %s" % (b, lq))
+        red(T.tz[:, 0:1], T.TT[:, 64:97], A.add, "TT TTx", "tz")
+        if t == 0:
+            ts(T.mask[:], T.c16[:], lb[:, 0:1], None, A.is_equal, None, "c16 lane", "mask")
+        else:
+            tr(T.Arow[:, PAD:PAD + C], T.AX[:], "AX", "Arow")
+        scan(T.TS[:], T.TT[:, 0:32], T.TT[:, 32:64], T.tz[:, 0:1], A.max, A.min, "TT tz", "TS")
+        cut = T.TS[:, 31:32]
+        for h in range(2):
+            act(T.sgn[:, HC * h:HC * h + HC], T.p3[:, HC * h:HC * h + HC], F.Sign, "p3 TS", "sgn%d" % h, bias=cut, scale=-1.0)
+        for h in range(2):
+            act(T.ge[:, HC * h:HC * h + HC], T.sgn[:, HC * h:HC * h + HC], F.Sign, "sgn%d" % h, "ge%d" % h, bias=1.0, scale=-1.0)
+        ts(T.gt[:, 0:C], T.p2[:, 0:C], cut, None, A.is_gt, None, "p2 TS", "gt")
+        if t == 0:
+            tr(T.Arow[:, PAD:PAD + C], T.AX[:], "AX", "Arow")
         scan(T.cap[:, ::-1], T.eone[:, 0:C], T.gt[:, C:0:-1], 96.0, A.mult, A.subtract, "eone gt gtx", "cap")
-        ts(T.ge[:], T.sgn[:], 0.5, None, A.is_lt, None, "sgn", "ge")
-        scan(T.cnt[:], T.ge[:], T.cap[:], 0.0, A.add, A.min, "ge cap", "cnt")
-        if t > 0:
-            halve_d((1,))
-        else:
-            halves(t, (2,))
-        for s in range(3):
-            act(JS[:, C * s:C * s + 336], T.cnt[:, 0:336], F.Sign, "cnt lc0", "JS%d cP%d" % (s, s),
+        if t == 0:
+            ts(T.m8[:], T.mask[:, 0:K], 8.0, None, A.mult, None, "mask", "m8")
+            ts(T.kp16[:], T.c16[:, 0:K], 0.0, None, A.is_gt, None, "c16", "kp16")
+        scan(T.cnt[:], T.ge[:], T.cap[:], 0.0, A.add, A.min, "ge0 ge1 cap", "cnt")
+        for s in range(2):
+            act(JS[:, C * s:C * s + 320], T.cnt[:, 0:320], F.Sign, "cnt lc0", "JS%d cP%d" % (s, s),
                 bias=lc[:, s:s + 1], scale=-1.0, accum_out=T.cP[:, s:s + 1])
-        for s in range(3):
-            ts(FL[:, C * s:C * s + 336], T.cnt[:, 48:C], lc[:, 3 + s:4 + s], None, A.is_le, None, "cnt lc0", "FL%d" % s)
-        for s in range(3):
+        for s in range(2, 6):
+            ts(FL[:, C * s:C * s + WIN], T.cnt[:, 16 * s:16 * s + WIN], lc[:, s:s + 1], None, A.is_le, None, "cnt lc0", "FL%d" % s)
+        W2 = WIN // 2
+        for s in range(2, 6):
             o = C * s
-            scan(SC[:, 192 * s:192 * s + 168], FL[:, o:o + 168], FL[:, o + 168:o + 336], -168.0, A.add, A.add, "FL%d" % s, "SC%d" % s)
-        tr(T.Arow[:], T.AX[:], "AX", "Arow")
-        ts(T.po[:, 3:6], SC[:, 167:576:192], 216.0, None, A.add, None, ks("SC", 3), "pob")
-        ts(T.po[:, 6:7], T.cP[:, 0:1], 0.5, 168.0, A.mult, A.add, "cP0", "poc")
-        ts(T.po[:, 0:3], T.cP[:, 0:3], 0.5, 168.0, A.mult, A.add, ks("cP", 3), "poa")
-        if t > 0:
-            halve_d((2, 3, 0))
-            halves(t, (2, 3))
+            scan(T.SC[:, W2 * (s - 2):W2 * (s - 1)], FL[:, o:o + W2], FL[:, o + W2:o + WIN], 16.0 * s - 200.0, A.add, A.add, "FL%d" % s, "SC%d" % s)
+        ts(SA[:, 12:14], T.cP[:], 0.5, 160.0 + PAD, A.mult, A.add, "cP0 cP1", "poa%d" % t)
+        ts(SA[:, 14:18], T.SC[:, W2 - 1::W2], 200.0 + PAD, None, A.add, None, ks("SC", 2, 6), "pob%d" % t)
+        po, pk = SA[:, 12:18], " poa%d pob%d" % (t, t)
+        Hp = T.Hpos[:, (PAD + C) * t:(PAD + C) * (t + 1)]
+        if t == 0:
+            act(T.mbig[:], T.mask[:, 0:C], F.Copy, "mask", "mbig", scale=256.0)
+        act(T.G8[:, 0:K], T.Arow[:].indirect(po), F.Copy, "Arow Arx" + pk, "G8", scale=8.0)
+        cp(T.G[:], T.Arow[:].indirect(po), "Arow Arx" + pk, "G")
+        act(T.G8[:, K:K + 1], T.G8[:, 0:1], F.Copy, "G8", "G8x")
+        if t == 0:
+            ms(Hp, 0.0, "Hpos0")
+            act(T.keep[:], T.mask[:], F.Identity, "mask", "keep", scale=-1.0, bias=1.0)
         else:
-            halves(t, (3,))
-            act(T.Y[:, 0:3 * C], T.Xh[:], F.Copy, ks("Xh", 3), ks("Y", 3) + ks("Y", 4, 7), scale=64.0)
-        ts(T.g8[:], T.Arow[:].indirect(T.po[:, 0:7]), 8.0, 1.0, A.mult, A.add, "Arow poa pob poc", "g8")
-        tt(T.hrow[:], T.Arow[:].indirect(T.po[:, 0:6]), T.g8[:, 1:97], A.add, "Arow g8 poa pob", "hrow")
-        ts(SA[:, 0:6], T.po[:, 0:6], -192.0, None, A.add, None, "poa pob", "saa%d" % t)
-        scan(T.hm[:], T.hrow[:], T.mask[:, 0:K], 0.0, A.max, A.mult, "hrow mask", "hm")
-        scan(T.hw[:], T.keep[:, 0:K], T.hm[:], 0.0, A.mult, A.add, "hm keep", "hw")
-        cp(SA[:, 6:12], T.hw[:, 15::16], "hw", "sad%d" % t)
-        send(t, LA[:], SA[:], "aa%d" % t, "saa%d sad%d" % (t, t))
+            scan(T.CH[:], T.mbig[:], T.cnt[:], 0.0, A.add, A.min, "mbig cnt", "CH")
+        scan(T.S1[:, ::-1], T.m8[:, ::-1], T.G[:, ::-1], T.G[:, 0:1], A.mult, A.add, "m8 G", "S1")
         if t == 0:
-            for b in range(4):
-                qmx("qe", "se", 128 * b, 128 * b + 128, T.ebf[:, 3 - b:515 - b], "ebf", "qe%d" % b)
-            unpack(t, range(4))
-            halve_d(range(4))
-        H = T.Hpos[:, C * t:C * t + C]
-        cp(H.indirect(T.po[:, 0:6]), T.hrow[:], "hrow poa pob", "Hpos%d" % t)
-        scan(T.CH[:], T.mbig[:], T.cnt[:], 0.0, A.add, A.min, "mbig cnt", "CH")
-        scan(T.Hm[:], H, T.mask[:], 0.0, A.max, A.mult, "Hpos%d mask" % t, "Hm")
-        cp(SB[:], T.CH[:, 15::16], "CH", sb)
+            scan(T.CH[:], T.mbig[:], T.cnt[:], 0.0, A.add, A.min, "mbig cnt", "CH")
+        else:
+            cp(SB[:], T.CH[:, 15::16], "CH", sb)
+        tt(T.hrow[:], T.G[:], T.G8[:, 1:K + 1], A.add, "G G8 G8x", "hrow")
+        scan(T.S2[:], T.kp16[:], T.S1[:], 0.0, A.mult, A.max, "kp16 S1", "S2")
+        if t == 0:
+            cp(SB[:], T.CH[:, 15::16], "CH", sb)
+        cp(SA[:, 0:6], T.S2[:, 15::16], "S2", "sad%d" % t)
+        cp(SA[:, 6:12], T.S2[:, 15::16], "S2", "sae%d" % t)
+        send(t, LA[:, 0:18], SA[:], "aa%d" % t, "sad%d sae%d" % (t, t) + pk)
         send(t, LB[:, 0:24], SB[:], "ab%d" % t, sb)
-        scan(T.T2[:, 0:C], T.keep[:], T.Hm[:], 0.0, A.mult, A.add, "Hm keep", "T2a")
-        ms(LB[:, 24:64], 0.0, "lbx%d" % t)
-        scan(T.T2[:, C:2 * C], T.keep[:], T.Hm[:], T.T2[:, C - 1:C], A.mult, A.add, "Hm keep T2a", "T2b")
-        if t == 0:
-            ms(T.vt[:, 24:32], 0.0, "vtx")
+        for b in (1, 2, 3, 0):
+            act(T.Dsb[:, C * b:C * b + C], T["p%d" % (4 + b)][:, 0:C], F.Copy, "p%d" % (4 + b), "Dsb%d" % b, scale=0.5)
+        cp(Hp.indirect(po), T.hrow[:], "hrow" + pk, "Hpos%d" % t)
         if t == R - 1:
             qmx("qv", "sv", 0, 128, T.vin[:], "vin", "qv")
+        else:
+            ms(T.Hpos[:, (PAD + C) * (t + 1):(PAD + C) * (t + 2)], 0.0, "Hpos%d" % (t + 1))
+        o = (PAD + C) * t + PAD
+        scan(T.Hm[:, 0:C], T.Hpos[:, o:o + C], T.mask[:, 0:C], 0.0, A.max, A.mult, "Hpos%d mask" % t, "Hm")
+        scan(T.Hm[:, C:400], T.Hpos[:, o:o + 16], T.mask[:, 0:16], 0.0, A.max, A.mult, "Hpos%d mask" % t, "Hmx")
+        if t == 0:
             ms(T.PR[:, 0:16], 0.0, "PRx")
-        else:
-            ms(T["sa%d" % (t + 1)][:, 8:16], 0.0, "sad%d" % (t + 1))
-        if t == 1:
-            ms(T.Hpos[:, 2 * C:3 * C], 0.0, "Hpos2")
-        cp(T.EX[:], LA[:].indirect(cu[:, O_H:O_H + 12]), la + " cu", "EX")
-        for j in (3, 2, 1, 0):
-            ts(T.off4[:, 6 * j:6 * j + 6], LA[:, 0:6], float(240 - 16 * j), None, A.add, None, la, "off%d" % j)
-            if j == 3:
-                tr(T.TX[:], T.EX[:], "EX", "TX")
-            if j == 2:
-                cp(T.hr4[:, 0:K], T.TX[:].indirect(cu[:, O_G:O_G + 6]), "TX cuG", "hra")
-        if t > 0:
-            act(T.hr4[:, K:2 * K], T.hr4[:, 0:K], F.Copy, "hra", "hrb")
-        else:
-            cp(T.hr4[:, K:2 * K], T.hr4[:, 0:K], "hra", "hrb")
-        cp(T.hr4[:, 2 * K:3 * K], T.hr4[:, 0:K], "hra", "hrc")
-        cp(T.hr4[:, 3 * K:4 * K], T.hr4[:, 0:K], "hra", "hrd")
-
-        def compact():
+        scan(T.T2[:, 782:399:-1], T.keep[:, 383:0:-1], T.Hm[:, 383:0:-1], 0.0, A.mult, A.add, "Hm keep", "T2b")
+        scan(T.T2[:, 0:400], T.keep[:], T.Hm[:], 0.0, A.mult, A.add, "Hm Hmx keep", "T2a")
+        cp(T.hr4[:, 0:2 * K], T.htab[:].indirect(LA[:, 0:12]), la + " htab", "hra")
+        act(T.hr4[:, 2 * K:4 * K], T.htab[:].indirect(LA[:, 0:12]), F.Copy, la + " htab", "hrb")
+        for j in (1, 2, 3):
+            ts(LA[:, 12 + 6 * j:18 + 6 * j], LA[:, 12:18], -16.0 * j, None, A.add, None, la, "off%d" % j)
+        if t == 0:
             for b in range(4):
-                act(T.Dc[:, 128 * b + 16:128 * b + 112], T.Dsb[:, C * b:C * b + C].indirect(T.off4[:, 18:24]), F.Copy,
-                    "Dsb%d off3" % b, "Dc%d" % b)
-            act(T.Dc[:, 15::128], T.Dc[:, 111::128], F.Copy, ks("Dc", 4), "Dcx")
-
-        if t > 0:
-            compact()
-        else:
-            act(T.Dc[:], T.eone[:, 0:512], F.Copy, "eone", ks("Dc", 4) + "Dcx", scale=0.0)
-        act(LB[:, 24:48], LB[:, 0:24], F.Copy, lbn, "lbx%d" % t)
+                const(T.Dc[:, 128 * b:128 * b + 16], 16, 0.0, "Dcx")
+        for b in range(4):
+            act(T.Dc[:, 128 * b + 16:128 * b + 112], T.Dsb[:, C * b:C * b + C].indirect(LA[:, 30:36]), F.Copy,
+                "Dsb%d off3" % b, "Dc%d" % b)
         for i in range(6):
-            tt(T.E[:, C * i:C * i + C], T.T2[:, 336 - 64 * i:2 * C].indirect(T.off4[:]), T.hr4[:], A.is_equal,
-               "T2a T2b hra hrb hrc hrd " + ks("off", 4), "E%d" % i)
+            tt(T.E[:, C * i:C * i + C], T.T2[:, 336 - 64 * i:2 * C].indirect(LA[:, 12:36]), T.hr4[:], A.is_equal,
+               "T2a T2b hra hrb off1 off2 off3 " + la, "E%d" % i)
             for bn in range(4 * i, 4 * i + 4):
                 if bn < 22:
                     act(T.JE[:, K * bn:K * bn + K], T.E[:, K * bn:K * bn + K], F.Identity, "E%d" % i, "JE%d vt%d" % (bn, bn),
                         accum_out=T.vt[:, bn:bn + 1])
                 else:
                     red(T.vt[:, bn:bn + 1], T.E[:, K * bn:K * bn + K], A.add, "E5", "vt%d" % bn)
-        if t == 0:
-            compact()
+            if i == 1:
+                act(T.Dc[:, 15::128], T.Dc[:, 111::128], F.Copy, ks("Dc", 4), "Dcx")
+            if i == 2:
+                act(LB[:, 24:48], LB[:, 0:24], F.Copy, lbn, "lbx%d" % t)
+        halves(t, (2, 3))
         if t == R - 1:
-            act(T.PX[:], LA[:].indirect(cu[:, O_P:O_P + 12]), F.Copy, la + " cu", "PX")
-        tr(T.vT[:], T.vt[:], ks("vt", 24) + "vtx", "vT")
-        scan(T.vs[:], T.kpV[:], T.vT[:], 0.0, A.mult, A.add, "kpV vT", "vs")
-        ts(T.vx[:], T.vs[:].indirect(cu[:, O_V:O_V + 2]), 64.0, lc[:, 8:9], A.mult, A.add, "vs cu lc2", "vx")
+            act(T.PR[:, 16:112], T.ptab[:].indirect(LA[:, 30:36]), F.Copy, "ptab off3", "PR")
+            act(T.PR[:, 15:16], T.PR[:, 111:112], F.Copy, "PR", "PRx")
+        tr(T.vT[:, :, 0:16], T.vt[:], ks("vt", 24) + "vtx", "vT")
         if t == 0:
             ms(T.alt[:], 1.0, "alt")
-        tr(T.vy[:], T.vx[:], "vx", "vy")
-        if t == R - 1:
-            tr(T.TP[:], T.PX[:], "PX", "TP")
-            act(T.PR[:, 16:112], T.TP[:].indirect(cu[:, O_G:O_G + 6]), F.Copy, "TP cuG", "PR")
-            act(T.PR[:, 15:16], T.PR[:, 111:112], F.Copy, "PR", "PRx")
-        red(T.mv[:, 0:1], T.vy[:], A.max, "vy", "mv0")
+        for e in range(2):
+            scan(T.vS[:, e, :], T.kpF[:], T.vT[:, e, :], 0.0, A.mult, A.add, "kpF vT vTx", "vS%d" % e)
         if t == 0:
             ms(T.alt[:, 0::2], 0.0, "alt")
-        ts(T.mv[:, 1:2], T.mv[:, 0:1], MAGIC, MAGIC, A.add, A.subtract, "mv0", "mv1")
-        ts(T.rot[:], lc[:, 6:8], T.mv[:, 0:1], T.mv[:, 1:2], A.subtract, A.add, "lc1 mv0 mv1", "rot")
+        for e in range(2):
+            tr(T.vy[:, 32 * e:32 * e + 32], T.vS[:, :, 16 + 16 * e:32 + 16 * e], "vS0 vS1", "vy%d" % e)
+        for e in range(2):
+            red(T.mv[:, e:e + 1], T.vy[:, 32 * e:32 * e + 32], A.max, "vy%d" % e, "mv%d" % e)
+        ts(T.rot[:], lc[:, 6:8], T.mv[:, 1:2], T.mv[:, 0:1], A.subtract, A.add, "lc1 lc2 mv0 mv1", "rot")
         ts(T.moff[:], LB[:].indirect(T.rot[:]), 15.0, None, A.add, None, lbn + " rot lbx%d" % t, "moff")
-        mo = T.moff[:, 0:24]
-        act(T.IB[:, 0::2], T.Dc[:, 384:496].indirect(mo), F.Copy, "Dc3 Dcx moff", "IB")
-        for b in (0, 3, 1, 2):
-            if b == 3:
-                scan(T.Z[:, 1::2], T.alt[:], T.IB[:], 0.0, A.mult, A.add, "alt IB Xh3", "Z1 Z3")
-            else:
-                tt(T.Z[:, b::4], T.Dc[:, 128 * b:128 * b + 112].indirect(mo), T.Xh[:, C * b:C * b + C], A.add,
-                   "Dc%d Xh%d Dcx moff" % (b, b), "Z%d" % b)
-        if t == 0:
-            act(T.Y[:, 3 * C:4 * C], T.xin[:, 3::4], F.Copy, "xa xb", "Y3 Y7", scale=32.0)
-            act(T.Hpos[:, C:2 * C], T.eone[:, 0:C], F.Copy, "eone", "Hpos1", scale=0.0)
-        if t == R - 1:
-            act(T.OL[:], T.PR[:].indirect(mo), F.Identity, "PR PRx moff", "OL", bias=192.0)
-            dma("S", T.ol[:], T.OL[0::16, :], "OL", "")
-        for h in range(2):
-            qmx("qz", "sz", HC * h, HC * h + HC, T.Z[:, 4 * HC * h:4 * HC * (h + 1)], ks("Z", 4), "qz%d" % h)
+
+        def win(b, h):
+            return T.Dc[:, 128 * b:128 * b + 112].indirect(T.moff[:, 12 * h:12 * h + 12])
+
+        def zv(b, h):
+            return T.Z[:, 4 * HC * h + b:4 * HC * (h + 1):4]
+
+        def fused(b, h):
+            tt(zv(b, h), win(b, h), xh(b, HC * h, HC * h + HC), A.add, "Dc%d Xh%d Dcx moff" % (b, b), "Z%d" % (4 * h + b))
+
+        def fetch(b, h):
+            act(T["IB%d" % b][:, C * h:C * h + C:2], win(b, h), F.Copy, "Dc%d Dcx moff" % b, "IB%d%d" % (b, h))
+
+        def pairs(b, h):
+            scan(T.Z[:, 4 * HC * h + b - 2:4 * HC * (h + 1):2], T.alt[:], T["IB%d" % b][:, C * h:C * h + C], 0.0, A.mult, A.add,
+                 "alt IB%d%d Xh%d" % (b, h, b), "Z%d Z%d" % (4 * h + b, 4 * h + b - 2))
+
+        def product(h):
+            qmx("qz", "sz", HC * h, HC * h + HC, T.Z[:, 4 * HC * h:4 * HC * (h + 1)], ks("Z", 4 * h, 4 * h + 4), "qz%d" % h)
             for b in range(4):
                 mm(4 * h + b, "qw", "sw", 128 * b, "qz", "sz", "qw sw qz%d" % h, HC * h, HC * h + HC)
-        for i in range(8):
+
+        def state(i):
             h, b = i // 4, i % 4
             Yb = T.Y[:, C * b + HC * h:C * b + HC * h + HC]
             Xb = T.X[:, 4 * HC * h + b:4 * HC * (h + 1):4]
             tt(Yb, T["p%d" % i][:, 0:HC], Yb, A.add, "p%d Y%d" % (i, i), "Y%d" % i)
             if i < 7:
                 act(Xb, Yb, F.Copy, "Y%d" % i, "X%d" % i, scale=2.0 ** -5)
-            if i == 5:
-                first_half(t + 1, T.X, ks("X", 4))
+            return Xb, Yb
+
+        fetch(2, 0)
+        fetch(2, 1)
+        fetch(3, 1)
+        if t == 0:
+            for b in range(4):
+                act(T.Y[:, C * b:C * b + C], T.xin[:, b::4], F.Copy, "xa xb", "Y%d Y%d" % (b, b + 4), scale=32.0)
+        if t == R - 1:
+            act(T.OL[:], T.PR[:].indirect(T.moff[:, 0:24]), F.Copy, "PR PRx moff", "OL")
+            dma("S", T.ol[:], T.OL[0::16, :], "OL", "")
+        fused(1, 0)
+        fused(3, 0)
+        pairs(2, 0)
+        pairs(2, 1)
+        fused(0, 0)
+        pairs(3, 1)
+        product(0)
+        fused(0, 1)
+        fused(1, 1)
+        state(0)
+        product(1)
+        for i in range(1, 7):
+            state(i)
+        qx, sx = "qx%d" % (t + 1), "sx%d" % (t + 1)
+        qmx(qx, sx, 0, HC, T.X[:, 0:4 * HC], ks("X", 4), qx + "a")
         if t < R - 1:
-            tr(St[:, 0:12, :], T.p3[:, 0:HC], "p3", "Sa")
+            mm(3, "qu", "su", 0, qx, sx, "qu %sa" % qx, 0, HC)
         else:
+            mm(3, "qv", "sv", 0, qx, sx, "qv %sa" % qx, 0, HC)
+            dma("Y", T.oc[:, 0:4 * HC], T[qx][:, 0:HC].bitcast(dt.uint8), qx + "a", "")
             act(T.ysb[:, 0:HC], T.p3[:, 0:HC], F.Copy, "p3", "ya")
             dma("S", T.y[:, 0:HC], T.ysb[:, 0:HC], "ya", "")
+        Xb, Yb = state(7)
         ts(Xb, Yb, 2.0 ** -5, None, A.mult, None, "Y7", "X7")
-        qmx("qx%d" % (t + 1), "sx%d" % (t + 1), HC, C, T.X[:, 4 * HC:4 * C], ks("X", 4, 8), "qx%db" % (t + 1))
+        if t < R - 1:
+            tr(St[:, 0:12, :], T.p3[:, 0:HC], "p3", "Sa")
+        qmx(qx, sx, HC, C, T.X[:, 4 * HC:4 * C], ks("X", 4, 8), qx + "b")
+        if t < R - 1:
+            sort_a(0)
+            sort_b(0)
+            sort_c(0)
 
-    qx, sx = "qx%d" % R, "sx%d" % R
     mm(0, "qv", "sv", 0, qx, sx, "qv %sb" % qx, HC, C)
     dma("Y", T.oc[:, 4 * HC:4 * C], T[qx][:, HC:C].bitcast(dt.uint8), qx + "b", "")
     for k in range(4):

@@ -14,13 +14,13 @@ CODE = "float8_e4m3fn_x4"
 SCRATCH = {}
 for _d, _l in (
         ("bfloat16", dict(xin=4 * C, uin=512, vin=512, X=4 * C, Z=4 * C, Y=4 * C, Xh=2 * C, IB2=2 * C, IB3=2 * C, alt=C, Dsb=4 * C, Dc=512,
-                          eone=528, ebf=528, c16=400, mask=400, keep=400, mbig=C, m8=K, kp16=K, horn=72, sg=72, aH=72, AX=C, Arow=PAD + C,
-                          FL=6 * C, ZB=16 * HC, JS=16 * C, gt=400, sgn=C, ge=C, cap=C, cnt=C, CH=C, SC=2 * WIN, G=K, G8=112, S1=K, S2=K,
-                          hrow=K, Hpos=R * (PAD + C), Hm=400, T2=784, hr4=C, E=24 * K, JE=24 * K, htab=80)),
-        ("float32", dict(cf=64, lc=16, lb=8, D0=16, D1=16, E0=16, E1=16, MM=32, cS=16, LL=48, LU=48, LN=48, kpN=24, kpF=48, TT=112, tz=2, TS=32,
-                         cP=2, vt=32, vy=64, mv=2, OL=C, ysb=C, ptab=C, PR=112)),
-        ("uint16", dict(cu=48, rot=2, moff=32)),
-        ("int32", dict(li=4)),
+                          eone=528, ebf=528, c16=C, mask=C, keep=C, mbig=C, horn=72, sg=72, aH=72, sh=32 * R, lh=32 * R, AX=C, BX=C,
+                          Arow=PAD + C, Am=PAD + C, Brow=PAD + C, FL=7 * C, ZB=16 * HC, JS=16 * C, gt=400, sgn=C, ge=C, cap=C, cnt=C, CH=C,
+                          SC=2 * WIN, G8=112, B8=112, hv=K, Hm=R * (PAD + C), T2=784, hr4=C, E=24 * K, JE=24 * K)),
+        ("float32", dict(cf=64, lc=16, lb=8, D0=16, D1=16, E0=8, E1=8, MM=32, cS=16, LL=48, LU=48, LN=48, kpN=24, kpF=48, TT=112, tz=2, TS=32,
+                         cP=2, hp=24, SP=24, vt=32, vy=64, mv=2, OL=C, ysb=C, ptab=C, PR=112)),
+        ("uint16", dict(cu=48, rot=2, moff=32, sa=8 * R, la=32 * R, sc=16 * R, ld=16 * R)),
+        ("int32", dict(li=4, lw=64)),
         (CODE, dict(qu=128, qu2=256, qu3=128, qv=128, qw=512, qe=512, qz=C, qx0=C, qx1=C, qx2=C, qx3=C, lq0=C, lq1=C, lq2=C)),
         ("uint8", dict(su=128, su2=256, su3=128, sv=128, sw=512, se=512, sz=C, sx0=C, sx1=C, sx2=C, sx3=C, ls0=C, ls1=C, ls2=C))):
     for _n in _l:
@@ -29,13 +29,10 @@ SCRATCH["St"] = ("sbuf", [128, 24, 16], "float32")
 SCRATCH["RR"] = ("sbuf", [128, 6, 24], "float32")
 for _n in ("vT", "vS"):
     SCRATCH[_n] = ("sbuf", [128, 2, 48], "float32")
-for _t in range(R):
-    for _n, _w, _d in (("sa", 18, "uint16"), ("la", 36, "uint16"), ("sb", 24, "bfloat16"), ("lb", 48, "bfloat16")):
-        SCRATCH["%s%d" % (_n, _t)] = ("sbuf", [128, _w], _d)
 for _b in range(8):
     SCRATCH["p%d" % _b] = ("psum", [128, 512], "float32")
 
-SEMAPHORES = ["cV", "cS", "cT", "cG", "sent"] + ["d%d" % i for i in range(16)] + [a + str(t) for a in ("aq", "aa", "ab") for t in range(R)]
+SEMAPHORES = ["cV", "cS", "cT", "cG", "sent"] + ["d%d" % i for i in range(16)] + [a + str(t) for a in ("aq", "ah", "aa", "ab") for t in range(R)]
 
 
 def rank_program(g, core, T, topo):
@@ -145,7 +142,7 @@ def rank_program(g, core, T, topo):
 
     for t in range(R):
         n = len(topo.engines(T.cores[(rank + STEP[t]) % N], core))
-        for key, sem, m in (("lq", "aq", 2 * n), ("la", "aa", n), ("lb", "ab", n)):
+        for key, sem, m in (("lq", "aq", 2 * n), ("lh", "ah", n), ("la", "aa", n), ("ld", "ab", n)):
             lastw[key + str(t)] = [(sem + str(t), m)]
             count[sem + str(t)] = m
 
@@ -161,12 +158,13 @@ def rank_program(g, core, T, topo):
     op("G", lambda: g.iota(T.li[:, 0:1], [[0, 1]], 0, 1), "", "li0")
     ms(T.eone[:], 1.0, "eone")
     op("G", lambda: g.affine_select(T.ebf[:], T.eone[:], [[-1, 528]], A.is_equal, 0.0, 3, 4), "eone", "ebf")
-    iota(cf[:, 24:48], [[3, 24]], 2, "cf2")
-    iota(T.c16[:], [[0, 25], [1, 16]], 0, "c16")
-    iota(T.htab[:], [[1, 80]], 0, "htab")
+    iota(cf[:, 24:48], [[1, 24]], 0, "cf2")
+    iota(T.hp[:], [[0, 12], [128, 2]], 0, "hp")
+    iota(T.c16[:], [[0, 24], [1, 16]], 0, "c16")
 
     ms(T.gt[:, C:400], 0.0, "gtx")
     ms(T.vt[:, 24:32], 0.0, "vtx")
+    ms(T.Dc[:], 0.0, "Dcy " + ks("Dc", 4))
     ms(T.kpF[:], 1.0, "kpF")
     ms(T.vT[:, :, 16:48], 0.0, "vTx")
     cp(cu[:, 0:24], cf[:, 0:24], "cf0 cf1", "cuU")
@@ -174,13 +172,11 @@ def rank_program(g, core, T, topo):
     ts(T.li[:, 2:3], T.li[:, 0:1], 31, None, A.bitwise_and, None, "li0", "li2")
     ms(T.kpF[:, 16:17], 64.0, "kpF")
     cp(lb[:, 0:2], T.li[:, 1:3], "li1 li2", "lane")
-    ms(T.Arow[:, 0:PAD], 0.0, "Arx")
     ts(lc[:, 0:6], cf[:, 16:22], lb[:, 0:1], 0.5, A.add, A.add, "cf1 lane", "lc0")
     ts(lc[:, 6:7], lb[:, 0:1], 31.0, None, A.add, None, "lane", "lc1")
     ts(lc[:, 7:8], lb[:, 0:1], 47.0, 54.0, A.add, A.min, "lane", "lc2")
     ts(T.vT[:, :, 32], T.eone[:, 0:2], 30.0, lb[:, 1:2], A.add, A.subtract, "eone lane", "vTx")
     const(T.D0[:, 0::2], 8, -B, "D0x")
-    const(T.E0[:, 0::2], 8, -B, "E0x")
     const(T.LL[:, 16:48], 32, -B, "LLx")
     const(T.LU[:, 16:48], 32, B, "LUx")
     const(T.LN[:, 16:48], 32, 0.0, "LNx")
@@ -190,18 +186,22 @@ def rank_program(g, core, T, topo):
     const(T.kpN[:, 5:24], 19, 1.0, "kpN2")
     for i in range(3):
         const(T.horn[:, i::3], 24, 2.0 if i else 0.0, "horn%d" % i)
-    qmx("qu", "su", 0, 128, T.uin[:], "uin", "qu")
-    for n, a, b in (("2", 0, 16), ("3", 16, 24)):
+    for n in ("Arow", "Am", "Brow"):
+        const(T[n][:, 0:PAD], PAD, 0.0, n + "x")
+
+    def pick_u(n, a, b):
         cp(T["qu" + n][:].bitcast(dt.uint32), T.qu[:].bitcast(dt.uint32).indirect(cu[:, a:b]), "qu cuU", "qu" + n)
         act(T["su" + n][:], T.su[:].indirect(cu[:, a:b]), F.Copy, "qu cuU", "su" + n)
-        if n == "2":
-            qmx("qx0", "sx0", 0, HC, T.xin[:, 0:4 * HC], "xa", "qx0a")
-            mm(3, "qu", "su", 0, "qx0", "sx0", "qu qx0a", 0, HC)
-            qmx("qx0", "sx0", HC, C, T.xin[:, 4 * HC:4 * C], "xb", "qx0b")
+
+    qmx("qu", "su", 0, 128, T.uin[:], "uin", "qu")
+    qmx("qx0", "sx0", 0, HC, T.xin[:, 0:4 * HC], "xa", "qx0a")
+    mm(3, "qu", "su", 0, "qx0", "sx0", "qu qx0a", 0, HC)
+    pick_u("2", 0, 16)
+    tr(St[:, 0:12, :], T.p3[:, 0:HC], "p3", "Sa")
+    qmx("qx0", "sx0", HC, C, T.xin[:, 4 * HC:4 * C], "xb", "qx0b")
     dma("Y", T.qw[:].bitcast(dt.uint8), T.wc[:], "xa xb", "qw")
     dma("Y", T.sw[:], T.ws[:], "", "sw")
     dma("Y", T.vin[:], T.v[:], "", "vin")
-    tr(St[:, 0:12, :], T.p3[:, 0:HC], "p3", "Sa")
 
     def abc(h):
         return [St[:, 12 * h + 4 * i:12 * h + 4 * i + 4, 0] for i in range(3)]
@@ -224,29 +224,32 @@ def rank_program(g, core, T, topo):
     def sort_c(h):
         c = abc(h)[2]
         k, s = "S" + "ab"[h], str(h)
-        tt(odd(T.E0, h), odd(T.D0, h), c, A.max, k + " mx" + s, "hi" + s)
-        tt(odd(T.E1, h), odd(T.D1, h), c, A.min, k + " mn" + s, "lo" + s)
+        tt(T.E0[:, 4 * h:4 * h + 4], odd(T.D0, h), c, A.max, k + " mx" + s, "hi" + s)
+        tt(T.E1[:, 4 * h:4 * h + 4], odd(T.D1, h), c, A.min, k + " mn" + s, "lo" + s)
 
-    def second(h):
-        s = str(h)
-        scan(MM[:, 16 + 8 * h:24 + 8 * h], T.E0[:, 8 * h:8 * h + 8], T.E1[:, 8 * h:8 * h + 8], 0.0, A.min, A.max,
-             "E0x hi%s lo%s za%s zb%s" % (s, s, s, s), "M%d" % (2 + h))
+    def second(*ns):
+        for n in ns:
+            ts(MM[:, 2 * n + 17:2 * n + 18], ZW(n, n + 1), T.E0[:, n:n + 1], T.E1[:, n:n + 1], A.min, A.max,
+               "hi%d lo%d z%d" % (n // 4, n // 4, n), "M%d" % (8 + n))
+
+    def mk(n):
+        return " M%d" % (n // 4 if n < 8 else n)
 
     def spass(n):
         bank = "p4" if n % 2 else "p0"
-        act(JS[:, C * n:C * n + C], T[bank][:, 0:C], F.Sign, bank + " M%d" % (n // 4), "JS%d cS%d" % (n, n),
+        act(JS[:, C * n:C * n + C], T[bank][:, 0:C], F.Sign, bank + mk(n), "JS%d cS%d" % (n, n),
             bias=MM[:, 2 * n + 1:2 * n + 2], scale=-1.0, accum_out=cS[:, n:n + 1])
 
     def vpass(n):
-        m = n // 2 - 2
-        ts(FL[:, C * m:C * m + C], T.p1[:, 0:C], MM[:, 2 * n + 1:2 * n + 2], H, A.is_gt, A.mult, "p1 M%d" % (n // 4), "FL%d" % m)
+        m = n // 2 - 1
+        ts(FL[:, C * m:C * m + C], T.p1[:, 0:C], MM[:, 2 * n + 1:2 * n + 2], H, A.is_gt, A.mult, "p1" + mk(n), "FL%d" % m)
 
     def vsum(n):
-        m = n // 2 - 2
+        m = n // 2 - 1
         scan(T.ZB[:, n::16], FL[:, C * m:C * m + HC], FL[:, C * m + HC:C * m + C], -95.5 * H, A.add, A.add, "FL%d" % m, "z%d" % n)
 
-    def zs(out, a, Rd, W):
-        ts(out, a, 192.5, -H, A.subtract, A.mult, Rd, W)
+    def zs(*r):
+        ts(ZW(*r), cS[:, r[0]:r[1]:r[2]], 192.5, -H, A.subtract, A.mult, ks("cS", *r), ks("z", *r))
 
     def xh(b, lo, hi):
         return T.Xh[:, C * b + lo:C * b + hi] if b < 2 else T["IB%d" % b][:, 2 * lo + 1:2 * hi:2]
@@ -262,65 +265,73 @@ def rank_program(g, core, T, topo):
     qmx("qe", "se", 0, 128, T.ebf[:, 3:515], "ebf", "qe0")
     sort_b(0)
     sort_c(0)
+    pick_u("3", 16, 24)
 
     for t in range(R):
-        qx, sx, lq, ls, sa, la, sb, lbn = ("%s%d" % (s, t) for s in ("qx", "sx", "lq", "ls", "sa", "la", "sb", "lb"))
-        SA, LA, SB, LB = T[sa], T[la], T[sb], T[lbn]
+        qx, sx, lq, ls, la, lh, ld, sh = ("%s%d" % (s, t) for s in ("qx", "sx", "lq", "ls", "la", "lh", "ld", "sh"))
+        SA = lambda a, b: T.sa[:, 8 * t + a:8 * t + b]
+        LA = lambda a, b: T.la[:, 32 * t + a:32 * t + b]
+        SH, LH = T.sh[:, 32 * t:32 * t + 24], T.lh[:, 32 * t:32 * t + 24]
         qk = "%sa %sb" % (qx, qx)
         mm(0, "qu2", "su2", 0, qx, sx, "qu2 su2 " + qk)
         mm(7, "qu", "su", 0, qx, sx, "qu " + qk, HC, C)
-        mm(4, "qu2", "su2", 128, qx, sx, "qu2 su2 " + qk)
         mm(1, "qu2", "su2", 128, qx, sx, "qu2 su2 " + qk)
+        mm(4, "qu2", "su2", 128, qx, sx, "qu2 su2 " + qk)
         mm(2, "qu3", "su3", 0, qx, sx, "qu3 su3 " + qk)
         mm(3, "qu3", "su3", 0, qx, sx, "qu3 su3 " + qk)
         send(t, T[lq][:].bitcast(dt.uint8), T[qx][:].bitcast(dt.uint8), "aq%d" % t, qk)
         send(t, T[ls][:], T[sx][:], "aq%d" % t, qk)
         if t == 0:
             iota(T.ptab[:], [[1, C]], 0, "ptab")
-        for n in (0, 2, 1, 3):
+        for n in (0, 2, 1):
             spass(n)
         tr(St[:, 12:24, :], T.p7[:, 0:HC], "p7", "Sb")
-        if t == 0:
-            qmx("qe", "se", 128, 256, T.ebf[:, 2:514], "ebf", "qe1")
         sort_a(1)
-        ts(T.sg[:], St[:, :, 1:4], 0.0, None, A.is_gt, None, "Sa Sb", "sg")
+        vpass(3)
         sort_b(1)
         sort_c(1)
         spass(4)
         spass(6)
+        vsum(3)
+        ts(T.sg[:], St[:, :, 1:4], 0.0, None, A.is_gt, None, "Sa Sb", "sg")
+        zs(0, 3, 1)
         vpass(5)
-        vpass(7)
-        vsum(5)
-        zs(T.E1[:, 0:8:2], cS[:, 0:4], ks("cS", 4), "za0 zb0")
-        vsum(7)
-        zs(ZW(1, 4, 2), cS[:, 1:4:2], "cS1 cS3", "z1 z3")
-        second(0)
-        scan(T.aH[:], T.horn[:], T.sg[:], 0.0, A.mult, A.add, ks("horn", 3) + "sg", "aH")
-        cp(T.E1[:, 10:16:4], ZW(5, 8, 2), "z5 z7", "zb1")
+        second(0, 2, 1, 3)
         spass(8)
         spass(10)
+        spass(11)
+        vpass(7)
+        vsum(5)
+        zs(4, 7, 2)
         vpass(9)
-        zs(T.E1[:, 8:16:4], cS[:, 4:8:2], "cS4 cS6", "za1")
-        vpass(11)
-        second(1)
+        second(4, 6)
         spass(12)
         spass(14)
+        vsum(7)
+        second(5)
         vsum(9)
-        vsum(11)
+        scan(T.aH[:], T.horn[:], T.sg[:], 0.0, A.mult, A.add, ks("horn", 3) + "sg", "aH")
+        second(7)
         vpass(13)
         vpass(15)
+        zs(11, 12, 1)
         vsum(13)
-        zs(ZW(0, 16, 2), cS[:, 0::2], ks("cS", 0, 16, 2), ks("z", 0, 16, 2))
+        if t == 0:
+            qmx("qe", "se", 128, 256, T.ebf[:, 2:514], "ebf", "qe1")
         vsum(15)
+        zs(8, 16, 2)
         if t == 0:
             cp(cu[:, 24:48], cf[:, 24:48], "cf2", "cuA")
-        act(T.AX[:], T.aH[:].indirect(cu[:, 24:48]), F.Identity, "aH cuA", "AX", bias=1.0)
-        halves(t, (0, 1))
+        act(SH, T.aH[:, 2::3], F.Identity, "aH", sh, bias=128.0)
+        send(t, LH, SH, "ah%d" % t, sh)
+        halves(t, (0,))
+        act(T.AX[:], SH.indirect(cu[:, 24:48]), F.Copy, sh + " cuA", "AX")
+        halves(t, (1,))
         for b in (1, 2, 3, 0) if t else ():
             mm(4 + b, "qe", "se", 128 * b, lq, ls, "qe%d %s" % (b, lq))
         zk = ks("z", 16)
-        tt(T.LL[:, 0:16], MM[:, 1::2], ZW(0, 16), A.min, ks("M", 4) + zk, "LL")
-        tt(T.LU[:, 0:16], MM[:, 1::2], ZW(0, 16), A.max, ks("M", 4) + zk, "LU")
+        tt(T.LL[:, 0:16], MM[:, 1::2], ZW(0, 16), A.min, "M0 M1 " + ks("M", 8, 16) + zk, "LL")
+        tt(T.LU[:, 0:16], MM[:, 1::2], ZW(0, 16), A.max, "M0 M1 " + ks("M", 8, 16) + zk, "LU")
         ts(T.LN[:, 0:16], ZW(0, 16), 0.0, H, A.is_lt, A.mult, zk, "LN")
         for e in range(2):
             scan(T.RR[:, e, :], T.LL[:, e::2], T.LL[:, e::2], -B, A.max, A.max, "LL LLx", "RR%d" % e)
@@ -342,18 +353,21 @@ def rank_program(g, core, T, topo):
             tr(T.Arow[:, PAD:PAD + C], T.AX[:], "AX", "Arow")
         scan(T.TS[:], T.TT[:, 0:32], T.TT[:, 32:64], T.tz[:, 0:1], A.max, A.min, "TT tz", "TS")
         cut = T.TS[:, 31:32]
-        for h in range(2):
-            act(T.sgn[:, HC * h:HC * h + HC], T.p3[:, HC * h:HC * h + HC], F.Sign, "p3 TS", "sgn%d" % h, bias=cut, scale=-1.0)
-        for h in range(2):
-            act(T.ge[:, HC * h:HC * h + HC], T.sgn[:, HC * h:HC * h + HC], F.Sign, "sgn%d" % h, "ge%d" % h, bias=1.0, scale=-1.0)
+        act(T.sgn[:, 0:HC], T.p3[:, 0:HC], F.Sign, "p3 TS", "sgn", bias=cut, scale=-1.0)
+        act(T.ge[:, 0:HC], T.sgn[:, 0:HC], F.Sign, "sgn", "ge0", bias=1.0, scale=-1.0)
         ts(T.gt[:, 0:C], T.p2[:, 0:C], cut, None, A.is_gt, None, "p2 TS", "gt")
+        ts(T.ge[:, HC:C], T.p2[:, HC:C], cut, None, A.is_ge, None, "p2 TS", "ge1")
+        scan(T.cap[:, ::-1], T.eone[:, 0:C], T.gt[:, C:0:-1], 96.0, A.mult, A.subtract, "eone gt gtx", "cap")
+        masked = lambda: scan(T.Am[:, PAD:PAD + C], T.Arow[:, PAD:PAD + C], T.mask[:], 0.0, A.max, A.mult, "Arow mask", "Am")
         if t == 0:
             tr(T.Arow[:, PAD:PAD + C], T.AX[:], "AX", "Arow")
-        scan(T.cap[:, ::-1], T.eone[:, 0:C], T.gt[:, C:0:-1], 96.0, A.mult, A.subtract, "eone gt gtx", "cap")
-        if t == 0:
-            ts(T.m8[:], T.mask[:, 0:K], 8.0, None, A.mult, None, "mask", "m8")
-            ts(T.kp16[:], T.c16[:, 0:K], 0.0, None, A.is_gt, None, "c16", "kp16")
+        else:
+            masked()
         scan(T.cnt[:], T.ge[:], T.cap[:], 0.0, A.add, A.min, "ge0 ge1 cap", "cnt")
+        act(T.BX[:], LH.indirect(cu[:, 24:48]), F.Copy, lh + " cuA", "BX")
+        o = (PAD + C) * t
+        Hp, Hm = T.Hm[:, o:o + PAD + C], lambda a, b, s=1, o=o + PAD: T.Hm[:, o + a:o + b:s]
+        ms(Hp, 0.0, "Hm%d" % t)
         for s in range(2):
             act(JS[:, C * s:C * s + 320], T.cnt[:, 0:320], F.Sign, "cnt lc0", "JS%d cP%d" % (s, s),
                 bias=lc[:, s:s + 1], scale=-1.0, accum_out=T.cP[:, s:s + 1])
@@ -363,87 +377,94 @@ def rank_program(g, core, T, topo):
         for s in range(2, 6):
             o = C * s
             scan(T.SC[:, W2 * (s - 2):W2 * (s - 1)], FL[:, o:o + W2], FL[:, o + W2:o + WIN], 16.0 * s - 200.0, A.add, A.add, "FL%d" % s, "SC%d" % s)
-        ts(SA[:, 12:14], T.cP[:], 0.5, 160.0 + PAD, A.mult, A.add, "cP0 cP1", "poa%d" % t)
-        ts(SA[:, 14:18], T.SC[:, W2 - 1::W2], 200.0 + PAD, None, A.add, None, ks("SC", 2, 6), "pob%d" % t)
-        po, pk = SA[:, 12:18], " poa%d pob%d" % (t, t)
-        Hp = T.Hpos[:, (PAD + C) * t:(PAD + C) * (t + 1)]
+        ts(SA(0, 2), T.cP[:], 0.5, 160.0 + PAD, A.mult, A.add, "cP0 cP1", "poa%d" % t)
+        ts(SA(6, 7), T.cP[:, 0:1], 0.5, 160.0 + PAD, A.mult, A.add, "cP0", "poc%d" % t)
+        ts(SA(2, 6), T.SC[:, W2 - 1::W2], 200.0 + PAD, None, A.add, None, ks("SC", 2, 6), "pob%d" % t)
+        pk = " poa%d pob%d poc%d" % (t, t, t)
+        send(t, LA(18, 25), SA(0, 7), "aa%d" % t, pk)
+
+        def next_signs(out, row, off, Rd, W):
+            act(out, row.indirect(off), F.Identity, Rd, W, scale=0.125, bias=-15.0)
+
+        def half_d(b):
+            act(T.Dsb[:, C * b:C * b + C], T["p%d" % (4 + b)][:, 0:C], F.Copy, "p%d" % (4 + b), "Dsb%d" % b, scale=0.5)
+
         if t == 0:
-            act(T.mbig[:], T.mask[:, 0:C], F.Copy, "mask", "mbig", scale=256.0)
-        act(T.G8[:, 0:K], T.Arow[:].indirect(po), F.Copy, "Arow Arx" + pk, "G8", scale=8.0)
-        cp(T.G[:], T.Arow[:].indirect(po), "Arow Arx" + pk, "G")
-        act(T.G8[:, K:K + 1], T.G8[:, 0:1], F.Copy, "G8", "G8x")
-        if t == 0:
-            ms(Hp, 0.0, "Hpos0")
+            act(T.mbig[:], T.mask[:], F.Copy, "mask", "mbig", scale=256.0)
             act(T.keep[:], T.mask[:], F.Identity, "mask", "keep", scale=-1.0, bias=1.0)
         else:
-            scan(T.CH[:], T.mbig[:], T.cnt[:], 0.0, A.add, A.min, "mbig cnt", "CH")
-        scan(T.S1[:, ::-1], T.m8[:, ::-1], T.G[:, ::-1], T.G[:, 0:1], A.mult, A.add, "m8 G", "S1")
+            halves(t, (2, 3))
+        next_signs(T.G8[:], T.Arow[:], SA(0, 7), "Arow Arowx" + pk, "G8")
         if t == 0:
-            scan(T.CH[:], T.mbig[:], T.cnt[:], 0.0, A.add, A.min, "mbig cnt", "CH")
-        else:
-            cp(SB[:], T.CH[:, 15::16], "CH", sb)
-        tt(T.hrow[:], T.G[:], T.G8[:, 1:K + 1], A.add, "G G8 G8x", "hrow")
-        scan(T.S2[:], T.kp16[:], T.S1[:], 0.0, A.mult, A.max, "kp16 S1", "S2")
-        if t == 0:
-            cp(SB[:], T.CH[:, 15::16], "CH", sb)
-        cp(SA[:, 0:6], T.S2[:, 15::16], "S2", "sad%d" % t)
-        cp(SA[:, 6:12], T.S2[:, 15::16], "S2", "sae%d" % t)
-        send(t, LA[:, 0:18], SA[:], "aa%d" % t, "sad%d sae%d" % (t, t) + pk)
-        send(t, LB[:, 0:24], SB[:], "ab%d" % t, sb)
-        for b in (1, 2, 3, 0):
-            act(T.Dsb[:, C * b:C * b + C], T["p%d" % (4 + b)][:, 0:C], F.Copy, "p%d" % (4 + b), "Dsb%d" % b, scale=0.5)
-        cp(Hp.indirect(po), T.hrow[:], "hrow" + pk, "Hpos%d" % t)
+            masked()
+        tr(T.Brow[:, PAD:PAD + C], T.BX[:], "BX", "Brow")
+        scan(T.CH[:], T.mbig[:], T.cnt[:], 0.0, A.add, A.min, "mbig cnt", "CH")
         if t == R - 1:
             qmx("qv", "sv", 0, 128, T.vin[:], "vin", "qv")
-        else:
-            ms(T.Hpos[:, (PAD + C) * (t + 1):(PAD + C) * (t + 2)], 0.0, "Hpos%d" % (t + 1))
-        o = (PAD + C) * t + PAD
-        scan(T.Hm[:, 0:C], T.Hpos[:, o:o + C], T.mask[:, 0:C], 0.0, A.max, A.mult, "Hpos%d mask" % t, "Hm")
-        scan(T.Hm[:, C:400], T.Hpos[:, o:o + 16], T.mask[:, 0:16], 0.0, A.max, A.mult, "Hpos%d mask" % t, "Hmx")
+        tt(T.hv[:], T.Am[:].indirect(SA(0, 6)), T.G8[:, 1:K + 1], A.mult, "Am Amx G8" + pk, "hv")
+        half_d(1)
+        half_d(2)
+        scan(T.SP[:], T.hp[:], T.CH[:, 15::16], 0.0, A.mult, A.add, "hp CH", "SP")
         if t == 0:
             ms(T.PR[:, 0:16], 0.0, "PRx")
-        scan(T.T2[:, 782:399:-1], T.keep[:, 383:0:-1], T.Hm[:, 383:0:-1], 0.0, A.mult, A.add, "Hm keep", "T2b")
-        scan(T.T2[:, 0:400], T.keep[:], T.Hm[:], 0.0, A.mult, A.add, "Hm Hmx keep", "T2a")
-        cp(T.hr4[:, 0:2 * K], T.htab[:].indirect(LA[:, 0:12]), la + " htab", "hra")
-        act(T.hr4[:, 2 * K:4 * K], T.htab[:].indirect(LA[:, 0:12]), F.Copy, la + " htab", "hrb")
+        cp(Hp.indirect(SA(0, 6)), T.hv[:], "hv" + pk, "Hm%d" % t)
+        cp(T.sc[:, 16 * t:16 * t + 12], T.SP[:, 1::2], "SP", "sc%d" % t)
+        send(t, T.ld[:, 16 * t:16 * t + 12], T.sc[:, 16 * t:16 * t + 12], "ab%d" % t, "sc%d" % t)
+        next_signs(T.B8[:], T.Brow[:], LA(18, 25), "Brow Browx " + la, "B8")
+        half_d(3)
+        half_d(0)
         for j in (1, 2, 3):
-            ts(LA[:, 12 + 6 * j:18 + 6 * j], LA[:, 12:18], -16.0 * j, None, A.add, None, la, "off%d" % j)
-        if t == 0:
-            for b in range(4):
-                const(T.Dc[:, 128 * b:128 * b + 16], 16, 0.0, "Dcx")
-        for b in range(4):
-            act(T.Dc[:, 128 * b + 16:128 * b + 112], T.Dsb[:, C * b:C * b + C].indirect(LA[:, 30:36]), F.Copy,
-                "Dsb%d off3" % b, "Dc%d" % b)
-        for i in range(6):
-            tt(T.E[:, C * i:C * i + C], T.T2[:, 336 - 64 * i:2 * C].indirect(LA[:, 12:36]), T.hr4[:], A.is_equal,
-               "T2a T2b hra hrb off1 off2 off3 " + la, "E%d" % i)
-            for bn in range(4 * i, 4 * i + 4):
-                if bn < 22:
-                    act(T.JE[:, K * bn:K * bn + K], T.E[:, K * bn:K * bn + K], F.Identity, "E%d" % i, "JE%d vt%d" % (bn, bn),
-                        accum_out=T.vt[:, bn:bn + 1])
+            ts(LA(18 - 6 * j, 24 - 6 * j), LA(18, 24), -16.0 * j, None, A.add, None, la, "off%d" % j)
+        scan(T.T2[:, 0:C], T.keep[:], Hm(0, C), 0.0, A.mult, A.add, "keep Hm%d" % t, "T2a")
+        scan(T.T2[:, 782:399:-1], T.keep[:, 383:0:-1], Hm(383, 0, -1), 0.0, A.mult, A.add, "keep Hm%d" % t, "T2b")
+        for i in range(2):
+            tt(T.hr4[:, K * i:K * i + K], T.Brow[:].indirect(LA(18, 24)), T.B8[:, 1:K + 1], A.mult, "Brow Browx B8 " + la, "hr%d" % i)
+            if i == 0:
+                scan(T.T2[:, C:400], T.keep[:, 0:16], Hm(0, 16), T.T2[:, C - 1:C], A.mult, A.add, "keep T2a Hm%d" % t, "T2c")
+        act(T.hr4[:, 2 * K:4 * K], T.hr4[:, 0:2 * K], F.Copy, "hr0 hr1", "hr2 hr3")
+        tk = "T2a T2b T2c " + la
+        calls = [(0, 0, 0), (1, 1, 0)] + [(b0, 3, 0) for b0 in range(3, 23, 4)] + [(20, 3, 3)]
+        at, last = 0, []
+        for i, (b0, j1, j0) in enumerate(calls):
+            n = j1 - j0 + 1
+            tt(T.E[:, K * at:K * (at + n)], T.T2[:, 336 - 16 * b0:2 * C].indirect(LA(18 - 6 * j1, 24 - 6 * j0)), T.hr4[:, 0:K * n], A.is_equal,
+               tk + " " + ks("hr", n) + ks("off", max(j0, 1), j1 + 1), "E%d" % i)
+            for m in range(n):
+                bn, e = b0 + j1 - m, K * (at + m)
+                if at + m < 21:
+                    act(T.JE[:, e:e + K], T.E[:, e:e + K], F.Identity, "E%d" % i, "JE%d vt%d" % (bn, bn), accum_out=T.vt[:, bn:bn + 1])
                 else:
-                    red(T.vt[:, bn:bn + 1], T.E[:, K * bn:K * bn + K], A.add, "E5", "vt%d" % bn)
-            if i == 1:
-                act(T.Dc[:, 15::128], T.Dc[:, 111::128], F.Copy, ks("Dc", 4), "Dcx")
-            if i == 2:
-                act(LB[:, 24:48], LB[:, 0:24], F.Copy, lbn, "lbx%d" % t)
-        halves(t, (2, 3))
+                    last.append((bn, e, i))
+            at += n
+        for bn, e, i in last:
+            red(T.vt[:, bn:bn + 1], T.E[:, e:e + K], A.add, "E%d" % i, "vt%d" % bn)
+        for b in range(4):
+            act(T.Dc[:, 128 * b + 16:128 * b + 112], T.Dsb[:, C * b:C * b + C].indirect(LA(0, 6)), F.Copy, "Dsb%d off3" % b, "Dc%d" % b)
+        if t == 0:
+            halves(t, (2, 3))
+        act(T.Dc[:, 15::128], T.Dc[:, 111::128], F.Copy, ks("Dc", 4) + "Dcy", "Dcx")
         if t == R - 1:
-            act(T.PR[:, 16:112], T.ptab[:].indirect(LA[:, 30:36]), F.Copy, "ptab off3", "PR")
+            act(T.PR[:, 16:112], T.ptab[:].indirect(LA(0, 6)), F.Copy, "ptab off3 PRx", "PR")
             act(T.PR[:, 15:16], T.PR[:, 111:112], F.Copy, "PR", "PRx")
+        lw = T.lw
+        cp(lw[:, 48:60], T.ld[:, 16 * t:16 * t + 12], ld, "lw")
         tr(T.vT[:, :, 0:16], T.vt[:], ks("vt", 24) + "vtx", "vT")
+        for e in range(2):
+            ts(lw[:, 24 * e:24 * e + 24:2], lw[:, 48:60], 7, None, A.arith_shift_right, None, "lw", "lwa%d" % e)
+        for e in range(2):
+            scan(T.vS[:, e, :], T.kpF[:], T.vT[:, e, :], 0.0, A.mult, A.add, "kpF vT vTx", "vS%d" % e)
+        for e in range(2):
+            ts(lw[:, 24 * e + 1:24 * e + 24:2], lw[:, 48:60], 127, None, A.bitwise_and, None, "lw", "lwb%d" % e)
+        for e in range(2):
+            tr(T.vy[:, 32 * e:32 * e + 32], T.vS[:, :, 16 + 16 * e:32 + 16 * e], "vS0 vS1", "vy%d" % e)
         if t == 0:
             ms(T.alt[:], 1.0, "alt")
         for e in range(2):
-            scan(T.vS[:, e, :], T.kpF[:], T.vT[:, e, :], 0.0, A.mult, A.add, "kpF vT vTx", "vS%d" % e)
+            red(T.mv[:, e:e + 1], T.vy[:, 32 * e:32 * e + 32], A.max, "vy%d" % e, "mv%d" % e)
         if t == 0:
             ms(T.alt[:, 0::2], 0.0, "alt")
-        for e in range(2):
-            tr(T.vy[:, 32 * e:32 * e + 32], T.vS[:, :, 16 + 16 * e:32 + 16 * e], "vS0 vS1", "vy%d" % e)
-        for e in range(2):
-            red(T.mv[:, e:e + 1], T.vy[:, 32 * e:32 * e + 32], A.max, "vy%d" % e, "mv%d" % e)
         ts(T.rot[:], lc[:, 6:8], T.mv[:, 1:2], T.mv[:, 0:1], A.subtract, A.add, "lc1 lc2 mv0 mv1", "rot")
-        ts(T.moff[:], LB[:].indirect(T.rot[:]), 15.0, None, A.add, None, lbn + " rot lbx%d" % t, "moff")
+        ts(T.moff[:], lw[:, 0:48].indirect(T.rot[:]), 15.0, None, A.add, None, "lwa0 lwa1 lwb0 lwb1 rot", "moff")
 
         def win(b, h):
             return T.Dc[:, 128 * b:128 * b + 112].indirect(T.moff[:, 12 * h:12 * h + 12])

@@ -13,12 +13,12 @@ CODE = "float8_e4m3fn_x4"
 
 SCRATCH = {}
 for _d, _l in (
-        ("bfloat16", dict(xin=4 * C, uin=512, vin=512, X=4 * C, Z=4 * C, Y=4 * C, Xh=2 * C, IB2=2 * C, IB3=2 * C, alt=C, Dsb=4 * C, Dc=512,
+        ("bfloat16", dict(xin=4 * C, uin=512, vin=512, X=4 * C, Z=4 * C, Y=4 * C, Xh=4 * C, IB=4 * C, Dsb=4 * C, Dc=512,
                           eone=528, ebf=528, c16=C, mask=C, keep=C, mbig=C, horn=72, sg=72, aH=72, sh=32 * R, lh=32 * R, AX=C, BX=C,
                           Arow=PAD + C, Am=PAD + C, Brow=PAD + C, FL=7 * C, ZB=16 * HC, JS=16 * C, gt=400, sgn=C, ge=C, cap=C, cnt=C, CH=C,
-                          SC=2 * WIN, G8=112, B8=112, hv=K, Hm=R * (PAD + C), T2=784, hr4=C, E=24 * K, JE=24 * K)),
-        ("float32", dict(cf=64, lc=16, lb=8, D0=16, D1=16, E0=8, E1=8, MM=32, cS=16, LL=48, LU=48, LN=48, kpN=24, kpF=48, TT=112, tz=2, TS=32,
-                         cP=2, hp=24, SP=24, vt=32, vy=64, mv=2, OL=C, ysb=C, ptab=C, PR=112)),
+                          SC=2 * WIN, G8=112, B8=112, hv=K, Hm=R * (PAD + C), T2=784, hr4=C, E=24 * K, GE=16 * K, B1=K, G1=K, CS=1584)),
+        ("float32", dict(cf=64, lc=16, lb=8, D0=16, D1=16, E0=8, E1=8, MM=32, cS=16, LL=48, LU=48, LN=48, kpN=24, cb=72, TT=112, tz=2, TS=32,
+                         cP=2, hp=24, SP=24, vy=64, mv=2, OL=C, ysb=C, ptab=C, PR=112)),
         ("uint16", dict(cu=48, rot=2, moff=32, sa=8 * R, la=32 * R, sc=16 * R, ld=16 * R)),
         ("int32", dict(li=4, lw=64)),
         (CODE, dict(qu=128, qu2=256, qu3=128, qv=128, qw=512, qe=512, qz=C, qx0=C, qx1=C, qx2=C, qx3=C, lq0=C, lq1=C, lq2=C)),
@@ -27,8 +27,8 @@ for _d, _l in (
         SCRATCH[_n] = ("sbuf", [128, _l[_n]], _d)
 SCRATCH["St"] = ("sbuf", [128, 24, 16], "float32")
 SCRATCH["RR"] = ("sbuf", [128, 6, 24], "float32")
-for _n in ("vT", "vS"):
-    SCRATCH[_n] = ("sbuf", [128, 2, 48], "float32")
+for _n, _d in (("vA", "bfloat16"), ("vB", "bfloat16"), ("vS", "float32")):
+    SCRATCH[_n] = ("sbuf", [128, 2, 48], _d)
 for _b in range(8):
     SCRATCH["p%d" % _b] = ("psum", [128, 512], "float32")
 
@@ -148,7 +148,7 @@ def rank_program(g, core, T, topo):
 
     dma("S", T.uin[:], T.u[:], "", "uin")
     dma("Y", T.xin[:, 0:768], T.x[:, 0:768], "", "xa")
-    dma("S", T.xin[:, 768:1536], T.x[:, 768:1536], "", "xb")
+    dma("Y", T.xin[:, 768:1536], T.x[:, 768:1536], "", "xb")
 
     cf, cu, lc, lb = T.cf, T.cu, T.lc, T.lb
     St, MM, FL, JS, cS = T.St, T.MM, T.FL, T.JS, T.cS
@@ -161,21 +161,18 @@ def rank_program(g, core, T, topo):
     iota(cf[:, 24:48], [[1, 24]], 0, "cf2")
     iota(T.hp[:], [[0, 12], [128, 2]], 0, "hp")
     iota(T.c16[:], [[0, 24], [1, 16]], 0, "c16")
+    iota(T.cb[:, 0:35], [[4, 7], [-1, 5]], 3, "cb")
 
     ms(T.gt[:, C:400], 0.0, "gtx")
-    ms(T.vt[:, 24:32], 0.0, "vtx")
     ms(T.Dc[:], 0.0, "Dcy " + ks("Dc", 4))
-    ms(T.kpF[:], 1.0, "kpF")
-    ms(T.vT[:, :, 16:48], 0.0, "vTx")
+    ms(T.vA[:, :, 16:48], 0.0, "vAx vAy")
+    ms(T.vB[:, :, 16:33], 0.0, "vBx")
+    ms(T.vB[:, :, 33:48], 2.0 ** -6, "vBy")
     cp(cu[:, 0:24], cf[:, 0:24], "cf0 cf1", "cuU")
     ts(T.li[:, 1:2], T.li[:, 0:1], 15, None, A.bitwise_and, None, "li0", "li1")
-    ts(T.li[:, 2:3], T.li[:, 0:1], 31, None, A.bitwise_and, None, "li0", "li2")
-    ms(T.kpF[:, 16:17], 64.0, "kpF")
-    cp(lb[:, 0:2], T.li[:, 1:3], "li1 li2", "lane")
+    ms(T.CS[:, 47::48], -192.0, "CSx " + ks("CS", 6))
+    cp(lb[:, 0:1], T.li[:, 1:2], "li1", "lane")
     ts(lc[:, 0:6], cf[:, 16:22], lb[:, 0:1], 0.5, A.add, A.add, "cf1 lane", "lc0")
-    ts(lc[:, 6:7], lb[:, 0:1], 31.0, None, A.add, None, "lane", "lc1")
-    ts(lc[:, 7:8], lb[:, 0:1], 47.0, 54.0, A.add, A.min, "lane", "lc2")
-    ts(T.vT[:, :, 32], T.eone[:, 0:2], 30.0, lb[:, 1:2], A.add, A.subtract, "eone lane", "vTx")
     const(T.D0[:, 0::2], 8, -B, "D0x")
     const(T.LL[:, 16:48], 32, -B, "LLx")
     const(T.LU[:, 16:48], 32, B, "LUx")
@@ -252,7 +249,7 @@ def rank_program(g, core, T, topo):
         ts(ZW(*r), cS[:, r[0]:r[1]:r[2]], 192.5, -H, A.subtract, A.mult, ks("cS", *r), ks("z", *r))
 
     def xh(b, lo, hi):
-        return T.Xh[:, C * b + lo:C * b + hi] if b < 2 else T["IB%d" % b][:, 2 * lo + 1:2 * hi:2]
+        return T.Xh[:, C * b + lo:C * b + hi]
 
     def halves(t, bs):
         for b in bs:
@@ -397,47 +394,70 @@ def rank_program(g, core, T, topo):
         next_signs(T.G8[:], T.Arow[:], SA(0, 7), "Arow Arowx" + pk, "G8")
         if t == 0:
             masked()
+            ms(T.cb[:, 4:30:5], 40.0, "cb")
+            ms(T.cb[:, 30:32], 40.0, "cb2")
         tr(T.Brow[:, PAD:PAD + C], T.BX[:], "BX", "Brow")
         scan(T.CH[:], T.mbig[:], T.cnt[:], 0.0, A.add, A.min, "mbig cnt", "CH")
+        cp(T.G1[:], T.Am[:].indirect(SA(0, 6)), "Am Amx" + pk, "G1")
         if t == R - 1:
             qmx("qv", "sv", 0, 128, T.vin[:], "vin", "qv")
-        tt(T.hv[:], T.Am[:].indirect(SA(0, 6)), T.G8[:, 1:K + 1], A.mult, "Am Amx G8" + pk, "hv")
+        tt(T.hv[:], T.G1[:], T.G8[:, 1:K + 1], A.mult, "G1 G8", "hv")
         half_d(1)
         half_d(2)
         scan(T.SP[:], T.hp[:], T.CH[:, 15::16], 0.0, A.mult, A.add, "hp CH", "SP")
         if t == 0:
             ms(T.PR[:, 0:16], 0.0, "PRx")
+            tr(T.cb[:, 40:72], T.cb[:, 0:32], "cb cb2", "cbt")
         cp(Hp.indirect(SA(0, 6)), T.hv[:], "hv" + pk, "Hm%d" % t)
         cp(T.sc[:, 16 * t:16 * t + 12], T.SP[:, 1::2], "SP", "sc%d" % t)
         send(t, T.ld[:, 16 * t:16 * t + 12], T.sc[:, 16 * t:16 * t + 12], "ab%d" % t, "sc%d" % t)
         next_signs(T.B8[:], T.Brow[:], LA(18, 25), "Brow Browx " + la, "B8")
+        if t == 0:
+            ts(T.vA[:, :, 32], T.cb[:, 40:42], -2.0 ** -6, None, A.mult, None, "cbt", "vAy")
+        act(T.B1[:], T.Brow[:].indirect(LA(18, 24)), F.Copy, "Brow Browx " + la, "B1")
         half_d(3)
         half_d(0)
         for j in (1, 2, 3):
             ts(LA(18 - 6 * j, 24 - 6 * j), LA(18, 24), -16.0 * j, None, A.add, None, la, "off%d" % j)
         scan(T.T2[:, 0:C], T.keep[:], Hm(0, C), 0.0, A.mult, A.add, "keep Hm%d" % t, "T2a")
         scan(T.T2[:, 782:399:-1], T.keep[:, 383:0:-1], Hm(383, 0, -1), 0.0, A.mult, A.add, "keep Hm%d" % t, "T2b")
-        for i in range(2):
-            tt(T.hr4[:, K * i:K * i + K], T.Brow[:].indirect(LA(18, 24)), T.B8[:, 1:K + 1], A.mult, "Brow Browx B8 " + la, "hr%d" % i)
-            if i == 0:
+        for i in (3, 2, 1, 0):
+            tt(T.hr4[:, K * i:K * i + K], T.B1[:], T.B8[:, 1:K + 1], A.mult, "B1 B8", "hr%d" % i)
+            if i == 3:
                 scan(T.T2[:, C:400], T.keep[:, 0:16], Hm(0, 16), T.T2[:, C - 1:C], A.mult, A.add, "keep T2a Hm%d" % t, "T2c")
-        act(T.hr4[:, 2 * K:4 * K], T.hr4[:, 0:2 * K], F.Copy, "hr0 hr1", "hr2 hr3")
-        tk = "T2a T2b T2c " + la
-        calls = [(0, 0, 0), (1, 1, 0)] + [(b0, 3, 0) for b0 in range(3, 23, 4)] + [(20, 3, 3)]
-        at, last = 0, []
-        for i, (b0, j1, j0) in enumerate(calls):
-            n = j1 - j0 + 1
-            tt(T.E[:, K * at:K * (at + n)], T.T2[:, 336 - 16 * b0:2 * C].indirect(LA(18 - 6 * j1, 24 - 6 * j0)), T.hr4[:, 0:K * n], A.is_equal,
-               tk + " " + ks("hr", n) + ks("off", max(j0, 1), j1 + 1), "E%d" % i)
-            for m in range(n):
-                bn, e = b0 + j1 - m, K * (at + m)
-                if at + m < 21:
-                    act(T.JE[:, e:e + K], T.E[:, e:e + K], F.Identity, "E%d" % i, "JE%d vt%d" % (bn, bn), accum_out=T.vt[:, bn:bn + 1])
-                else:
-                    last.append((bn, e, i))
-            at += n
-        for bn, e, i in last:
-            red(T.vt[:, bn:bn + 1], T.E[:, e:e + K], A.add, "E%d" % i, "vt%d" % bn)
+
+        def table(i, a, b):
+            return T.T2[:, 336 - 64 * i:2 * C].indirect(LA(6 * a, 6 * b))
+
+        tk = "T2a T2b T2c off1 off2 off3 " + la
+
+        def whole(i, a=0, b=4):
+            tt(T.E[:, C * i + K * a:C * i + K * b], table(i, a, b), T.hr4[:, K * a:K * b], A.is_equal, tk + " " + ks("hr", a, b),
+               " ".join("E%d%d" % (i, m) for m in range(a, b)))
+
+        def match(i):
+            tt(T.E[:, C * i:C * i + C], T.GE[:, C * i:C * i + C], T.hr4[:], A.is_equal, "GE%d " % i + ks("hr", 4), ks("E%d" % i, 4))
+
+        def total(i):
+            scan(T.CS[:, 240 * i + 48:240 * i + 240], T.E[:, C * i:C * i + C:2], T.E[:, C * i + 1:C * i + C:2], -192.0, A.add, A.add,
+                 ks("E%d" % i, 4), "CS%d" % i)
+
+        for i in range(4):
+            act(T.GE[:, C * i:C * i + C], table(i, 0, 4), F.Copy, tk, "GE%d" % i)
+        whole(4, 3, 4)
+        whole(4, 0, 3)
+        whole(5)
+        match(0)
+        total(4)
+        match(1)
+        total(5)
+        match(2)
+        total(0)
+        total(1)
+        match(3)
+        total(2)
+        cp(T.lw[:, 48:60], T.ld[:, 16 * t:16 * t + 12], ld, "lw")
+        total(3)
         for b in range(4):
             act(T.Dc[:, 128 * b + 16:128 * b + 112], T.Dsb[:, C * b:C * b + C].indirect(LA(0, 6)), F.Copy, "Dsb%d off3" % b, "Dc%d" % b)
         if t == 0:
@@ -447,24 +467,22 @@ def rank_program(g, core, T, topo):
             act(T.PR[:, 16:112], T.ptab[:].indirect(LA(0, 6)), F.Copy, "ptab off3 PRx", "PR")
             act(T.PR[:, 15:16], T.PR[:, 111:112], F.Copy, "PR", "PRx")
         lw = T.lw
-        cp(lw[:, 48:60], T.ld[:, 16 * t:16 * t + 12], ld, "lw")
-        tr(T.vT[:, :, 0:16], T.vt[:], ks("vt", 24) + "vtx", "vT")
         for e in range(2):
             ts(lw[:, 24 * e:24 * e + 24:2], lw[:, 48:60], 7, None, A.arith_shift_right, None, "lw", "lwa%d" % e)
-        for e in range(2):
-            scan(T.vS[:, e, :], T.kpF[:], T.vT[:, e, :], 0.0, A.mult, A.add, "kpF vT vTx", "vS%d" % e)
+        tr(T.vA[:, :, 0:16], T.CS[:, 95::48], ks("CS", 6) + "CSx", "vA")
+        tr(T.vB[:, :, 0:16], T.CS[:, 47:1536:48], ks("CS", 6) + "CSx", "vB")
         for e in range(2):
             ts(lw[:, 24 * e + 1:24 * e + 24:2], lw[:, 48:60], 127, None, A.bitwise_and, None, "lw", "lwb%d" % e)
         for e in range(2):
+            scan(T.vS[:, e, :], T.vA[:, e, :], T.vB[:, e, :], 0.0, A.add, A.subtract, "vA vB vAx vAy vBx vBy", "vS%d" % e)
+        for e in range(2):
             tr(T.vy[:, 32 * e:32 * e + 32], T.vS[:, :, 16 + 16 * e:32 + 16 * e], "vS0 vS1", "vy%d" % e)
-        if t == 0:
-            ms(T.alt[:], 1.0, "alt")
         for e in range(2):
             red(T.mv[:, e:e + 1], T.vy[:, 32 * e:32 * e + 32], A.max, "vy%d" % e, "mv%d" % e)
-        if t == 0:
-            ms(T.alt[:, 0::2], 0.0, "alt")
-        ts(T.rot[:], lc[:, 6:8], T.mv[:, 1:2], T.mv[:, 0:1], A.subtract, A.add, "lc1 lc2 mv0 mv1", "rot")
-        ts(T.moff[:], lw[:, 0:48].indirect(T.rot[:]), 15.0, None, A.add, None, "lwa0 lwa1 lwb0 lwb1 rot", "moff")
+        ts(T.rot[:, 0:1], T.mv[:, 0:1], T.mv[:, 1:2], 64.0, A.subtract, A.mult, "mv0 mv1", "rot")
+        for e in range(2):
+            ts(T.moff[:, 16 * e:16 * e + 16], lw[:, 16 * e:16 * e + 40].indirect(T.rot[:, 0:1]), 15.0, None, A.add, None,
+               "lw lwa0 lwa1 lwb0 lwb1 rot", "moff%d" % e)
 
         def win(b, h):
             return T.Dc[:, 128 * b:128 * b + 112].indirect(T.moff[:, 12 * h:12 * h + 12])
@@ -473,14 +491,15 @@ def rank_program(g, core, T, topo):
             return T.Z[:, 4 * HC * h + b:4 * HC * (h + 1):4]
 
         def fused(b, h):
-            tt(zv(b, h), win(b, h), xh(b, HC * h, HC * h + HC), A.add, "Dc%d Xh%d Dcx moff" % (b, b), "Z%d" % (4 * h + b))
+            tt(zv(b, h), win(b, h), xh(b, HC * h, HC * h + HC), A.add, "Dc%d Xh%d Dcx " % (b, b) + ks("moff", h + 1), "Z%d" % (4 * h + b))
 
         def fetch(b, h):
-            act(T["IB%d" % b][:, C * h:C * h + C:2], win(b, h), F.Copy, "Dc%d Dcx moff" % b, "IB%d%d" % (b, h))
+            o = C * b + HC * h
+            act(T.IB[:, o:o + HC], win(b, h), F.Copy, "Dc%d Dcx " % b + ks("moff", h + 1), "IB%d%d" % (b, h))
 
         def pairs(b, h):
-            scan(T.Z[:, 4 * HC * h + b - 2:4 * HC * (h + 1):2], T.alt[:], T["IB%d" % b][:, C * h:C * h + C], 0.0, A.mult, A.add,
-                 "alt IB%d%d Xh%d" % (b, h, b), "Z%d Z%d" % (4 * h + b, 4 * h + b - 2))
+            o = C * b + HC * h
+            tt(zv(b, h), T.IB[:, o:o + HC], xh(b, HC * h, HC * h + HC), A.add, "IB%d%d Xh%d" % (b, h, b), "Z%d" % (4 * h + b))
 
         def product(h):
             qmx("qz", "sz", HC * h, HC * h + HC, T.Z[:, 4 * HC * h:4 * HC * (h + 1)], ks("Z", 4 * h, 4 * h + 4), "qz%d" % h)
@@ -496,29 +515,30 @@ def rank_program(g, core, T, topo):
                 act(Xb, Yb, F.Copy, "Y%d" % i, "X%d" % i, scale=2.0 ** -5)
             return Xb, Yb
 
-        fetch(2, 0)
-        fetch(2, 1)
-        fetch(3, 1)
+        for b, h in ((2, 0), (3, 0), (1, 1), (2, 1), (3, 1)):
+            fetch(b, h)
         if t == 0:
             for b in range(4):
                 act(T.Y[:, C * b:C * b + C], T.xin[:, b::4], F.Copy, "xa xb", "Y%d Y%d" % (b, b + 4), scale=32.0)
         if t == R - 1:
-            act(T.OL[:], T.PR[:].indirect(T.moff[:, 0:24]), F.Copy, "PR PRx moff", "OL")
+            act(T.OL[:], T.PR[:].indirect(T.moff[:, 0:24]), F.Copy, "PR PRx moff0 moff1", "OL")
             dma("S", T.ol[:], T.OL[0::16, :], "OL", "")
-        fused(1, 0)
-        fused(3, 0)
-        pairs(2, 0)
-        pairs(2, 1)
         fused(0, 0)
-        pairs(3, 1)
-        product(0)
+        fused(1, 0)
+        pairs(2, 0)
+        pairs(3, 0)
         fused(0, 1)
-        fused(1, 1)
+        product(0)
+        pairs(1, 1)
+        pairs(2, 1)
+        pairs(3, 1)
         state(0)
         product(1)
         for i in range(1, 7):
             state(i)
         qx, sx = "qx%d" % (t + 1), "sx%d" % (t + 1)
+        if t == R - 1:
+            Xb, Yb = state(7)
         qmx(qx, sx, 0, HC, T.X[:, 0:4 * HC], ks("X", 4), qx + "a")
         if t < R - 1:
             mm(3, "qu", "su", 0, qx, sx, "qu %sa" % qx, 0, HC)
@@ -527,7 +547,8 @@ def rank_program(g, core, T, topo):
             dma("Y", T.oc[:, 0:4 * HC], T[qx][:, 0:HC].bitcast(dt.uint8), qx + "a", "")
             act(T.ysb[:, 0:HC], T.p3[:, 0:HC], F.Copy, "p3", "ya")
             dma("S", T.y[:, 0:HC], T.ysb[:, 0:HC], "ya", "")
-        Xb, Yb = state(7)
+        if t < R - 1:
+            Xb, Yb = state(7)
         ts(Xb, Yb, 2.0 ** -5, None, A.mult, None, "Y7", "X7")
         if t < R - 1:
             tr(St[:, 0:12, :], T.p3[:, 0:HC], "p3", "Sa")

@@ -9,20 +9,21 @@ H = 2.0 ** 88
 B = 2.0 ** 97
 PAD = 48
 WIN = 304
+ROWS = ((0, 0), (1, 128), (4, 128))
 CODE = "float8_e4m3fn_x4"
 
 SCRATCH = {}
 for _d, _l in (
         ("bfloat16", dict(xin=4 * C, uin=512, vin=512, X=4 * C, Z=4 * C, Y=4 * C, Xh=4 * C, IB=4 * C, Dsb=4 * C, Dc=512,
                           eone=528, ebf=528, c16=C, mask=C, keep=C, mbig=C, horn=72, sg=72, aH=72, sh=32 * R, lh=32 * R, AX=C, BX=C,
-                          Arow=PAD + C, Am=PAD + C, Brow=PAD + C, FL=7 * C, ZB=16 * HC, JS=16 * C, gt=400, sgn=C, ge=C, cap=C, cnt=C, CH=C,
-                          SC=2 * WIN, G8=112, B8=112, hv=K, Hm=R * (PAD + C), T2=784, hr4=C, E=24 * K, GE=16 * K, B1=K, G1=K, CS=1584)),
+                          Arow=PAD + C, Am=PAD + C, Brow=PAD + C, FL=7 * C, ZB=16 * HC, JS=16 * C, gt=C, sgn=HC, ge=16 + C, cap=16 + C, cnt=16 + C, CH=C,
+                          SC=2 * WIN, G8=112, B8=112, hv=K, Hm=R * (PAD + C), T2=784, hr4=C, E=24 * K, GE=16 * K, B1=K, G1=K, zero=2 * C, CS=1584)),
         ("float32", dict(cf=64, lc=16, lb=8, D0=16, D1=16, E0=8, E1=8, MM=32, cS=16, LL=48, LU=48, LN=48, kpN=24, cb=72, TT=112, tz=2, TS=32,
-                         cP=2, hp=24, SP=24, vy=64, mv=2, OL=C, ysb=C, ptab=C, PR=112)),
+                         cP=2, hp=24, SP=48, vy=64, mv=64, OL=C, ysb=C, ptab=C, PR=112)),
         ("uint16", dict(cu=48, rot=2, moff=32, sa=8 * R, la=32 * R, sc=16 * R, ld=16 * R)),
         ("int32", dict(li=4, lw=64)),
-        (CODE, dict(qu=128, qu2=256, qu3=128, qv=128, qw=512, qe=512, qz=C, qx0=C, qx1=C, qx2=C, qx3=C, lq0=C, lq1=C, lq2=C)),
-        ("uint8", dict(su=128, su2=256, su3=128, sv=128, sw=512, se=512, sz=C, sx0=C, sx1=C, sx2=C, sx3=C, ls0=C, ls1=C, ls2=C))):
+        (CODE, dict(qu=128, qu2=256, qu3=128, qv=128, qw=512, qe=512, qz=C, qx0=HC + C, qx1=HC + C, qx2=HC + C, qx3=C, lq0=C, lq1=C, lq2=C)),
+        ("uint8", dict(su=128, su2=256, su3=128, sv=128, sw=512, se=512, sz=C, sx0=HC + C, sx1=HC + C, sx2=HC + C, sx3=C, ls0=C, ls1=C, ls2=C))):
     for _n in _l:
         SCRATCH[_n] = ("sbuf", [128, _l[_n]], _d)
 SCRATCH["St"] = ("sbuf", [128, 24, 16], "float32")
@@ -126,9 +127,9 @@ def rank_program(g, core, T, topo):
     def qmx(qn, sn, lo, hi, a, Rd, W):
         op("V", lambda: V.quantize_mx(T[qn][:, lo:hi], T[sn][:, lo:hi], a), Rd, W)
 
-    def mm(bank, wq, wsn, wlo, mq, msn, Rd, lo=0, hi=C):
+    def mm(bank, wq, wsn, wlo, mq, msn, Rd, lo=0, hi=C, start=True, stop=True):
         op("T", lambda: PE.matmul_mx(T["p%d" % bank][:, 0:hi - lo], T[wq][:, wlo:wlo + 128], T[wsn][:, wlo:wlo + 128],
-                                     T[mq][:, lo:hi], T[msn][:, lo:hi], True, True), Rd, "p%d" % bank)
+                                     T[mq][:, lo:hi], T[msn][:, lo:hi], start, stop), Rd, "p%d" % bank)
 
     def iota(out, pat, base, W):
         op("G", lambda: g.iota(out, pat, base, 0, allow_small_or_imprecise_dtypes=True), "", W)
@@ -152,18 +153,19 @@ def rank_program(g, core, T, topo):
 
     cf, cu, lc, lb = T.cf, T.cu, T.lc, T.lb
     St, MM, FL, JS, cS = T.St, T.MM, T.FL, T.JS, T.cS
-    ZW = lambda a, b, s=1: T.ZB[:, 16 * (HC - 1) + a:16 * (HC - 1) + b:s]
+    ZW = lambda a, b, s=1: T.ZB[:, HC * a + HC - 1:HC * b:HC * s]
     iota(cf[:, 0:16], [[16, 2], [32, 4], [0, 2]], 0, "cf0")
     iota(cf[:, 16:24], [[16, 8]], 0, "cf1")
     op("G", lambda: g.iota(T.li[:, 0:1], [[0, 1]], 0, 1), "", "li0")
     ms(T.eone[:], 1.0, "eone")
-    op("G", lambda: g.affine_select(T.ebf[:], T.eone[:], [[-1, 528]], A.is_equal, 0.0, 3, 4), "eone", "ebf")
     iota(cf[:, 24:48], [[1, 24]], 0, "cf2")
-    iota(T.hp[:], [[0, 12], [128, 2]], 0, "hp")
-    iota(T.c16[:], [[0, 24], [1, 16]], 0, "c16")
     iota(T.cb[:, 0:35], [[4, 7], [-1, 5]], 3, "cb")
+    op("G", lambda: g.affine_select(T.ebf[:], T.eone[:], [[-1, 528]], A.is_equal, 0.0, 3, 4), "eone", "ebf")
+    iota(T.c16[:], [[0, 24], [1, 16]], 0, "c16")
+    iota(T.hp[:], [[0, 12], [128, 2]], 0, "hp")
 
-    ms(T.gt[:, C:400], 0.0, "gtx")
+    ms(T.ge[:, 15:16], -96.0, "gex")
+    ms(T.cap[:, 15:16], 128.0, "capx")
     ms(T.Dc[:], 0.0, "Dcy " + ks("Dc", 4))
     ms(T.vA[:, :, 16:48], 0.0, "vAx vAy")
     ms(T.vB[:, :, 16:33], 0.0, "vBx")
@@ -172,7 +174,9 @@ def rank_program(g, core, T, topo):
     ts(T.li[:, 1:2], T.li[:, 0:1], 15, None, A.bitwise_and, None, "li0", "li1")
     ms(T.CS[:, 47::48], -192.0, "CSx " + ks("CS", 6))
     cp(lb[:, 0:1], T.li[:, 1:2], "li1", "lane")
-    ts(lc[:, 0:6], cf[:, 16:22], lb[:, 0:1], 0.5, A.add, A.add, "cf1 lane", "lc0")
+    cp(cu[:, 24:48], cf[:, 24:48], "cf2", "cuA")
+    ms(T.cb[:, 4:30:5], 40.0, "cb")
+    ms(T.cb[:, 30:32], 40.0, "cb2")
     const(T.D0[:, 0::2], 8, -B, "D0x")
     const(T.LL[:, 16:48], 32, -B, "LLx")
     const(T.LU[:, 16:48], 32, B, "LUx")
@@ -191,11 +195,13 @@ def rank_program(g, core, T, topo):
         act(T["su" + n][:], T.su[:].indirect(cu[:, a:b]), F.Copy, "qu cuU", "su" + n)
 
     qmx("qu", "su", 0, 128, T.uin[:], "uin", "qu")
-    qmx("qx0", "sx0", 0, HC, T.xin[:, 0:4 * HC], "xa", "qx0a")
-    mm(3, "qu", "su", 0, "qx0", "sx0", "qu qx0a", 0, HC)
+    qmx("qx0", "sx0", HC, C, T.xin[:, 0:4 * HC], "xa", "qx0a")
+    mm(3, "qu", "su", 0, "qx0", "sx0", "qu qx0a", HC, C)
     pick_u("2", 0, 16)
+    ts(lc[:, 0:6], cf[:, 16:22], lb[:, 0:1], 0.5, A.add, A.add, "cf1 lane", "lc0")
+    ts(T.cnt[:, 0:6], cf[:, 16:22], lb[:, 0:1], 0.5, A.add, A.add, "cf1 lane", "lc2")
     tr(St[:, 0:12, :], T.p3[:, 0:HC], "p3", "Sa")
-    qmx("qx0", "sx0", HC, C, T.xin[:, 4 * HC:4 * C], "xb", "qx0b")
+    qmx("qx0", "sx0", C, HC + C, T.xin[:, 4 * HC:4 * C], "xb", "qx0b")
     dma("Y", T.qw[:].bitcast(dt.uint8), T.wc[:], "xa xb", "qw")
     dma("Y", T.sw[:], T.ws[:], "", "sw")
     dma("Y", T.vin[:], T.v[:], "", "vin")
@@ -243,7 +249,7 @@ def rank_program(g, core, T, topo):
 
     def vsum(n):
         m = n // 2 - 1
-        scan(T.ZB[:, n::16], FL[:, C * m:C * m + HC], FL[:, C * m + HC:C * m + C], -95.5 * H, A.add, A.add, "FL%d" % m, "z%d" % n)
+        scan(T.ZB[:, HC * n:HC * n + HC], FL[:, C * m:C * m + HC], FL[:, C * m + HC:C * m + C], -95.5 * H, A.add, A.add, "FL%d" % m, "z%d" % n)
 
     def zs(*r):
         ts(ZW(*r), cS[:, r[0]:r[1]:r[2]], 192.5, -H, A.subtract, A.mult, ks("cS", *r), ks("z", *r))
@@ -270,66 +276,81 @@ def rank_program(g, core, T, topo):
         LA = lambda a, b: T.la[:, 32 * t + a:32 * t + b]
         SH, LH = T.sh[:, 32 * t:32 * t + 24], T.lh[:, 32 * t:32 * t + 24]
         qk = "%sa %sb" % (qx, qx)
-        mm(0, "qu2", "su2", 0, qx, sx, "qu2 su2 " + qk)
-        mm(7, "qu", "su", 0, qx, sx, "qu " + qk, HC, C)
-        mm(1, "qu2", "su2", 128, qx, sx, "qu2 su2 " + qk)
-        mm(4, "qu2", "su2", 128, qx, sx, "qu2 su2 " + qk)
-        mm(2, "qu3", "su3", 0, qx, sx, "qu3 su3 " + qk)
-        mm(3, "qu3", "su3", 0, qx, sx, "qu3 su3 " + qk)
-        send(t, T[lq][:].bitcast(dt.uint8), T[qx][:].bitcast(dt.uint8), "aq%d" % t, qk)
-        send(t, T[ls][:], T[sx][:], "aq%d" % t, qk)
+        for bank, w in ROWS:
+            mm(bank, "qu2", "su2", w, qx, sx, "qu2 su2 " + qk, C if t else HC, HC + C, t == 0, True)
+            if bank == 0:
+                mm(7, "qu", "su", 0, qx, sx, "qu " + qk, C, HC + C)
+        mm(2, "qu3", "su3", 0, qx, sx, "qu3 su3 " + qk, HC, HC + C)
+        mm(3, "qu3", "su3", 0, qx, sx, "qu3 su3 " + qk, HC, HC + C)
+        send(t, T[lq][:].bitcast(dt.uint8), T[qx][:, HC:HC + C].bitcast(dt.uint8), "aq%d" % t, qk)
+        send(t, T[ls][:], T[sx][:, HC:HC + C], "aq%d" % t, qk)
         if t == 0:
+            iota(T.zero[:], [[0, 2 * C]], 0, "zero")
+        if t == 1:
             iota(T.ptab[:], [[1, C]], 0, "ptab")
         for n in (0, 2, 1):
             spass(n)
         tr(St[:, 12:24, :], T.p7[:, 0:HC], "p7", "Sb")
-        sort_a(1)
-        vpass(3)
-        sort_b(1)
-        sort_c(1)
+        signs = lambda: ts(T.sg[:], St[:, :, 1:4], 0.0, None, A.is_gt, None, "Sa Sb", "sg")
+        if t == 0:
+            ts(T.mask[:], T.c16[:], lb[:, 0:1], None, A.is_equal, None, "c16 lane", "mask")
+            sort_a(1)
+            vpass(3)
+            sort_b(1)
+            sort_c(1)
+            vsum(3)
+            signs()
+        else:
+            vpass(3)
+            sort_a(1)
+            vsum(3)
+            signs()
+            sort_b(1)
+            sort_c(1)
         spass(4)
         spass(6)
-        vsum(3)
-        ts(T.sg[:], St[:, :, 1:4], 0.0, None, A.is_gt, None, "Sa Sb", "sg")
+        if t == 0:
+            vpass(5)
+        second(3)
+        scan(T.aH[:], T.horn[:], T.sg[:], 0.0, A.mult, A.add, ks("horn", 3) + "sg", "aH")
+        if t > 0:
+            vpass(5)
+        spass(11)
         zs(0, 3, 1)
-        vpass(5)
-        second(0, 2, 1, 3)
+        vpass(7)
+        second(0, 2, 1)
         spass(8)
         spass(10)
-        spass(11)
-        vpass(7)
         vsum(5)
+        vsum(7)
         zs(4, 7, 2)
         vpass(9)
-        second(4, 6)
+        second(5, 7, 4, 6)
         spass(12)
         spass(14)
-        vsum(7)
-        second(5)
-        vsum(9)
-        scan(T.aH[:], T.horn[:], T.sg[:], 0.0, A.mult, A.add, ks("horn", 3) + "sg", "aH")
-        second(7)
         vpass(13)
+        vsum(9)
         vpass(15)
         zs(11, 12, 1)
         vsum(13)
-        if t == 0:
-            qmx("qe", "se", 128, 256, T.ebf[:, 2:514], "ebf", "qe1")
         vsum(15)
         zs(8, 16, 2)
-        if t == 0:
-            cp(cu[:, 24:48], cf[:, 24:48], "cf2", "cuA")
         act(SH, T.aH[:, 2::3], F.Identity, "aH", sh, bias=128.0)
         send(t, LH, SH, "ah%d" % t, sh)
         halves(t, (0,))
         act(T.AX[:], SH.indirect(cu[:, 24:48]), F.Copy, sh + " cuA", "AX")
-        halves(t, (1,))
+        halves(t, (1, 2))
         for b in (1, 2, 3, 0) if t else ():
             mm(4 + b, "qe", "se", 128 * b, lq, ls, "qe%d %s" % (b, lq))
         zk = ks("z", 16)
+        if t == 0:
+            tr(T.cb[:, 40:72], T.cb[:, 0:32], "cb cb2", "cbt")
+            ts(T.mbig[:], T.mask[:], 256.0, None, A.mult, None, "mask", "mbig")
         tt(T.LL[:, 0:16], MM[:, 1::2], ZW(0, 16), A.min, "M0 M1 " + ks("M", 8, 16) + zk, "LL")
         tt(T.LU[:, 0:16], MM[:, 1::2], ZW(0, 16), A.max, "M0 M1 " + ks("M", 8, 16) + zk, "LU")
         ts(T.LN[:, 0:16], ZW(0, 16), 0.0, H, A.is_lt, A.mult, zk, "LN")
+        if t == 0:
+            ts(T.vA[:, :, 32], T.cb[:, 40:42], -2.0 ** -6, None, A.mult, None, "cbt", "vAy")
         for e in range(2):
             scan(T.RR[:, e, :], T.LL[:, e::2], T.LL[:, e::2], -B, A.max, A.max, "LL LLx", "RR%d" % e)
         for e in range(2):
@@ -341,35 +362,33 @@ def rank_program(g, core, T, topo):
         tr(T.TT[:, 0:96], T.RR[:, :, 8:24], ks("RR", 6), "TT")
         if t == 0:
             qmx("qe", "se", 384, 512, T.ebf[:, 0:512], "ebf", "qe3")
+        red(T.tz[:, 0:1], T.TT[:, 64:97], A.add, "TT TTx", "tz")
+        tr(T.Arow[:, PAD:PAD + C], T.AX[:], "AX", "Arow")
+        scan(T.TS[:], T.TT[:, 0:32], T.TT[:, 32:64], T.tz[:, 0:1], A.max, A.min, "TT tz", "TS")
+        if t == 0:
+            qmx("qe", "se", 128, 256, T.ebf[:, 2:514], "ebf", "qe1")
             for b in (1, 2, 3, 0):
                 mm(4 + b, "qe", "se", 128 * b, lq, ls, "qe%d %s" % (b, lq))
-        red(T.tz[:, 0:1], T.TT[:, 64:97], A.add, "TT TTx", "tz")
-        if t == 0:
-            ts(T.mask[:], T.c16[:], lb[:, 0:1], None, A.is_equal, None, "c16 lane", "mask")
-        else:
-            tr(T.Arow[:, PAD:PAD + C], T.AX[:], "AX", "Arow")
-        scan(T.TS[:], T.TT[:, 0:32], T.TT[:, 32:64], T.tz[:, 0:1], A.max, A.min, "TT tz", "TS")
+            act(T.keep[:], T.mask[:], F.Identity, "mask", "keep", scale=-1.0, bias=1.0)
         cut = T.TS[:, 31:32]
         act(T.sgn[:, 0:HC], T.p3[:, 0:HC], F.Sign, "p3 TS", "sgn", bias=cut, scale=-1.0)
-        act(T.ge[:, 0:HC], T.sgn[:, 0:HC], F.Sign, "sgn", "ge0", bias=1.0, scale=-1.0)
-        ts(T.gt[:, 0:C], T.p2[:, 0:C], cut, None, A.is_gt, None, "p2 TS", "gt")
-        ts(T.ge[:, HC:C], T.p2[:, HC:C], cut, None, A.is_ge, None, "p2 TS", "ge1")
-        scan(T.cap[:, ::-1], T.eone[:, 0:C], T.gt[:, C:0:-1], 96.0, A.mult, A.subtract, "eone gt gtx", "cap")
-        masked = lambda: scan(T.Am[:, PAD:PAD + C], T.Arow[:, PAD:PAD + C], T.mask[:], 0.0, A.max, A.mult, "Arow mask", "Am")
-        if t == 0:
-            tr(T.Arow[:, PAD:PAD + C], T.AX[:], "AX", "Arow")
-        else:
-            masked()
-        scan(T.cnt[:], T.ge[:], T.cap[:], 0.0, A.add, A.min, "ge0 ge1 cap", "cnt")
+        act(T.ge[:, 16:16 + HC], T.sgn[:, 0:HC], F.Sign, "sgn", "ge0", bias=1.0, scale=-1.0)
+        ts(T.gt[:], T.p2[:, 0:C], cut, None, A.is_gt, None, "p2 TS", "gt")
+        ts(T.ge[:, 16 + HC:16 + C], T.p2[:, HC:C], cut, None, A.is_ge, None, "p2 TS", "ge1")
+        scan(T.cap[:, 16:16 + C], T.eone[:, 0:C], T.gt[:], 0.0, A.mult, A.add, "eone gt", "cap")
+        above = T.cap[:, 15 + C:16 + C]
+        scan(T.Am[:, PAD:PAD + C], T.Arow[:, PAD:PAD + C], T.mask[:], 0.0, A.max, A.mult, "Arow mask", "Am")
+        scan(T.cnt[:, 15:16 + C], T.ge[:, 15:16 + C], T.cap[:, 15:16 + C], above, A.add, A.min, "ge0 ge1 gex cap capx", "cnt")
+        ts(lc[:, 8:10], lc[:, 0:2], above, -96.0, A.add, A.add, "lc0 cap", "lc1")
         act(T.BX[:], LH.indirect(cu[:, 24:48]), F.Copy, lh + " cuA", "BX")
         o = (PAD + C) * t
         Hp, Hm = T.Hm[:, o:o + PAD + C], lambda a, b, s=1, o=o + PAD: T.Hm[:, o + a:o + b:s]
         ms(Hp, 0.0, "Hm%d" % t)
         for s in range(2):
-            act(JS[:, C * s:C * s + 320], T.cnt[:, 0:320], F.Sign, "cnt lc0", "JS%d cP%d" % (s, s),
-                bias=lc[:, s:s + 1], scale=-1.0, accum_out=T.cP[:, s:s + 1])
+            act(JS[:, C * s:C * s + 320], T.cnt[:, 16:336], F.Sign, "cnt lc1", "JS%d cP%d" % (s, s),
+                bias=lc[:, 8 + s:9 + s], scale=-1.0, accum_out=T.cP[:, s:s + 1])
         for s in range(2, 6):
-            ts(FL[:, C * s:C * s + WIN], T.cnt[:, 16 * s:16 * s + WIN], lc[:, s:s + 1], None, A.is_le, None, "cnt lc0", "FL%d" % s)
+            ts(FL[:, C * s:C * s + WIN], T.cnt[:, 16 * s + 16:16 * s + 16 + WIN], T.cnt[:, 15:16], T.cnt[:, s:s + 1], A.subtract, A.is_le, "cnt lc2", "FL%d" % s)
         W2 = WIN // 2
         for s in range(2, 6):
             o = C * s
@@ -386,140 +405,135 @@ def rank_program(g, core, T, topo):
         def half_d(b):
             act(T.Dsb[:, C * b:C * b + C], T["p%d" % (4 + b)][:, 0:C], F.Copy, "p%d" % (4 + b), "Dsb%d" % b, scale=0.5)
 
-        if t == 0:
-            act(T.mbig[:], T.mask[:], F.Copy, "mask", "mbig", scale=256.0)
-            act(T.keep[:], T.mask[:], F.Identity, "mask", "keep", scale=-1.0, bias=1.0)
-        else:
-            halves(t, (2, 3))
+        halves(t, (3,))
         next_signs(T.G8[:], T.Arow[:], SA(0, 7), "Arow Arowx" + pk, "G8")
-        if t == 0:
-            masked()
-            ms(T.cb[:, 4:30:5], 40.0, "cb")
-            ms(T.cb[:, 30:32], 40.0, "cb2")
         tr(T.Brow[:, PAD:PAD + C], T.BX[:], "BX", "Brow")
-        scan(T.CH[:], T.mbig[:], T.cnt[:], 0.0, A.add, A.min, "mbig cnt", "CH")
         cp(T.G1[:], T.Am[:].indirect(SA(0, 6)), "Am Amx" + pk, "G1")
-        if t == R - 1:
-            qmx("qv", "sv", 0, 128, T.vin[:], "vin", "qv")
+        scan(T.CH[:], T.mbig[:], T.cnt[:, 16:16 + C], 0.0, A.add, A.min, "mbig cnt", "CH")
         tt(T.hv[:], T.G1[:], T.G8[:, 1:K + 1], A.mult, "G1 G8", "hv")
         half_d(1)
         half_d(2)
-        scan(T.SP[:], T.hp[:], T.CH[:, 15::16], 0.0, A.mult, A.add, "hp CH", "SP")
-        if t == 0:
-            ms(T.PR[:, 0:16], 0.0, "PRx")
-            tr(T.cb[:, 40:72], T.cb[:, 0:32], "cb cb2", "cbt")
+        ts(T.SP[:, 24:48], T.CH[:, 15::16], T.cnt[:, 15:16], None, A.subtract, None, "CH cnt", "SQ")
+        if t == R - 1:
+            qmx("qv", "sv", 0, 128, T.vin[:], "vin", "qv")
         cp(Hp.indirect(SA(0, 6)), T.hv[:], "hv" + pk, "Hm%d" % t)
-        cp(T.sc[:, 16 * t:16 * t + 12], T.SP[:, 1::2], "SP", "sc%d" % t)
-        send(t, T.ld[:, 16 * t:16 * t + 12], T.sc[:, 16 * t:16 * t + 12], "ab%d" % t, "sc%d" % t)
+        scan(T.SP[:, 0:24], T.hp[:], T.SP[:, 24:48], 0.0, A.mult, A.add, "hp SQ", "SP")
         next_signs(T.B8[:], T.Brow[:], LA(18, 25), "Brow Browx " + la, "B8")
-        if t == 0:
-            ts(T.vA[:, :, 32], T.cb[:, 40:42], -2.0 ** -6, None, A.mult, None, "cbt", "vAy")
         act(T.B1[:], T.Brow[:].indirect(LA(18, 24)), F.Copy, "Brow Browx " + la, "B1")
         half_d(3)
-        half_d(0)
+        scan(T.T2[:, 0:C], T.keep[:], Hm(0, C), 0.0, A.mult, A.add, "keep Hm%d" % t, "T2a")
+        cp(T.sc[:, 16 * t:16 * t + 12], T.SP[:, 1:24:2], "SP", "sc%d" % t)
+        send(t, T.ld[:, 16 * t:16 * t + 12], T.sc[:, 16 * t:16 * t + 12], "ab%d" % t, "sc%d" % t)
         for j in (1, 2, 3):
             ts(LA(18 - 6 * j, 24 - 6 * j), LA(18, 24), -16.0 * j, None, A.add, None, la, "off%d" % j)
-        scan(T.T2[:, 0:C], T.keep[:], Hm(0, C), 0.0, A.mult, A.add, "keep Hm%d" % t, "T2a")
-        scan(T.T2[:, 782:399:-1], T.keep[:, 383:0:-1], Hm(383, 0, -1), 0.0, A.mult, A.add, "keep Hm%d" % t, "T2b")
-        for i in (3, 2, 1, 0):
+        scan(T.T2[:, C:2 * C], T.keep[:], Hm(0, C), T.T2[:, C - 1:C], A.mult, A.add, "keep T2a Hm%d" % t, "T2b")
+        for i in range(4):
             tt(T.hr4[:, K * i:K * i + K], T.B1[:], T.B8[:, 1:K + 1], A.mult, "B1 B8", "hr%d" % i)
-            if i == 3:
-                scan(T.T2[:, C:400], T.keep[:, 0:16], Hm(0, 16), T.T2[:, C - 1:C], A.mult, A.add, "keep T2a Hm%d" % t, "T2c")
 
         def table(i, a, b):
             return T.T2[:, 336 - 64 * i:2 * C].indirect(LA(6 * a, 6 * b))
 
-        tk = "T2a T2b T2c off1 off2 off3 " + la
+        tk = "T2a T2b off1 off2 off3 " + la
 
         def whole(i, a=0, b=4):
             tt(T.E[:, C * i + K * a:C * i + K * b], table(i, a, b), T.hr4[:, K * a:K * b], A.is_equal, tk + " " + ks("hr", a, b),
                " ".join("E%d%d" % (i, m) for m in range(a, b)))
 
-        def match(i):
-            tt(T.E[:, C * i:C * i + C], T.GE[:, C * i:C * i + C], T.hr4[:], A.is_equal, "GE%d " % i + ks("hr", 4), ks("E%d" % i, 4))
+        def match(i, b=4):
+            tt(T.E[:, C * i:C * i + K * b], T.GE[:, C * i:C * i + K * b], T.hr4[:, 0:K * b], A.is_equal, "GE%d " % i + ks("hr", b), ks("E%d" % i, b))
 
         def total(i):
             scan(T.CS[:, 240 * i + 48:240 * i + 240], T.E[:, C * i:C * i + C:2], T.E[:, C * i + 1:C * i + C:2], -192.0, A.add, A.add,
                  ks("E%d" % i, 4), "CS%d" % i)
 
-        for i in range(4):
-            act(T.GE[:, C * i:C * i + C], table(i, 0, 4), F.Copy, tk, "GE%d" % i)
-        whole(4, 3, 4)
-        whole(4, 0, 3)
+        for i, b in ((0, 4), (1, 4), (2, 4), (3, 2)):
+            act(T.GE[:, C * i:C * i + K * b], table(i, 0, b), F.Copy, tk, "GE%d" % i)
+        half_d(0)
+        whole(4, 0, 1)
+        whole(4, 1, 4)
         whole(5)
         match(0)
-        total(4)
+        whole(3, 2, 4)
         match(1)
-        total(5)
+        total(4)
         match(2)
+        total(5)
         total(0)
+        match(3, 2)
         total(1)
-        match(3)
         total(2)
-        cp(T.lw[:, 48:60], T.ld[:, 16 * t:16 * t + 12], ld, "lw")
         total(3)
-        for b in range(4):
+        cp(T.lw[:, 48:60], T.ld[:, 16 * t:16 * t + 12], ld, "lw")
+        for b in (1, 2, 3, 0):
             act(T.Dc[:, 128 * b + 16:128 * b + 112], T.Dsb[:, C * b:C * b + C].indirect(LA(0, 6)), F.Copy, "Dsb%d off3" % b, "Dc%d" % b)
-        if t == 0:
-            halves(t, (2, 3))
-        act(T.Dc[:, 15::128], T.Dc[:, 111::128], F.Copy, ks("Dc", 4) + "Dcy", "Dcx")
+        for b in range(4):
+            if t == 0:
+                act(T.Y[:, C * b:C * b + C], T.xin[:, b::4], F.Copy, "xa xb", "Y%d Y%d" % (b, b + 4), scale=32.0)
+            if b == 0:
+                act(T.Dc[:, 15::128], T.Dc[:, 111::128], F.Copy, ks("Dc", 4) + "Dcy", "Dcx")
         if t == R - 1:
             act(T.PR[:, 16:112], T.ptab[:].indirect(LA(0, 6)), F.Copy, "ptab off3 PRx", "PR")
             act(T.PR[:, 15:16], T.PR[:, 111:112], F.Copy, "PR", "PRx")
         lw = T.lw
-        for e in range(2):
-            ts(lw[:, 24 * e:24 * e + 24:2], lw[:, 48:60], 7, None, A.arith_shift_right, None, "lw", "lwa%d" % e)
         tr(T.vA[:, :, 0:16], T.CS[:, 95::48], ks("CS", 6) + "CSx", "vA")
         tr(T.vB[:, :, 0:16], T.CS[:, 47:1536:48], ks("CS", 6) + "CSx", "vB")
         for e in range(2):
-            ts(lw[:, 24 * e + 1:24 * e + 24:2], lw[:, 48:60], 127, None, A.bitwise_and, None, "lw", "lwb%d" % e)
+            ts(lw[:, 24 * e:24 * e + 24:2], lw[:, 48:60], 7, None, A.arith_shift_right, None, "lw", "lwa%d" % e)
         for e in range(2):
             scan(T.vS[:, e, :], T.vA[:, e, :], T.vB[:, e, :], 0.0, A.add, A.subtract, "vA vB vAx vAy vBx vBy", "vS%d" % e)
         for e in range(2):
-            tr(T.vy[:, 32 * e:32 * e + 32], T.vS[:, :, 16 + 16 * e:32 + 16 * e], "vS0 vS1", "vy%d" % e)
+            ts(lw[:, 24 * e + 1:24 * e + 24:2], lw[:, 48:60], 127, None, A.bitwise_and, None, "lw", "lwb%d" % e)
         for e in range(2):
-            red(T.mv[:, e:e + 1], T.vy[:, 32 * e:32 * e + 32], A.max, "vy%d" % e, "mv%d" % e)
-        ts(T.rot[:, 0:1], T.mv[:, 0:1], T.mv[:, 1:2], 64.0, A.subtract, A.mult, "mv0 mv1", "rot")
+            tr(T.vy[:, 32 * e:32 * e + 32], T.vS[:, :, 16 + 16 * e:32 + 16 * e], "vS0 vS1", "vy%d" % e)
+        if t == 0:
+            ms(T.PR[:, 0:16], 0.0, "PRx")
+        scan(T.mv[:, ::-1], T.vy[:, ::-1], T.vy[:, ::-1], -1.0, A.max, A.max, "vy0 vy1", "mv")
+        ts(T.rot[:, 0:1], T.mv[:, 0:1], T.mv[:, 32:33], 64.0, A.subtract, A.mult, "mv", "rot")
+        if t < R - 1:
+            qmx("qx%d" % (t + 1), "sx%d" % (t + 1), 0, HC, T.zero[:], "zero", "qx%dz" % (t + 1))
         for e in range(2):
             ts(T.moff[:, 16 * e:16 * e + 16], lw[:, 16 * e:16 * e + 40].indirect(T.rot[:, 0:1]), 15.0, None, A.add, None,
                "lw lwa0 lwa1 lwb0 lwb1 rot", "moff%d" % e)
 
-        def win(b, h):
-            return T.Dc[:, 128 * b:128 * b + 112].indirect(T.moff[:, 12 * h:12 * h + 12])
+        cutc = (0, HC if t < R - 1 else 224, C)
 
-        def zv(b, h):
-            return T.Z[:, 4 * HC * h + b:4 * HC * (h + 1):4]
+        def win(b, h):
+            return T.Dc[:, 128 * b:128 * b + 112].indirect(T.moff[:, cutc[h] // 16:cutc[h + 1] // 16])
+
+        def plane(tile, b, h):
+            return tile[:, C * b + cutc[h]:C * b + cutc[h + 1]]
+
+        def woven(tile, b, h):
+            return tile[:, 4 * cutc[h] + b:4 * cutc[h + 1]:4]
 
         def fused(b, h):
-            tt(zv(b, h), win(b, h), xh(b, HC * h, HC * h + HC), A.add, "Dc%d Xh%d Dcx " % (b, b) + ks("moff", h + 1), "Z%d" % (4 * h + b))
+            tt(woven(T.Z, b, h), win(b, h), plane(T.Xh, b, h), A.add, "Dc%d Xh%d Dcx " % (b, b) + ks("moff", h + 1), "Z%d" % (4 * h + b))
 
         def fetch(b, h):
-            o = C * b + HC * h
-            act(T.IB[:, o:o + HC], win(b, h), F.Copy, "Dc%d Dcx " % b + ks("moff", h + 1), "IB%d%d" % (b, h))
+            act(plane(T.IB, b, h), win(b, h), F.Copy, "Dc%d Dcx " % b + ks("moff", h + 1), "IB%d%d" % (b, h))
 
         def pairs(b, h):
-            o = C * b + HC * h
-            tt(zv(b, h), T.IB[:, o:o + HC], xh(b, HC * h, HC * h + HC), A.add, "IB%d%d Xh%d" % (b, h, b), "Z%d" % (4 * h + b))
+            tt(woven(T.Z, b, h), plane(T.IB, b, h), plane(T.Xh, b, h), A.add, "IB%d%d Xh%d" % (b, h, b), "Z%d" % (4 * h + b))
 
         def product(h):
-            qmx("qz", "sz", HC * h, HC * h + HC, T.Z[:, 4 * HC * h:4 * HC * (h + 1)], ks("Z", 4 * h, 4 * h + 4), "qz%d" % h)
+            lo, hi = cutc[h], cutc[h + 1]
+            qmx("qz", "sz", lo, hi, T.Z[:, 4 * lo:4 * hi], ks("Z", 4 * h, 4 * h + 4), "qz%d" % h)
             for b in range(4):
-                mm(4 * h + b, "qw", "sw", 128 * b, "qz", "sz", "qw sw qz%d" % h, HC * h, HC * h + HC)
+                mm(4 * h + b, "qw", "sw", 128 * b, "qz", "sz", "qw sw qz%d" % h, lo, hi)
 
         def state(i):
             h, b = i // 4, i % 4
-            Yb = T.Y[:, C * b + HC * h:C * b + HC * h + HC]
-            Xb = T.X[:, 4 * HC * h + b:4 * HC * (h + 1):4]
-            tt(Yb, T["p%d" % i][:, 0:HC], Yb, A.add, "p%d Y%d" % (i, i), "Y%d" % i)
-            if i < 7:
-                act(Xb, Yb, F.Copy, "Y%d" % i, "X%d" % i, scale=2.0 ** -5)
-            return Xb, Yb
+            Yb = plane(T.Y, b, h)
+            yk = "Y%d" % i if t < R - 1 else "Y%d Y%d" % (b, b + 4)
+            tt(Yb, T["p%d" % i][:, 0:cutc[h + 1] - cutc[h]], Yb, A.add, "p%d " % i + yk, "Y%d" % i if t < R - 1 else "W%d" % i)
+            if b < 3:
+                act(woven(T.X, b, h), Yb, F.Copy, ("Y%d" if t < R - 1 else "W%d") % i, "X%d" % i, scale=2.0 ** -5)
+
+        def cast(i):
+            ts(woven(T.X, 3, i // 4), plane(T.Y, 3, i // 4), 2.0 ** -5, None, A.mult, None, ("Y%d" if t < R - 1 else "W%d") % i, "X%d" % i)
 
         for b, h in ((2, 0), (3, 0), (1, 1), (2, 1), (3, 1)):
             fetch(b, h)
-        if t == 0:
-            for b in range(4):
-                act(T.Y[:, C * b:C * b + C], T.xin[:, b::4], F.Copy, "xa xb", "Y%d Y%d" % (b, b + 4), scale=32.0)
         if t == R - 1:
             act(T.OL[:], T.PR[:].indirect(T.moff[:, 0:24]), F.Copy, "PR PRx moff0 moff1", "OL")
             dma("S", T.ol[:], T.OL[0::16, :], "OL", "")
@@ -532,36 +546,42 @@ def rank_program(g, core, T, topo):
         pairs(1, 1)
         pairs(2, 1)
         pairs(3, 1)
-        state(0)
+        if t < R - 1:
+            state(0)
         product(1)
-        for i in range(1, 7):
+        for i in range(1 if t < R - 1 else 0, 5):
             state(i)
+        cast(3)
+        state(5)
         qx, sx = "qx%d" % (t + 1), "sx%d" % (t + 1)
-        if t == R - 1:
-            Xb, Yb = state(7)
-        qmx(qx, sx, 0, HC, T.X[:, 0:4 * HC], ks("X", 4), qx + "a")
+        h = cutc[1]
         if t < R - 1:
-            mm(3, "qu", "su", 0, qx, sx, "qu %sa" % qx, 0, HC)
-        else:
-            mm(3, "qv", "sv", 0, qx, sx, "qv %sa" % qx, 0, HC)
-            dma("Y", T.oc[:, 0:4 * HC], T[qx][:, 0:HC].bitcast(dt.uint8), qx + "a", "")
-            act(T.ysb[:, 0:HC], T.p3[:, 0:HC], F.Copy, "p3", "ya")
-            dma("S", T.y[:, 0:HC], T.ysb[:, 0:HC], "ya", "")
-        if t < R - 1:
-            Xb, Yb = state(7)
-        ts(Xb, Yb, 2.0 ** -5, None, A.mult, None, "Y7", "X7")
-        if t < R - 1:
+            qmx(qx, sx, HC, C, T.X[:, 0:4 * h], ks("X", 4), qx + "a")
+            mm(3, "qu", "su", 0, qx, sx, "qu %sa" % qx, HC, C)
+            state(6)
+            state(7)
+            for bank, w in ROWS:
+                mm(bank, "qu2", "su2", w, qx, sx, "qu2 su2 %sa %sz" % (qx, qx), 0, C, True, False)
+            cast(7)
             tr(St[:, 0:12, :], T.p3[:, 0:HC], "p3", "Sa")
-        qmx(qx, sx, HC, C, T.X[:, 4 * HC:4 * C], ks("X", 4, 8), qx + "b")
-        if t < R - 1:
+            qmx(qx, sx, C, HC + C, T.X[:, 4 * h:4 * C], ks("X", 4, 8), qx + "b")
             sort_a(0)
             sort_b(0)
             sort_c(0)
 
-    mm(0, "qv", "sv", 0, qx, sx, "qv %sb" % qx, HC, C)
-    dma("Y", T.oc[:, 4 * HC:4 * C], T[qx][:, HC:C].bitcast(dt.uint8), qx + "b", "")
+    state(6)
+    state(7)
+    qmx(qx, sx, 0, h, T.X[:, 0:4 * h], ks("X", 4), "qa")
+    mm(3, "qv", "sv", 0, qx, sx, "qv qa", 0, h)
+    dma("Y", T.oc[:, 0:4 * h], T[qx][:, 0:h].bitcast(dt.uint8), "qa", "")
+    cast(7)
+    qmx(qx, sx, h, C, T.X[:, 4 * h:4 * C], ks("X", 4, 8), "qb")
+    mm(0, "qv", "sv", 0, qx, sx, "qv qb", h, C)
+    act(T.ysb[:, 0:h], T.p3[:, 0:h], F.Copy, "p3", "ya")
+    dma("Y", T.oc[:, 4 * h:4 * C], T[qx][:, h:C].bitcast(dt.uint8), "qb", "")
     for k in range(4):
-        dma("S", T.osc[4 * k:4 * k + 4, :], T[sx][32 * k:32 * k + 4, :], "%sa %sb" % (qx, qx), "")
-    cp(T.ysb[:, HC:C], T.p0[:, 0:HC], "p0", "yb")
-    dma("Y", T.y[:, HC:C], T.ysb[:, HC:C], "yb", "")
+        dma("Y", T.osc[4 * k:4 * k + 4, :], T[sx][32 * k:32 * k + 4, 0:C], "qa qb", "")
+    dma("S", T.y[:, 0:h], T.ysb[:, 0:h], "ya", "")
+    cp(T.ysb[:, h:C], T.p0[:, 0:C - h], "p0", "yb")
+    dma("S", T.y[:, h:C], T.ysb[:, h:C], "yb", "")
     need("G", [(s, count[s]) for s in count])

from concourse.mybir import dt, AluOpType, AxisListType, ActivationFunctionType

A = AluOpType
F = ActivationFunctionType
C, K, R, N = 384, 96, 3, 8
HC = C // 2
STEP = [1, 2, 3]
H = 2.0 ** 88
B = 2.0 ** 97
PAD = 48
WIN = 304
ROWS = ((0, 0), (1, 128), (4, 128))
CODE = "float8_e4m3fn_x4"

SCRATCH = {}
for _d, _l in (
        ("bfloat16", dict(xin=4 * C, uin=512, vin=512, X=4 * C, Z=4 * C, Y=4 * C, Xh=4 * C, IB=4 * C, Dsb=4 * C, Dc=512,
                          eone=528, ebf=528, c16=C, mask=C, keep=C, mbig=C, horn=72, sg=72, aH=72, sh=32 * R, lh=32 * R, AX=C, BX=C,
                          Arow=PAD + C, Am=PAD + C, Brow=PAD + C, FL=7 * C, ZB=16 * HC, JS=16 * C, gt=C, sgn=HC, ge=16 + C, cap=16 + C, cnt=16 + C, CH=C,
                          SC=2 * WIN, G8=112, B8=112, hv=K, Hm=R * (PAD + C), T2=784, hr4=C, E=24 * K, GE=16 * K, B1=K, G1=K, zero=2 * C, CS=1584)),
        ("float32", dict(cf=64, lc=16, lb=8, D0=16, D1=16, E0=8, E1=8, MM=32, cS=16, LL=48, LU=48, LN=48, kpN=24, cb=72, TT=112, tz=2, TS=32,
                         cP=2, hp=24, SP=48, vy=64, mv=64, OL=C, ysb=C, ptab=C, PR=112)),
        ("uint16", dict(cu=48, rot=2, moff=32, sa=8 * R, la=32 * R, sc=16 * R, ld=16 * R)),
        ("int32", dict(li=4, lw=64)),
        (CODE, dict(qu=128, qu2=256, qu3=128, qv=128, qw=512, qe=512, qz=C, qx0=HC + C, qx1=HC + C, qx2=HC + C, qx3=C, lq0=C, lq1=C, lq2=C)),
        ("uint8", dict(su=128, su2=256, su3=128, sv=128, sw=512, se=512, sz=C, sx0=HC + C, sx1=HC + C, sx2=HC + C, sx3=C, ls0=C, ls1=C, ls2=C))):
    for _n in _l:
        SCRATCH[_n] = ("sbuf", [128, _l[_n]], _d)
SCRATCH["St"] = ("sbuf", [128, 24, 16], "float32")
SCRATCH["RR"] = ("sbuf", [128, 6, 24], "float32")
for _n, _d in (("vA", "bfloat16"), ("vB", "bfloat16"), ("vS", "float32")):
    SCRATCH[_n] = ("sbuf", [128, 2, 48], _d)
for _b in range(8):
    SCRATCH["p%d" % _b] = ("psum", [128, 512], "float32")

SEMAPHORES = ["cV", "cS", "cT", "cG", "sent"] + ["d%d" % i for i in range(16)] + [a + str(t) for a in ("aq", "ah", "aa", "ab") for t in range(R)]


def rank_program(g, core, T, topo):
    rank = T.rank_of(core)
    if rank is None:
        return
    eng = {"V": g.vector, "S": g.scalar, "T": g.tensor, "G": g, "Y": g.sync}
    csem = {"V": "cV", "S": "cS", "T": "cT", "G": "cG"}
    count = {}
    waited = {q: {} for q in eng}
    lastw, readers = {}, {}
    ndma = [0]

    def need(q, toks):
        best = {}
        for (s, v) in toks:
            if v > best.get(s, 0):
                best[s] = v
        for s in best:
            if waited[q].get(s, 0) < best[s]:
                eng[q].wait_ge(T.sem[s], best[s])
                waited[q][s] = best[s]

    def deps(q, Rd, W):
        toks = []
        for k in Rd.split():
            toks += lastw.get(k, [])
            if k[0] == "p" and k[1:].isdigit():
                toks += [x for x in readers.get(k, []) if x[0] != csem.get(q)]
        for k in W.split():
            toks += lastw.get(k, []) + readers.get(k, [])
        need(q, toks)

    def done(tok, Rd, W):
        for k in Rd.split():
            readers.setdefault(k, []).append(tok)
        for k in W.split():
            lastw[k] = [tok]
            readers[k] = []

    def op(q, fn, Rd, W):
        deps(q, Rd, W)
        s = csem[q]
        count[s] = count.get(s, 0) + 1
        fn().then_inc(T.sem[s], 1)
        done((s, count[s]), Rd, W)

    def dma(q, out, in_, Rd, W):
        deps(q, Rd, W)
        sem = "d%d" % ndma[0]
        ndma[0] += 1
        count[sem] = 16
        eng[q].dma_start(out, in_).then_inc(T.sem[sem], 16)
        done((sem, 16), Rd, W)

    V, S, PE = g.vector, g.scalar, g.tensor

    def ks(p, *r):
        return " ".join(p + str(i) for i in range(*r)) + " "

    def ts(out, in0, s1, s2, o0, o1, Rd, W):
        if o1 is None:
            op("V", lambda: V.tensor_scalar(out, in0, s1, None, o0), Rd, W)
        else:
            op("V", lambda: V.tensor_scalar(out, in0, s1, s2, o0, o1), Rd, W)

    def tt(out, a, b, o, Rd, W):
        op("V", lambda: V.tensor_tensor(out, a, b, o), Rd, W)

    def cp(out, a, Rd, W):
        op("V", lambda: V.tensor_copy(out, a), Rd, W)

    def scan(out, d0, d1, init, o0, o1, Rd, W):
        op("V", lambda: V.tensor_tensor_scan(out, d0, d1, init, o0, o1), Rd, W)

    def tr(out, a, Rd, W):
        op("V", lambda: V.transpose(out, a), Rd, W)

    def red(out, a, o, Rd, W):
        op("V", lambda: V.tensor_reduce(out, a, AxisListType.X, o), Rd, W)

    def ms(ap, c, W):
        op("V", lambda: V.memset(ap, c), "", W)

    def act(out, a, f, Rd, W, **kw):
        op("S", lambda: S.activation(out, a, f, **kw), Rd, W)

    def const(out, n, c, W):
        act(out, T.eone[:, 0:n], F.Copy, "eone", W, scale=float(c))

    def qmx(qn, sn, lo, hi, a, Rd, W):
        op("V", lambda: V.quantize_mx(T[qn][:, lo:hi], T[sn][:, lo:hi], a), Rd, W)

    def mm(bank, wq, wsn, wlo, mq, msn, Rd, lo=0, hi=C, start=True, stop=True):
        op("T", lambda: PE.matmul_mx(T["p%d" % bank][:, 0:hi - lo], T[wq][:, wlo:wlo + 128], T[wsn][:, wlo:wlo + 128],
                                     T[mq][:, lo:hi], T[msn][:, lo:hi], start, stop), Rd, "p%d" % bank)

    def iota(out, pat, base, W):
        op("G", lambda: g.iota(out, pat, base, 0, allow_small_or_imprecise_dtypes=True), "", W)

    def send(t, out, in_, rsem, Rd):
        dst = T.cores[(rank - STEP[t]) % N]
        rid, pid, _ = topo.addr(dst)
        deps("G", Rd, "")
        g.remote_dma(out, in_, T.sem[rsem], T.sem.sent, pid, rid, topo.mask(core, dst))
        count["sent"] = count.get("sent", 0) + len(topo.engines(core, dst))

    for t in range(R):
        n = len(topo.engines(T.cores[(rank + STEP[t]) % N], core))
        for key, sem, m in (("lq", "aq", 2 * n), ("lh", "ah", n), ("la", "aa", n), ("ld", "ab", n)):
            lastw[key + str(t)] = [(sem + str(t), m)]
            count[sem + str(t)] = m

    dma("S", T.uin[:], T.u[:], "", "uin")
    dma("Y", T.xin[:, 0:768], T.x[:, 0:768], "", "xa")
    dma("Y", T.xin[:, 768:1536], T.x[:, 768:1536], "", "xb")

    cf, cu, lc, lb = T.cf, T.cu, T.lc, T.lb
    St, MM, FL, JS, cS = T.St, T.MM, T.FL, T.JS, T.cS
    ZW = lambda a, b, s=1: T.ZB[:, HC * a + HC - 1:HC * b:HC * s]
    iota(cf[:, 0:16], [[16, 2], [32, 4], [0, 2]], 0, "cf0")
    iota(cf[:, 16:24], [[16, 8]], 0, "cf1")
    op("G", lambda: g.iota(T.li[:, 0:1], [[0, 1]], 0, 1), "", "li0")
    ms(T.eone[:], 1.0, "eone")
    iota(cf[:, 24:48], [[1, 24]], 0, "cf2")
    iota(T.cb[:, 0:35], [[4, 7], [-1, 5]], 3, "cb")
    op("G", lambda: g.affine_select(T.ebf[:], T.eone[:], [[-1, 528]], A.is_equal, 0.0, 3, 4), "eone", "ebf")
    iota(T.c16[:], [[0, 24], [1, 16]], 0, "c16")
    iota(T.hp[:], [[0, 12], [128, 2]], 0, "hp")

    ms(T.ge[:, 15:16], -96.0, "gex")
    ms(T.cap[:, 15:16], 128.0, "capx")
    ms(T.Dc[:], 0.0, "Dcy " + ks("Dc", 4))
    ms(T.vA[:, :, 16:48], 0.0, "vAx vAy")
    ms(T.vB[:, :, 16:33], 0.0, "vBx")
    ms(T.vB[:, :, 33:48], 2.0 ** -6, "vBy")
    cp(cu[:, 0:24], cf[:, 0:24], "cf0 cf1", "cuU")
    ts(T.li[:, 1:2], T.li[:, 0:1], 15, None, A.bitwise_and, None, "li0", "li1")
    ms(T.CS[:, 47::48], -192.0, "CSx " + ks("CS", 6))
    cp(lb[:, 0:1], T.li[:, 1:2], "li1", "lane")
    cp(cu[:, 24:48], cf[:, 24:48], "cf2", "cuA")
    ms(T.cb[:, 4:30:5], 40.0, "cb")
    ms(T.cb[:, 30:32], 40.0, "cb2")
    const(T.D0[:, 0::2], 8, -B, "D0x")
    const(T.LL[:, 16:48], 32, -B, "LLx")
    const(T.LU[:, 16:48], 32, B, "LUx")
    const(T.LN[:, 16:48], 32, 0.0, "LNx")
    const(T.TT[:, 96:97], 1, -95.5 * H, "TTx")
    const(T.kpN[:, 0:4], 4, 1.0, "kpN0")
    const(T.kpN[:, 4:5], 1, 2.0, "kpN1")
    const(T.kpN[:, 5:24], 19, 1.0, "kpN2")
    for i in range(3):
        const(T.horn[:, i::3], 24, 2.0 if i else 0.0, "horn%d" % i)
    for n in ("Arow", "Am", "Brow"):
        const(T[n][:, 0:PAD], PAD, 0.0, n + "x")

    def pick_u(n, a, b):
        cp(T["qu" + n][:].bitcast(dt.uint32), T.qu[:].bitcast(dt.uint32).indirect(cu[:, a:b]), "qu cuU", "qu" + n)
        act(T["su" + n][:], T.su[:].indirect(cu[:, a:b]), F.Copy, "qu cuU", "su" + n)

    qmx("qu", "su", 0, 128, T.uin[:], "uin", "qu")
    qmx("qx0", "sx0", HC, C, T.xin[:, 0:4 * HC], "xa", "qx0a")
    mm(3, "qu", "su", 0, "qx0", "sx0", "qu qx0a", HC, C)
    pick_u("2", 0, 16)
    ts(lc[:, 0:6], cf[:, 16:22], lb[:, 0:1], 0.5, A.add, A.add, "cf1 lane", "lc0")
    ts(T.cnt[:, 0:6], cf[:, 16:22], lb[:, 0:1], 0.5, A.add, A.add, "cf1 lane", "lc2")
    tr(St[:, 0:12, :], T.p3[:, 0:HC], "p3", "Sa")
    qmx("qx0", "sx0", C, HC + C, T.xin[:, 4 * HC:4 * C], "xb", "qx0b")
    dma("Y", T.qw[:].bitcast(dt.uint8), T.wc[:], "xa xb", "qw")
    dma("Y", T.sw[:], T.ws[:], "", "sw")
    dma("Y", T.vin[:], T.v[:], "", "vin")

    def abc(h):
        return [St[:, 12 * h + 4 * i:12 * h + 4 * i + 4, 0] for i in range(3)]

    def odd(t, h):
        return t[:, 8 * h + 1:8 * h + 8:2]

    def sort_a(h):
        a, b, c = abc(h)
        k, s = "S" + "ab"[h], str(h)
        tt(odd(T.D0, h), a, b, A.max, k, "mx" + s)
        tt(odd(T.D1, h), a, b, A.min, k, "mn" + s)
        cp(T.D1[:, 8 * h:8 * h + 8:2], c, k, "cc" + s)

    def sort_b(h):
        s = str(h)
        scan(MM[:, 8 * h:8 * h + 8], T.D0[:, 8 * h:8 * h + 8], T.D1[:, 8 * h:8 * h + 8], 0.0, A.min, A.max,
             "D0x mx%s mn%s cc%s" % (s, s, s), "M" + s)

    def sort_c(h):
        c = abc(h)[2]
        k, s = "S" + "ab"[h], str(h)
        tt(T.E0[:, 4 * h:4 * h + 4], odd(T.D0, h), c, A.max, k + " mx" + s, "hi" + s)
        tt(T.E1[:, 4 * h:4 * h + 4], odd(T.D1, h), c, A.min, k + " mn" + s, "lo" + s)

    def second(*ns):
        for n in ns:
            ts(MM[:, 2 * n + 17:2 * n + 18], ZW(n, n + 1), T.E0[:, n:n + 1], T.E1[:, n:n + 1], A.min, A.max,
               "hi%d lo%d z%d" % (n // 4, n // 4, n), "M%d" % (8 + n))

    def mk(n):
        return " M%d" % (n // 4 if n < 8 else n)

    def spass(n):
        bank = "p4" if n % 2 else "p0"
        act(JS[:, C * n:C * n + C], T[bank][:, 0:C], F.Sign, bank + mk(n), "JS%d cS%d" % (n, n),
            bias=MM[:, 2 * n + 1:2 * n + 2], scale=-1.0, accum_out=cS[:, n:n + 1])

    def vpass(n):
        m = n // 2 - 1
        ts(FL[:, C * m:C * m + C], T.p1[:, 0:C], MM[:, 2 * n + 1:2 * n + 2], H, A.is_gt, A.mult, "p1" + mk(n), "FL%d" % m)

    def vsum(n):
        m = n // 2 - 1
        scan(T.ZB[:, HC * n:HC * n + HC], FL[:, C * m:C * m + HC], FL[:, C * m + HC:C * m + C], -95.5 * H, A.add, A.add, "FL%d" % m, "z%d" % n)

    def zs(*r):
        ts(ZW(*r), cS[:, r[0]:r[1]:r[2]], 192.5, -H, A.subtract, A.mult, ks("cS", *r), ks("z", *r))

    def xh(b, lo, hi):
        return T.Xh[:, C * b + lo:C * b + hi]

    def halves(t, bs):
        for b in bs:
            if t == 0:
                act(xh(b, 0, C), T.xin[:, b::4], F.Copy, "xa xb", "Xh%d" % b, scale=0.5)
            else:
                act(xh(b, 0, C), T.Y[:, C * b:C * b + C], F.Copy, "Y%d Y%d" % (b, b + 4), "Xh%d" % b, scale=2.0 ** -6)

    sort_a(0)
    qmx("qe", "se", 0, 128, T.ebf[:, 3:515], "ebf", "qe0")
    sort_b(0)
    sort_c(0)
    pick_u("3", 16, 24)

    for t in range(R):
        qx, sx, lq, ls, la, lh, ld, sh = ("%s%d" % (s, t) for s in ("qx", "sx", "lq", "ls", "la", "lh", "ld", "sh"))
        SA = lambda a, b: T.sa[:, 8 * t + a:8 * t + b]
        LA = lambda a, b: T.la[:, 32 * t + a:32 * t + b]
        SH, LH = T.sh[:, 32 * t:32 * t + 24], T.lh[:, 32 * t:32 * t + 24]
        qk = "%sa %sb" % (qx, qx)
        for bank, w in ROWS:
            mm(bank, "qu2", "su2", w, qx, sx, "qu2 su2 " + qk, C if t else HC, HC + C, t == 0, True)
            if bank == 0:
                mm(7, "qu", "su", 0, qx, sx, "qu " + qk, C, HC + C)
        mm(2, "qu3", "su3", 0, qx, sx, "qu3 su3 " + qk, HC, HC + C)
        mm(3, "qu3", "su3", 0, qx, sx, "qu3 su3 " + qk, HC, HC + C)
        send(t, T[lq][:].bitcast(dt.uint8), T[qx][:, HC:HC + C].bitcast(dt.uint8), "aq%d" % t, qk)
        send(t, T[ls][:], T[sx][:, HC:HC + C], "aq%d" % t, qk)
        if t == 0:
            iota(T.zero[:], [[0, 2 * C]], 0, "zero")
        if t == 1:
            iota(T.ptab[:], [[1, C]], 0, "ptab")
        for n in (0, 2, 1):
            spass(n)
        tr(St[:, 12:24, :], T.p7[:, 0:HC], "p7", "Sb")
        signs = lambda: ts(T.sg[:], St[:, :, 1:4], 0.0, None, A.is_gt, None, "Sa Sb", "sg")
        if t == 0:
            ts(T.mask[:], T.c16[:], lb[:, 0:1], None, A.is_equal, None, "c16 lane", "mask")
            sort_a(1)
            vpass(3)
            sort_b(1)
            sort_c(1)
            vsum(3)
            signs()
        else:
            vpass(3)
            sort_a(1)
            vsum(3)
            signs()
            sort_b(1)
            sort_c(1)
        spass(4)
        spass(6)
        if t == 0:
            vpass(5)
        second(3)
        scan(T.aH[:], T.horn[:], T.sg[:], 0.0, A.mult, A.add, ks("horn", 3) + "sg", "aH")
        if t > 0:
            vpass(5)
        spass(11)
        zs(0, 3, 1)
        vpass(7)
        second(0, 2, 1)
        spass(8)
        spass(10)
        vsum(5)
        vsum(7)
        zs(4, 7, 2)
        vpass(9)
        second(5, 7, 4, 6)
        spass(12)
        spass(14)
        vpass(13)
        vsum(9)
        vpass(15)
        zs(11, 12, 1)
        vsum(13)
        vsum(15)
        zs(8, 16, 2)
        act(SH, T.aH[:, 2::3], F.Identity, "aH", sh, bias=128.0)
        send(t, LH, SH, "ah%d" % t, sh)
        halves(t, (0,))
        act(T.AX[:], SH.indirect(cu[:, 24:48]), F.Copy, sh + " cuA", "AX")
        halves(t, (1, 2))
        for b in (1, 2, 3, 0) if t else ():
            mm(4 + b, "qe", "se", 128 * b, lq, ls, "qe%d %s" % (b, lq))
        zk = ks("z", 16)
        if t == 0:
            tr(T.cb[:, 40:72], T.cb[:, 0:32], "cb cb2", "cbt")
            ts(T.mbig[:], T.mask[:], 256.0, None, A.mult, None, "mask", "mbig")
        tt(T.LL[:, 0:16], MM[:, 1::2], ZW(0, 16), A.min, "M0 M1 " + ks("M", 8, 16) + zk, "LL")
        tt(T.LU[:, 0:16], MM[:, 1::2], ZW(0, 16), A.max, "M0 M1 " + ks("M", 8, 16) + zk, "LU")
        ts(T.LN[:, 0:16], ZW(0, 16), 0.0, H, A.is_lt, A.mult, zk, "LN")
        if t == 0:
            ts(T.vA[:, :, 32], T.cb[:, 40:42], -2.0 ** -6, None, A.mult, None, "cbt", "vAy")
        for e in range(2):
            scan(T.RR[:, e, :], T.LL[:, e::2], T.LL[:, e::2], -B, A.max, A.max, "LL LLx", "RR%d" % e)
        for e in range(2):
            scan(T.RR[:, 2 + e, :], T.LU[:, e::2], T.LU[:, e::2], B, A.min, A.min, "LU LUx", "RR%d" % (2 + e))
        for e in range(2):
            scan(T.RR[:, 4 + e, :], T.kpN[:], T.LN[:, e::2], 0.0, A.mult, A.add, "LN LNx " + ks("kpN", 3), "RR%d" % (4 + e))
        if t == 0:
            qmx("qe", "se", 256, 384, T.ebf[:, 1:513], "ebf", "qe2")
        tr(T.TT[:, 0:96], T.RR[:, :, 8:24], ks("RR", 6), "TT")
        if t == 0:
            qmx("qe", "se", 384, 512, T.ebf[:, 0:512], "ebf", "qe3")
        red(T.tz[:, 0:1], T.TT[:, 64:97], A.add, "TT TTx", "tz")
        tr(T.Arow[:, PAD:PAD + C], T.AX[:], "AX", "Arow")
        scan(T.TS[:], T.TT[:, 0:32], T.TT[:, 32:64], T.tz[:, 0:1], A.max, A.min, "TT tz", "TS")
        if t == 0:
            qmx("qe", "se", 128, 256, T.ebf[:, 2:514], "ebf", "qe1")
            for b in (1, 2, 3, 0):
                mm(4 + b, "qe", "se", 128 * b, lq, ls, "qe%d %s" % (b, lq))
            act(T.keep[:], T.mask[:], F.Identity, "mask", "keep", scale=-1.0, bias=1.0)
        cut = T.TS[:, 31:32]
        act(T.sgn[:, 0:HC], T.p3[:, 0:HC], F.Sign, "p3 TS", "sgn", bias=cut, scale=-1.0)
        act(T.ge[:, 16:16 + HC], T.sgn[:, 0:HC], F.Sign, "sgn", "ge0", bias=1.0, scale=-1.0)
        ts(T.gt[:], T.p2[:, 0:C], cut, None, A.is_gt, None, "p2 TS", "gt")
        ts(T.ge[:, 16 + HC:16 + C], T.p2[:, HC:C], cut, None, A.is_ge, None, "p2 TS", "ge1")
        scan(T.cap[:, 16:16 + C], T.eone[:, 0:C], T.gt[:], 0.0, A.mult, A.add, "eone gt", "cap")
        above = T.cap[:, 15 + C:16 + C]
        scan(T.Am[:, PAD:PAD + C], T.Arow[:, PAD:PAD + C], T.mask[:], 0.0, A.max, A.mult, "Arow mask", "Am")
        scan(T.cnt[:, 15:16 + C], T.ge[:, 15:16 + C], T.cap[:, 15:16 + C], above, A.add, A.min, "ge0 ge1 gex cap capx", "cnt")
        ts(lc[:, 8:10], lc[:, 0:2], above, -96.0, A.add, A.add, "lc0 cap", "lc1")
        act(T.BX[:], LH.indirect(cu[:, 24:48]), F.Copy, lh + " cuA", "BX")
        o = (PAD + C) * t
        Hp, Hm = T.Hm[:, o:o + PAD + C], lambda a, b, s=1, o=o + PAD: T.Hm[:, o + a:o + b:s]
        ms(Hp, 0.0, "Hm%d" % t)
        for s in range(2):
            act(JS[:, C * s:C * s + 320], T.cnt[:, 16:336], F.Sign, "cnt lc1", "JS%d cP%d" % (s, s),
                bias=lc[:, 8 + s:9 + s], scale=-1.0, accum_out=T.cP[:, s:s + 1])
        for s in range(2, 6):
            ts(FL[:, C * s:C * s + WIN], T.cnt[:, 16 * s + 16:16 * s + 16 + WIN], T.cnt[:, 15:16], T.cnt[:, s:s + 1], A.subtract, A.is_le, "cnt lc2", "FL%d" % s)
        W2 = WIN // 2
        for s in range(2, 6):
            o = C * s
            scan(T.SC[:, W2 * (s - 2):W2 * (s - 1)], FL[:, o:o + W2], FL[:, o + W2:o + WIN], 16.0 * s - 200.0, A.add, A.add, "FL%d" % s, "SC%d" % s)
        ts(SA(0, 2), T.cP[:], 0.5, 160.0 + PAD, A.mult, A.add, "cP0 cP1", "poa%d" % t)
        ts(SA(6, 7), T.cP[:, 0:1], 0.5, 160.0 + PAD, A.mult, A.add, "cP0", "poc%d" % t)
        ts(SA(2, 6), T.SC[:, W2 - 1::W2], 200.0 + PAD, None, A.add, None, ks("SC", 2, 6), "pob%d" % t)
        pk = " poa%d pob%d poc%d" % (t, t, t)
        send(t, LA(18, 25), SA(0, 7), "aa%d" % t, pk)

        def next_signs(out, row, off, Rd, W):
            act(out, row.indirect(off), F.Identity, Rd, W, scale=0.125, bias=-15.0)

        def half_d(b):
            act(T.Dsb[:, C * b:C * b + C], T["p%d" % (4 + b)][:, 0:C], F.Copy, "p%d" % (4 + b), "Dsb%d" % b, scale=0.5)

        halves(t, (3,))
        next_signs(T.G8[:], T.Arow[:], SA(0, 7), "Arow Arowx" + pk, "G8")
        tr(T.Brow[:, PAD:PAD + C], T.BX[:], "BX", "Brow")
        cp(T.G1[:], T.Am[:].indirect(SA(0, 6)), "Am Amx" + pk, "G1")
        scan(T.CH[:], T.mbig[:], T.cnt[:, 16:16 + C], 0.0, A.add, A.min, "mbig cnt", "CH")
        tt(T.hv[:], T.G1[:], T.G8[:, 1:K + 1], A.mult, "G1 G8", "hv")
        half_d(1)
        half_d(2)
        ts(T.SP[:, 24:48], T.CH[:, 15::16], T.cnt[:, 15:16], None, A.subtract, None, "CH cnt", "SQ")
        if t == R - 1:
            qmx("qv", "sv", 0, 128, T.vin[:], "vin", "qv")
        cp(Hp.indirect(SA(0, 6)), T.hv[:], "hv" + pk, "Hm%d" % t)
        scan(T.SP[:, 0:24], T.hp[:], T.SP[:, 24:48], 0.0, A.mult, A.add, "hp SQ", "SP")
        next_signs(T.B8[:], T.Brow[:], LA(18, 25), "Brow Browx " + la, "B8")
        act(T.B1[:], T.Brow[:].indirect(LA(18, 24)), F.Copy, "Brow Browx " + la, "B1")
        half_d(3)
        scan(T.T2[:, 0:C], T.keep[:], Hm(0, C), 0.0, A.mult, A.add, "keep Hm%d" % t, "T2a")
        cp(T.sc[:, 16 * t:16 * t + 12], T.SP[:, 1:24:2], "SP", "sc%d" % t)
        send(t, T.ld[:, 16 * t:16 * t + 12], T.sc[:, 16 * t:16 * t + 12], "ab%d" % t, "sc%d" % t)
        for j in (1, 2, 3):
            ts(LA(18 - 6 * j, 24 - 6 * j), LA(18, 24), -16.0 * j, None, A.add, None, la, "off%d" % j)
        scan(T.T2[:, C:2 * C], T.keep[:], Hm(0, C), T.T2[:, C - 1:C], A.mult, A.add, "keep T2a Hm%d" % t, "T2b")
        for i in range(4):
            tt(T.hr4[:, K * i:K * i + K], T.B1[:], T.B8[:, 1:K + 1], A.mult, "B1 B8", "hr%d" % i)

        def table(i, a, b):
            return T.T2[:, 336 - 64 * i:2 * C].indirect(LA(6 * a, 6 * b))

        tk = "T2a T2b off1 off2 off3 " + la

        def whole(i, a=0, b=4):
            tt(T.E[:, C * i + K * a:C * i + K * b], table(i, a, b), T.hr4[:, K * a:K * b], A.is_equal, tk + " " + ks("hr", a, b),
               " ".join("E%d%d" % (i, m) for m in range(a, b)))

        def match(i, b=4):
            tt(T.E[:, C * i:C * i + K * b], T.GE[:, C * i:C * i + K * b], T.hr4[:, 0:K * b], A.is_equal, "GE%d " % i + ks("hr", b), ks("E%d" % i, b))

        def total(i):
            scan(T.CS[:, 240 * i + 48:240 * i + 240], T.E[:, C * i:C * i + C:2], T.E[:, C * i + 1:C * i + C:2], -192.0, A.add, A.add,
                 ks("E%d" % i, 4), "CS%d" % i)

        for i, b in ((0, 4), (1, 4), (2, 4), (3, 2)):
            act(T.GE[:, C * i:C * i + K * b], table(i, 0, b), F.Copy, tk, "GE%d" % i)
        half_d(0)
        whole(4, 0, 1)
        whole(4, 1, 4)
        whole(5)
        match(0)
        whole(3, 2, 4)
        match(1)
        total(4)
        match(2)
        total(5)
        total(0)
        match(3, 2)
        total(1)
        total(2)
        total(3)
        cp(T.lw[:, 48:60], T.ld[:, 16 * t:16 * t + 12], ld, "lw")
        for b in (1, 2, 3, 0):
            act(T.Dc[:, 128 * b + 16:128 * b + 112], T.Dsb[:, C * b:C * b + C].indirect(LA(0, 6)), F.Copy, "Dsb%d off3" % b, "Dc%d" % b)
        for b in range(4):
            if t == 0:
                act(T.Y[:, C * b:C * b + C], T.xin[:, b::4], F.Copy, "xa xb", "Y%d Y%d" % (b, b + 4), scale=32.0)
            if b == 0:
                act(T.Dc[:, 15::128], T.Dc[:, 111::128], F.Copy, ks("Dc", 4) + "Dcy", "Dcx")
        if t == R - 1:
            act(T.PR[:, 16:112], T.ptab[:].indirect(LA(0, 6)), F.Copy, "ptab off3 PRx", "PR")
            act(T.PR[:, 15:16], T.PR[:, 111:112], F.Copy, "PR", "PRx")
        lw = T.lw
        tr(T.vA[:, :, 0:16], T.CS[:, 95::48], ks("CS", 6) + "CSx", "vA")
        tr(T.vB[:, :, 0:16], T.CS[:, 47:1536:48], ks("CS", 6) + "CSx", "vB")
        for e in range(2):
            ts(lw[:, 24 * e:24 * e + 24:2], lw[:, 48:60], 7, None, A.arith_shift_right, None, "lw", "lwa%d" % e)
        for e in range(2):
            scan(T.vS[:, e, :], T.vA[:, e, :], T.vB[:, e, :], 0.0, A.add, A.subtract, "vA vB vAx vAy vBx vBy", "vS%d" % e)
        for e in range(2):
            ts(lw[:, 24 * e + 1:24 * e + 24:2], lw[:, 48:60], 127, None, A.bitwise_and, None, "lw", "lwb%d" % e)
        for e in range(2):
            tr(T.vy[:, 32 * e:32 * e + 32], T.vS[:, :, 16 + 16 * e:32 + 16 * e], "vS0 vS1", "vy%d" % e)
        if t == 0:
            ms(T.PR[:, 0:16], 0.0, "PRx")
        scan(T.mv[:, ::-1], T.vy[:, ::-1], T.vy[:, ::-1], -1.0, A.max, A.max, "vy0 vy1", "mv")
        ts(T.rot[:, 0:1], T.mv[:, 0:1], T.mv[:, 32:33], 64.0, A.subtract, A.mult, "mv", "rot")
        if t < R - 1:
            qmx("qx%d" % (t + 1), "sx%d" % (t + 1), 0, HC, T.zero[:], "zero", "qx%dz" % (t + 1))
        for e in range(2):
            ts(T.moff[:, 16 * e:16 * e + 16], lw[:, 16 * e:16 * e + 40].indirect(T.rot[:, 0:1]), 15.0, None, A.add, None,
               "lw lwa0 lwa1 lwb0 lwb1 rot", "moff%d" % e)

        cutc = (0, HC if t < R - 1 else 224, C)

        def win(b, h):
            return T.Dc[:, 128 * b:128 * b + 112].indirect(T.moff[:, cutc[h] // 16:cutc[h + 1] // 16])

        def plane(tile, b, h):
            return tile[:, C * b + cutc[h]:C * b + cutc[h + 1]]

        def woven(tile, b, h):
            return tile[:, 4 * cutc[h] + b:4 * cutc[h + 1]:4]

        def fused(b, h):
            tt(woven(T.Z, b, h), win(b, h), plane(T.Xh, b, h), A.add, "Dc%d Xh%d Dcx " % (b, b) + ks("moff", h + 1), "Z%d" % (4 * h + b))

        def fetch(b, h):
            act(plane(T.IB, b, h), win(b, h), F.Copy, "Dc%d Dcx " % b + ks("moff", h + 1), "IB%d%d" % (b, h))

        def pairs(b, h):
            tt(woven(T.Z, b, h), plane(T.IB, b, h), plane(T.Xh, b, h), A.add, "IB%d%d Xh%d" % (b, h, b), "Z%d" % (4 * h + b))

        def product(h):
            lo, hi = cutc[h], cutc[h + 1]
            qmx("qz", "sz", lo, hi, T.Z[:, 4 * lo:4 * hi], ks("Z", 4 * h, 4 * h + 4), "qz%d" % h)
            for b in range(4):
                mm(4 * h + b, "qw", "sw", 128 * b, "qz", "sz", "qw sw qz%d" % h, lo, hi)

        def state(i):
            h, b = i // 4, i % 4
            Yb = plane(T.Y, b, h)
            yk = "Y%d" % i if t < R - 1 else "Y%d Y%d" % (b, b + 4)
            tt(Yb, T["p%d" % i][:, 0:cutc[h + 1] - cutc[h]], Yb, A.add, "p%d " % i + yk, "Y%d" % i if t < R - 1 else "W%d" % i)
            if b < 3:
                act(woven(T.X, b, h), Yb, F.Copy, ("Y%d" if t < R - 1 else "W%d") % i, "X%d" % i, scale=2.0 ** -5)

        def cast(i):
            ts(woven(T.X, 3, i // 4), plane(T.Y, 3, i // 4), 2.0 ** -5, None, A.mult, None, ("Y%d" if t < R - 1 else "W%d") % i, "X%d" % i)

        for b, h in ((2, 0), (3, 0), (1, 1), (2, 1), (3, 1)):
            fetch(b, h)
        if t == R - 1:
            act(T.OL[:], T.PR[:].indirect(T.moff[:, 0:24]), F.Copy, "PR PRx moff0 moff1", "OL")
            dma("S", T.ol[:], T.OL[0::16, :], "OL", "")
        fused(0, 0)
        fused(1, 0)
        pairs(2, 0)
        pairs(3, 0)
        fused(0, 1)
        product(0)
        pairs(1, 1)
        pairs(2, 1)
        pairs(3, 1)
        if t < R - 1:
            state(0)
        product(1)
        for i in range(1 if t < R - 1 else 0, 5):
            state(i)
        cast(3)
        state(5)
        qx, sx = "qx%d" % (t + 1), "sx%d" % (t + 1)
        h = cutc[1]
        if t < R - 1:
            qmx(qx, sx, HC, C, T.X[:, 0:4 * h], ks("X", 4), qx + "a")
            mm(3, "qu", "su", 0, qx, sx, "qu %sa" % qx, HC, C)
            state(6)
            state(7)
            for bank, w in ROWS:
                mm(bank, "qu2", "su2", w, qx, sx, "qu2 su2 %sa %sz" % (qx, qx), 0, C, True, False)
            cast(7)
            tr(St[:, 0:12, :], T.p3[:, 0:HC], "p3", "Sa")
            qmx(qx, sx, C, HC + C, T.X[:, 4 * h:4 * C], ks("X", 4, 8), qx + "b")
            sort_a(0)
            sort_b(0)
            sort_c(0)

    state(6)
    state(7)
    qmx(qx, sx, 0, h, T.X[:, 0:4 * h], ks("X", 4), "qa")
    mm(3, "qv", "sv", 0, qx, sx, "qv qa", 0, h)
    dma("Y", T.oc[:, 0:4 * h], T[qx][:, 0:h].bitcast(dt.uint8), "qa", "")
    cast(7)
    qmx(qx, sx, h, C, T.X[:, 4 * h:4 * C], ks("X", 4, 8), "qb")
    mm(0, "qv", "sv", 0, qx, sx, "qv qb", h, C)
    act(T.ysb[:, 0:h], T.p3[:, 0:h], F.Copy, "p3", "ya")
    dma("Y", T.oc[:, 4 * h:4 * C], T[qx][:, h:C].bitcast(dt.uint8), "qb", "")
    for k in range(4):
        dma("Y", T.osc[4 * k:4 * k + 4, :], T[sx][32 * k:32 * k + 4, 0:C], "qa qb", "")
    dma("S", T.y[:, 0:h], T.ysb[:, 0:h], "ya", "")
    cp(T.ysb[:, h:C], T.p0[:, 0:C - h], "p0", "yb")
    dma("S", T.y[:, h:C], T.ysb[:, h:C], "yb", "")
    need("G", [(s, count[s]) for s in count])
